import numpy as np, ml_dtypes
CORES = [8,9,10,11,12,13]
N = 6
BF = ml_dtypes.bfloat16
W, K, P, RO, LIM = 8192, 32, 128, 6, 56
def hashed(u, v):
    u = u & 4095; v = v & 4095
    return ((u * v >> 5) + 37 * u) & (W - 1)
def probe(w, v):
    s = np.matmul(w, v.astype(np.float32)).astype(np.int64)
    return hashed(s[:, :, 0], s[:, :, 1])
def masks(rng, size):
    o = np.argsort(np.argsort(rng.random((N, 8, 16, K)), axis=2), axis=2)
    return (o < size[:, :, None, :]).astype(np.int32)
def parts(rng):
    x = rng.integers(0, 256, (N, 8, 16, W), dtype=np.uint8).astype(np.int32)
    return x, masks(rng, rng.integers(4, 12, (N, 8, K))), rng.integers(0, 256, (N, 8, 16, P)), rng.integers(0, 256, (N, 8, 16, 2))
def pack(x, m, z, w):
    return {a: np.ascontiguousarray(v.reshape(N, 128, n)).astype(np.float32).astype(BF) for a, v, n in (("xr", x, W), ("m0", m, K), ("z0", z, P), ("wt", w, 2))}
def setup_inputs(rng):
    return pack(*parts(rng))
def setup_inputs_spread(rng):
    def uneven(n):
        v = (np.exp2(8 * rng.random((N, 8, 1, n))) * rng.random((N, 8, 16, n))).astype(np.int32)
        return np.where(rng.random((N, 8, 1, n)) < 0.5, v, 255 - v)
    lo = rng.choice(np.array([0, 2, 5]), (N, 8, 1))
    return pack(uneven(W), masks(rng, lo + ((17 - lo) * rng.random((N, 8, K))).astype(np.int64)), uneven(P), np.exp2(8 * rng.random((N, 8, 16, 2))).astype(np.int64))
def setup_inputs_ends(rng):
    def two(n): return 255 * rng.integers(0, 2, (N, 8, 16, n), dtype=np.int32)
    x, z, w = two(W), two(P), two(2); m = rng.integers(0, 2, (N, 8, 16, K))
    s = 255 * rng.integers(0, 2, (8, 8, 1)); s[7] = 255
    z[N - 1, :, :8] = s; x[N - 1, :, :8] = 255 - s
    z[1, 7, :8] = 255; x[1, 7, :8] = 0
    for q, g in [(N - 1, g) for g in range(8)] + [(1, 7)]:
        a = rng.integers(0, 8, K); b = (a + rng.integers(1, 8, K)) % 8
        m[q, g, a, np.arange(K)] = 1; m[q, g, b, np.arange(K)] = 1
    m[1, 7, :, K - 1] = 0; m[1, 7, 15, K - 1] = 1
    w[N - 1, 7] = 255; m[N - 1, 7, :, 0] = 1; m[N - 1, 7, :, K - 1] = 1
    for i in (0, 1, 6, P - 1): z[N - 1, 7, :, i] = 255
    x[N - 1, 7, :, int(hashed(16 * 255 * 255, 16 * 255 * 255))] = 0
    for i in (0, 3, P - 1): z[0, 7, :, i] = 0
    x[0, 7, :, 0] = 0; m[0, 6, :, K - 1] = 0
    for g, e in ((7, 0), (5, 1)):
        w[2, g, :, e] = 255; w[2, g, :, 1 - e] = 255 * (rng.permutation(16) < rng.integers(1, 16))
        m[2, g, :, 0] = 1; x[2, g, 0] = 0
        for i in (0, 3, P - 1): z[2, g, :, i] = 255
        x[2, g, :, int(hashed(255 * int(np.sum(w[2, g, :, 0])), 255 * int(np.sum(w[2, g, :, 1]))))] = 255
    x[2, 6, 14:16] = 0; z[2, 6, 14:16, :8] = 255
    m[2, 6, :, 0] = 0; m[2, 6, 14] = 0; m[2, 6, 14:16, 0] = 1
    return pack(x, m, z, w)
def setup_inputs_corners(rng):
    x, m, z, w = parts(rng); idx = np.concatenate([np.arange(0, P, 2), np.array([P - 1])])
    t = np.argwhere(hashed(np.arange(256)[:, None], np.arange(256)[None, :]) == W - 1)
    for q in range(N):
        order = rng.permutation(8)
        want = {0: 0, 1: 7, N - 2: 0, N - 1: 4}.get(q)
        if want is not None:
            i = int(np.argmax(order == want)); order[i] = order[7]; order[7] = want
        for g in range(8):
            a, b, c, e = x[q, g], m[q, g], z[q, g], w[q, g]; kind = int(order[g])
            if kind == 0: b[:, 0] = 0
            if kind == 1: b[:] = 1
            if kind == 2:
                b[:] = 1; b[:, K - 1] = 0; b[15, K - 1] = 1
            if kind == 3:
                a[:] = rng.integers(250, 256, a.shape); c[:] = rng.integers(0, 6, c.shape)
                b[:] = np.argsort(np.argsort(rng.random((16, K)), axis=0), axis=0) < rng.integers(2, 4, (1, K))
            if kind == 4:
                e[:] = 0; e[0, 0] = 1; e[1, 1] = 1; b[0:2] = 1
                p = t[rng.integers(0, len(t), len(idx))]; c[0, idx] = p[:, 0]; c[1, idx] = p[:, 1]; c[0, 1] = 0
            if kind == 5:
                e[:] = 0; e[0] = 15; e[1] = 27; b[0:2] = 1; c[0, idx] = 255; c[1, idx] = 10
            if kind == 6:
                a[:] = 128; c[:] = 128 + rng.choice(np.array([-LIM - 1, -LIM, LIM, LIM + 1]), c.shape)
    p = t[rng.integers(0, len(t))]; odd = np.arange(2 * int(rng.integers(0, P // 4)) + 1, P, 2)
    m[N - 1, 7, :, 0] = 0; m[N - 1, 7, 0:2, 0] = 1; x[N - 1, 7, 0:2, W - 1] = p
    z[N - 1, 7, 0] = 0; z[N - 1, 7, 0, odd] = p[0]; z[N - 1, 7, 1, odd] = p[1]
    z[N - 2, 7, 0] = p[0]; z[N - 2, 7, 1] = p[1]; x[N - 2, 7, :, 0] = 0
    o = rng.permutation(256)[:P]
    w[1, 7] = 0; w[1, 7, 0, 0] = 1; m[1, 7, :, 0] = 0; m[1, 7, 0, 0] = 1; z[1, 7, 0] = o
    z[0, 7, 0] = o[P - 1]; x[0, 7, :, 0] = 0
    return pack(x, m, z, w)
def setup_inputs_crowd(rng):
    x, m, z, w = parts(rng); role = rng.permutation(N)
    for q in range(N):
        r = int(role[q]); k = rng.permutation(8)
        if r == 1: k = np.roll(k, 4 - int(np.argmax(k == rng.integers(3, 5))))
        if r < 3: x[q] = rng.integers(200, 256, (8, 16, W))
        if r < 2: z[q] = rng.integers(0, 101, (8, 16, P))
        if r == 2: z[q] = rng.integers(200, 256, (8, 16, P))
        w[q, k[0]] = 0; w[q, k[1]] = 0
        for g in k[2:4]:
            w[q, g] = 0; w[q, g, 0] = 1; m[q, g, 0] = 1
            c = int(rng.integers(0, 100)) if r < 2 else int(rng.integers(200, 255))
            z[q, g, 0] = c; z[q, g, 0, int(rng.integers(0, P))] = c + 1
        if r == 1: z[q, k[4], :, int(rng.integers(0, P))] = 210
        if r == 2: z[q, k[4], :, int(rng.integers(0, P))] = 50
    return pack(x, m, z, w)
def check_inputs(d):
    bad = []
    for k, lo, hi in (("xr", 0, 255), ("m0", 0, 1), ("z0", 0, 255), ("wt", 0, 255)):
        a = np.asarray(d[k]).astype(np.float32)
        if not (np.min(a) >= lo and np.max(a) <= hi): bad.append("range of " + k)
        elif np.any(a != np.floor(a)): bad.append("whole numbers in " + k)
    return bad
def reference(xr, m0, z0, wt):
    X = xr.astype(np.float32).astype(np.int16).reshape(N, 8, 16, W)
    M = np.repeat(m0.astype(np.float32).astype(np.int16).reshape(N, 8, 16, K)[..., None], P, axis=4)
    z = z0.astype(np.float32).astype(np.int16).reshape(N, 8, 16, P)
    w = np.ascontiguousarray(wt.astype(np.float32).reshape(N, 8, 16, 2).transpose(0, 1, 3, 2))
    A = np.zeros(N, np.int64); kk = np.arange(K)[None, None, :, None]; steps = []
    for t in range(RO):
        zk = z[:, :, :, None, :]
        h = probe(w, (M * zk).reshape(N, 8, 16, K * P))
        Xh = np.take_along_axis(X, h[:, :, None, :], 3).reshape(N, 8, 16, K, P)
        F = M * (np.abs(Xh - zk) > LIM)
        ok = np.add.reduce(F, axis=2, dtype=np.int16) <= (1 + (A & 1))[:, None, None, None]
        j = np.where(np.any(ok, axis=2), np.argmax(ok, axis=2), K)
        first = F * (np.add.accumulate(F, axis=2, dtype=np.int16) == 1)
        U = np.max(first * (kk < j[:, :, None, :])[:, :, None], axis=3)
        hit = (j < K)[:, :, None, :]; s = np.where(j < K, j, 0)[:, :, None, None, :]
        U = np.maximum(U, hit * np.take_along_axis(M, s, 3)[:, :, :, 0])
        xs = np.take_along_axis(Xh, s, 3)[:, :, :, 0]
        new = np.where(hit, np.abs(z - xs), (z + xs) >> 1)
        down = (kk[:, :, 1:] <= j[:, :, None, :])[:, :, None]
        M = np.concatenate([U[:, :, :, None], np.where(down, M[:, :, :, :-1], M[:, :, :, 1:])], axis=3)
        if t < RO - 1:
            place = probe(w, U * z)
            for q in range(N):
                for g in range(8):
                    v, i = np.unique(place[q, g], return_index=True)
                    X[q, g][:, v] = z[q, g][:, i]
        A = np.add.reduce((j == K).astype(np.int64), axis=(1, 2))
        steps.append(new); z = np.roll(new, 1, axis=0)
    return {"ym": M.reshape(N, 128, K * P).astype(np.float32).astype(BF), "yz": np.stack(steps, axis=3).reshape(N, 128, RO * P).astype(np.float32).astype(BF)}

@@ -1,0 +1,556 @@
+from concourse.mybir import AluOpType as AL, ActivationFunctionType as AF
+
+RO = 6
+CFG = {"abs": (0, 0, 0, 0), "eng": 16, "slack": 0.0}
+DT = {"f": "float32", "i": "int32", "b": "bfloat16", "u": "uint16"}
+SCRATCH = {}
+LN2 = 0.6931471805599453
+BIG = 262144.0
+C1 = 1.5 * 2.0 ** 23
+
+
+def build():
+    ops = []
+    used = {"f": 0, "i": 0, "b": 0, "u": 0}
+
+    def new(d, n):
+        lo = used[d]
+        used[d] = lo + (n + 15) // 16 * 16
+        return ("p" + d, lo, lo + n, 1, 128)
+
+    def own(name, d, n, where="sbuf"):
+        SCRATCH[name] = (where, [128, n], DT[d])
+        return (name, 0, n, 1, 128)
+
+    def sl(r, a, b, st=1, pn=128):
+        return (r[0], r[1] + a, r[1] + b, st, pn)
+
+    def cnt(r):
+        if r[0] == "@":
+            return 16 * cnt(r[2])
+        return len(range(r[1], r[2], r[3]))
+
+    def two(r):
+        return r[0] in ("pb", "pu", "X", "WX", "WM", "zM", "NP", "zin", "yzb", "ymb")
+
+    def add(e, k, a, rd, wr, cost):
+        R = []
+        W = []
+        for r in rd:
+            if isinstance(r, tuple):
+                if r[0] == "@":
+                    R.extend([r[1], r[2]])
+                else:
+                    R.append(r)
+        for r in wr:
+            if r[0] == "@":
+                W.append(r[1])
+                R.append(r[2])
+            else:
+                W.append(r)
+        ops.append({"e": e, "k": k, "a": a, "r": R, "w": W, "c": cost})
+
+    def vc(out, ins, tt=False):
+        n = cnt(out)
+        if out[0] == "@":
+            return 0.05 + n * 3.8e-3
+        if ins[0][0] == "@":
+            return 0.05 + n * 1.56e-3
+        f = 0.5 if all(two(r) for r in ins + [out]) else 1.0
+        if tt and all(r[0][0] != "B" for r in ins):
+            f *= 2
+        return 0.04 + max(64, n * f) * 1e-3
+
+    def TS(out, in0, s1, s2, o0, o1=None):
+        add("v", "ts", (out, in0, s1, s2, o0, o1), [in0, s1, s2], [out], vc(out, [in0]))
+
+    def TT(out, a, b, o):
+        add("v", "tt", (out, a, b, o), [a, b], [out], vc(out, [a, b], True))
+
+    def CP(out, a):
+        add("v", "cp", (out, a), [a], [out], vc(out, [a]))
+
+    def SC(out, a, b, ini, o0, o1):
+        add("v", "sc", (out, a, b, ini, o0, o1), [a, b], [out], vc(out, [a, b]))
+
+    def MS(out, v):
+        add("v", "ms", (out, v), [], [out], vc(out, [out]))
+
+    def AC(out, a, fn, bias=0.0, scale=1.0, acc=None):
+        n = cnt(out)
+        add("a", "ac", (out, a, fn, bias, scale, acc), [a, bias, scale], [out] + ([acc] if acc else []),
+            0.07 + max(64, n * (1.56 if a[0] == "@" else 1.0)) * 1e-3)
+
+    def MM(lst):
+        c = 0.03
+        for o, l, r, s0, s1 in lst:
+            c += max(min(64, cnt(l)), cnt(r)) * (4 if l[0] == "pf" else 1) * 0.5e-3
+        add("p", "mm", lst, [x[1] for x in lst] + [x[2] for x in lst], [x[0] for x in lst], c)
+
+    def ACC(out, pairs):
+        n = len(pairs)
+        return [(out, l, r, i == 0, i == n - 1) for i, (l, r) in enumerate(pairs)]
+
+    def TR(out, a, ident):
+        add("p", "tr", (out, a, ident), [a, ident], [out], 0.03 + 128 * 4 * 0.5e-3)
+
+    def IO(out, pat, base, cm):
+        add("g", "io", (out, pat, base, cm), [], [out], 0.13 + cnt(out) * 2e-3)
+
+    def DMA(q, out, a, cost):
+        add(q, "dma", (out, a), [a], [out], cost)
+
+    X = own("X", "b", 8256)
+    WX = own("WX", "b", 4224)
+    WM = own("WM", "b", 4224)
+    zM = own("zM", "b", 4096)
+    NP = own("NP", "b", 4096)
+    zin = own("zin", "b", 768)
+    yzb = own("yzb", "b", 768)
+    ymb = own("ymb", "b", 4096)
+    B = [own("B%d" % k, "f", 512, "psum") for k in range(8)]
+    m0s = own("m0s", "b", 32)
+    wts = own("wts", "b", 2)
+
+    DMA("s", sl(zin, 0, 128), ("z0", 0, 128, 1, 128), 2.0)
+    DMA("a", m0s, ("m0", 0, 32, 1, 128), 2.0)
+    DMA("a", wts, ("wt", 0, 2, 1, 128), 2.0)
+    DMA("s", sl(X, 0, 8192), ("xr", 0, 8192, 1, 128), 10.0)
+
+    dif = new("i", 128); IO(dif, [[-1, 128]], 128, 1)
+    ip = new("i", 1); IO(ip, [[0, 1]], 0, 1)
+    ip16 = new("i", 1); IO(ip16, [[0, 1]], 0, 16)
+    ib = new("f", 128); IO(ib, [[16, 8], [0, 16]], 0, 0)
+    im = new("i", 128); IO(im, [[1, 32], [0, 4]], 0, 0)
+    k8 = new("f", 8); IO(k8, [[0, 2], [16, 4]], 0, 0)
+    d5 = new("f", 5); IO(d5, [[-3, 5]], 0, 0)
+    i64 = new("f", 64); IO(i64, [[1, 64]], 0, 0)
+    i16 = new("f", 64); IO(i16, [[0, 4], [1, 16]], 0, 0)
+    I = new("b", 128); TS(I, dif, 128.0, None, AL.is_equal)
+    If = new("f", 128); TS(If, dif, 128.0, None, AL.is_equal)
+    t1 = new("i", 1); pg = new("f", 1); TS(t1, ip, 112, None, AL.bitwise_and); CP(pg, t1)
+    t2 = new("i", 1); pp = new("f", 1); TS(t2, ip, 15, None, AL.bitwise_and); CP(pp, t2)
+    t3 = new("i", 1); s64 = new("f", 1); TS(t3, ip16, 1984, None, AL.bitwise_and); CP(s64, t3)
+    BD = new("b", 128); TS(BD, ib, pg, None, AL.is_equal)
+    G8 = sl(BD, 0, 128, 16)
+    Wh = new("b", 16); Wr = [new("b", 128), new("b", 128)]
+    for e in range(2):
+        TS(sl(Wh, 8 * e, 8 * e + 8), G8, sl(wts, e, e + 1), None, AL.mult)
+        TS(Wr[e], BD, sl(wts, e, e + 1), None, AL.mult)
+    om = new("u", 128); CP(om, im)
+    TS(sl(WM, 2112, 4160), ("@", m0s, om), -4096.0, 4096.0, AL.mult, AL.add)
+    AC(sl(WM, 0, 2048), ("@", m0s, om), AF.Identity, 4096.0, -4096.0)
+    MS(sl(WM, 2048, 2112), 4096.0); MS(sl(WM, 4160, 4224), 4096.0)
+    t4 = new("i", 128); TS(t4, dif, 3, None, AL.bitwise_and)
+    B4 = new("b", 128); TS(B4, t4, 0.0, None, AL.is_equal)
+    SEL = sl(B4, 0, 4)
+
+    def scaled(src, v):
+        o = new("b", 128)
+        AC(o, src, AF.Copy, 0.0, v)
+        return o
+    I9 = scaled(I, 9.0); In9 = scaled(I, -9.0); Ig = scaled(I, -2.0 ** 18); Iw = scaled(I, 1.5 * 2.0 ** -63)
+    I7 = scaled(I, -0.875); Ih = scaled(I, 0.5); Inh = scaled(I, -0.5); Iq = scaled(I, 0.25); B4q = scaled(B4, 0.25)
+    Ia = scaled(I, -32.5); Ib = scaled(I, 32.0); Ic = scaled(I, 4096.0); Id = scaled(I, -4096.0)
+    ones = new("b", 128); MS(ones, 1.0)
+    nones = new("b", 128); MS(nones, -1.0)
+    SH = new("b", 128); TS(SH, dif, 124.0, None, AL.is_equal)
+    KOf = new("f", 8); TS(KOf, k8, pp, None, AL.add)
+    KO = new("b", 8); CP(KO, KOf)
+    rad = new("f", 4); TS(rad, sl(KOf, 0, 4), 1.0 / 128, None, AL.mult)
+    negt = new("f", 4); TS(negt, sl(KOf, 0, 4), -1.0, -8192.0, AL.mult, AL.add)
+    ioK = new("f", 64); TS(ioK, i64, 1.0 / 64, None, AL.mult)
+    t6 = new("f", 64); TS(t6, i64, -1.0 / 128, 1.0 / 128, AL.mult, AL.add)
+    t7 = new("f", 64); TS(t7, i16, pp, BIG, AL.not_equal, AL.mult)
+    NM = new("f", 64); TT(NM, t6, t7, AL.add)
+    rs1 = new("f", 64); MS(rs1, 0.0); MS(sl(rs1, 0, 64, 16), BIG)
+    rs2 = new("f", 256); MS(rs2, 0.0); MS(sl(rs2, 0, 256, 64), BIG)
+    Dm = new("f", 5); TS(Dm, d5, pp, None, AL.add)
+    e0 = new("f", 5); e1 = new("f", 5); e2 = new("f", 5); e3 = new("f", 5)
+    TS(e0, Dm, 0.0, 2.0 ** 18, AL.is_equal, AL.mult); TS(e1, Dm, 1.0, 512.0, AL.is_equal, AL.mult)
+    TS(e2, Dm, 2.0, None, AL.is_equal); TS(e3, Dm, 0.0, -2.0 ** 19, AL.is_lt, AL.mult)
+    f0 = new("f", 5); f1 = new("f", 5); tw = new("f", 5)
+    TT(f0, e0, e1, AL.add); TT(f1, e2, e3, AL.add); TT(tw, f0, f1, AL.add)
+    g0 = new("f", 5); g1 = new("f", 5); g2 = new("f", 5); rw = new("f", 5)
+    TS(g0, e0, 2.0 ** -36, None, AL.mult); TS(g1, e1, 2.0 ** -18, None, AL.mult)
+    TT(g2, g0, g1, AL.add); TT(rw, g2, e2, AL.add)
+    CN = new("b", 48); CM = new("b", 48); RT = new("f", 41)
+    TS(sl(CN, 0, 8), G8, -1.0, None, AL.mult)
+    for a in range(5):
+        TS(sl(CN, 8 * a + 8, 8 * a + 16), G8, sl(tw, a, a + 1), None, AL.mult)
+        AC(sl(RT, 8 * a, 8 * a + 8), G8, AF.Copy, 0.0, sl(rw, a, a + 1))
+    MS(sl(RT, 40, 41), -0.5)
+    TS(CM, CN, -1.0 / 4096, None, AL.mult)
+    REP = new("f", 128)
+    TR(sl(B[7], 128, 256, 1, 41), RT, If)
+    AC(sl(REP, 0, 128, 1, 41), sl(B[7], 128, 256, 1, 41), AF.Copy)
+    OG = new("b", 8); OP = new("b", 8); OT = new("b", 8); EZ = new("b", 128); EN = new("b", 128)
+    s6m = new("f", 1); TS(s6m, s64, -2048.0, None, AL.add)
+    TS(sl(OG, 0, 4), SEL, s6m, 0.5, AL.mult, AL.mult); MS(sl(OG, 4, 8), 0.0)
+    TS(sl(OP, 0, 4), SEL, 1024.0, None, AL.mult); TS(sl(OP, 4, 8), SEL, s64, 0.5, AL.mult, AL.mult)
+    TS(sl(OT, 0, 4), SEL, s64, -0.5, AL.mult, AL.mult); TS(sl(OT, 4, 8), SEL, s64, -0.5, AL.mult, AL.mult)
+    MS(sl(EZ, 4, 128), 0.0); MS(sl(EN, 4, 128), 0.0)
+    TS(sl(EZ, 0, 4), SEL, s64, 0.5, AL.mult, AL.mult); TS(sl(EN, 0, 4), SEL, s64, -0.5, AL.mult, AL.mult)
+    cb = new("f", 1); TS(cb, s64, -1.0 / 64, 15.5, AL.mult, AL.add)
+    thr = [new("f", 1) for t in range(RO)]
+    MS(thr[0], 2.0)
+    H = []
+    for h in range(2):
+        d = {}
+        for nm, dt_, n in (("w", "b", 128), ("L", "b", 256), ("rk", "b", 128), ("sig", "b", 384), ("x0", "b", 64), ("cm", "b", 128),
+                           ("hi", "i", 256), ("hj", "i", 256), ("h3", "i", 128),
+                           ("h4", "i", 128), ("h5", "i", 128), ("h6", "i", 128), ("h7", "i", 128), ("hf", "f", 128),
+                           ("off", "u", 128), ("r", "b", 128), ("mw", "b", 128), ("ge", "b", 128), ("gp", "b", 128),
+                           ("gt", "b", 128), ("D", "b", 64), ("e", "b", 64), ("ya", "f", 64), ("yb", "f", 64),
+                           ("Q", "b", 640), ("Rs", "f", 64), ("hh", "f", 64), ("nz", "b", 64), ("U", "b", 64),
+                           ("zU", "b", 64), ("ui", "i", 128), ("uj", "i", 128), ("u3", "i", 64), ("u4", "i", 64),
+                           ("u5", "i", 64), ("u6", "i", 64), ("u7", "i", 64), ("key", "f", 64), ("md", "f", 64),
+                           ("no", "f", 64), ("dd", "f", 256), ("mn", "f", 256), ("fa", "f", 4), ("fb", "f", 4),
+                           ("fc", "f", 4), ("ow", "u", 4), ("wt_", "f", 128), ("sg", "b", 128), ("cd", "b", 128),
+                           ("dl", "b", 128), ("junk", "b", 128), ("Hc", "f", 1), ("ab0", "b", 512), ("ab1", "b", 512)):
+            d[nm] = new(dt_, n)
+        d["o"] = [new("u", 8), new("u", 8)]
+        H.append(d)
+        TS(d["rk"], ones, s64, 1.0 / 64, AL.mult, AL.mult)
+        AC(d["w"], d["rk"], AF.Exp, 30 * LN2, -3 * LN2)
+        TS(sl(d["L"], 0, 128), ones, s64, None, AL.mult)
+        MS(sl(d["L"], 128, 256), 0.0)
+        CP(d["o"][1], KOf)
+        MS(sl(d["Rs"], 0, 64, 1, 64), 1.0)
+    par = [new("f", 1) for k in range(5)]
+    fo = new("u", 256)
+    npiece = [0]
+
+    def hashv(src, n, i0, i1, i3, i4, i5, i6, i7):
+        CP(i0, src)
+        TS(i1, i0, 4095, None, AL.bitwise_and)
+        TT(i3, sl(i1, 0, n), sl(i1, n, 2 * n), AL.mult)
+        TS(i5, sl(i1, 0, n), 37.0, None, AL.mult)
+        TS(i4, i3, 5, None, AL.arith_shift_right)
+        TT(i6, i4, i5, AL.add)
+        TS(i7, i6, 8191, None, AL.bitwise_and)
+
+    def front(t, h):
+        d = H[h]
+        z = sl(zin, 128 * t + 64 * h, 128 * t + 64 * h + 64)
+        MM([(sl(B[0], 64 * k, 64 * k + 64), I, z, True, True) for k in range(8)])
+        for q in range(4):
+            TT(sl(zM, 2048 * h + 512 * q, 2048 * h + 512 * q + 512), sl(WM, 2112 * h + 512 * q, 2112 * h + 512 * q + 512),
+               B[0], AL.max)
+        MM([(sl(B[5], b, 256, 16), sl(zM, 2048 * h + b, 2048 * h + 2048, 16), Wh, True, True) for b in range(16)])
+        hashv(sl(B[5], 0, 256), 128, d["hi"], d["hj"], d["h3"], d["h4"], d["h5"], d["h6"], d["h7"])
+        CP(d["hf"], d["h7"])
+        TR(sl(B[5], 256, 384), d["hf"], If)
+        CP(d["off"], sl(B[5], 256, 384))
+
+    def probe(t, h):
+        d = H[h]
+        z = sl(zin, 128 * t + 64 * h, 128 * t + 64 * h + 64)
+        for x in range(2):
+            MM([(sl(B[3 + x], 64 + k, 384, 8), sl(WM, 2112 * h + 2 * k + x, 2112 * h + 2048, 16), sl(CM, 8, 48), k == 0, False)
+                for k in range(8)])
+        MM([(sl(B[5], 384 + b, 512, 16), sl(WM, 2112 * h + b, 2112 * h + 2048, 16), sl(CM, 0, 8), True, True) for b in range(16)])
+        AC(d["cm"], sl(B[5], 384, 512), AF.Copy)
+        for q in range(4):
+            xh = sl(WX, 2112 * h + 512 * q, 2112 * h + 512 * q + 512)
+            np_ = sl(NP, 2048 * h + 512 * q, 2048 * h + 512 * q + 512)
+            AC(xh, ("@", sl(X, 0, 8192), sl(d["off"], 32 * q, 32 * q + 32)), AF.Copy)
+            bk = B[1 + npiece[0] % 2]
+            npiece[0] += 1
+            MM(ACC(bk, [(I9, xh), (In9, sl(zM, 2048 * h + 512 * q, 2048 * h + 512 * q + 512))]))
+            if CFG["abs"][q]:
+                ab = d["ab%d" % (q // 2)]
+                AC(ab, bk, AF.Abs)
+                TS(np_, ab, 508.0, None, AL.is_gt)
+            else:
+                TS(np_, bk, 1.5 * 2.0 ** 33, 1.5 * 2.0 ** 33, AL.add, AL.not_equal)
+        AC(d["x0"], ("@", sl(WX, 2112 * h, 2112 * h + 2048), sl(d["o"][(t + 1) % 2], 4, 8)), AF.Copy)
+        MM(ACC(sl(B[5], 384, 448), [(Ih, z), (Inh, d["x0"]), (Iq, sl(ones, 0, 64))]))
+        AC(d["yb"], sl(B[5], 384, 448), AF.Identity, C1)
+        AC(sl(WX, 2112 * h + 2048, 2112 * h + 2112), d["yb"], AF.Identity, -C1)
+
+    def back(t, h):
+        d = H[h]
+        last = t == RO - 1
+        z = sl(zin, 128 * t + 64 * h, 128 * t + 64 * h + 64)
+        gt, ge, gp = sl(d["sig"], 0, 128), sl(d["sig"], 128, 256), sl(d["sig"], 256, 384)
+        w, o = d["w"], d["o"][t % 2]
+        MM([(sl(B[6], 0, 128), I, d["cm"], True, False)]
+           + [(sl(B[6], b, 128, 16), sl(NP, 2048 * h + b, 2048 * h + 2048, 16), sl(CN, 0, 8), False, b == 15) for b in range(16)])
+        AC(d["r"], sl(B[6], 0, 128), AF.Relu, thr[t])
+        for x in range(2):
+            MM([(sl(B[3 + x], 64 + k, 384, 8), sl(NP, 2048 * h + 2 * k + x, 2048 * h + 2048, 16), sl(CN, 8, 48), False, False)
+                for k in range(8)])
+        TT(d["mw"], d["r"], w, AL.mult)
+        MM(ACC(sl(B[6], 0, 128), [(I7, w), (B4q, d["mw"])]))
+        AC(gt, sl(B[6], 0, 128), AF.Sign)
+        MM(ACC(sl(B[6], 128, 256), [(I7, w), (B4, d["mw"])]) + ACC(sl(B[6], 256, 384), [(I7, w), (Iw, ones), (B4, d["mw"])]))
+        AC(sl(d["sig"], 128, 384), sl(B[6], 128, 384), AF.Sign)
+        MM(ACC(sl(B[7], 64, 72), [(I, KO), (gt, OT), (ge, OG), (gp, OP)]))
+        CP(o, sl(B[7], 64, 72))
+        TT(d["D"], ("@", sl(WX, 2112 * h, 2112 * h + 2112), sl(o, 0, 4)), z, AL.subtract)
+        nzr = sl(yzb, 128 * t + 64 * h, 128 * t + 64 * h + 64)
+        AC(nzr, d["D"], AF.Abs)
+        if not last:
+            add("g", "send", (sl(zin, 128 * t + 128 + 64 * h, 128 * t + 192 + 64 * h), nzr, "ar%d_%d" % (t, h)), [nzr],
+                [sl(zin, 128 * t + 128 + 64 * h, 128 * t + 192 + 64 * h)], 2.5)
+        if h == 0:
+            DMA("s", ("yz", 128 * t, 128 * t + 128, 1, 128), sl(yzb, 128 * t, 128 * t + 128), 2.0)
+        for x in range(2):
+            MM([(sl(B[3 + x], 64 * a + 64, 64 * a + 128), Ig, sl(gt, x, 128, 2), False, a == 4) for a in range(5)])
+            AC(sl(d["Q"], x, 640, 2), sl(B[3 + x], 64, 384), AF.Relu, -2.0 ** 18)
+        MM([(sl(B[7], b, 64, 16, 40), sl(d["Q"], b, 640, 16), SEL, True, True) for b in range(16)])
+        AC(sl(d["Rs"], 0, 64, 1, 40), sl(B[7], 0, 64, 1, 40), AF.Copy)
+        y = sl(B[7], 64, 128)
+        MM(ACC(y, [(sl(REP, 0, 128, 1, 41), sl(d["Rs"], 0, 64, 1, 41))]))
+        TS(d["hh"], y, 1.5 * 2.0 ** 32, -1.5 * 2.0 ** 32, AL.add, AL.add)
+        TT(d["nz"], y, d["hh"], AL.is_lt)
+        TT(d["U"], ("@", sl(WM, 2112 * h, 2112 * h + 2112), sl(o, 0, 4)), d["nz"], AL.mult)
+        CP(("@", sl(WM, 2112 * h, 2112 * h + 2048), sl(o, 4, 8)), d["U"])
+        if not last:
+            TT(d["zU"], d["U"], z, AL.max)
+            MM(ACC(sl(B[7], 384, 448), [(Wr[0], d["zU"])]) + ACC(sl(B[7], 448, 512), [(Wr[1], d["zU"])]))
+            hashv(sl(B[7], 384, 512), 64, d["ui"], d["uj"], d["u3"], d["u4"], d["u5"], d["u6"], d["u7"])
+            TT(d["md"], NM, d["u7"], AL.subtract)
+            TT(d["key"], d["u7"], ioK, AL.add)
+            SC(d["no"], rs1, d["md"], 0.0, AL.add, AL.min)
+            for c in range(4):
+                AC(sl(d["dd"], 64 * c, 64 * c + 64), d["key"], AF.Abs, sl(d["no"], 16 * c + 15, 16 * c + 16))
+            SC(d["mn"], rs2, d["dd"], 0.0, AL.add, AL.min)
+            TT(d["fa"], sl(d["mn"], 63, 256, 64), rad, AL.is_lt)
+            TT(d["fb"], d["fa"], negt, AL.mult)
+            TT(d["fc"], d["fb"], sl(d["no"], 15, 64, 16), AL.min)
+            TS(d["ow"], d["fc"], -1.0, None, AL.mult)
+            MM(ACC(sl(B[6], 384, 512), [(I, d["rk"]), (Ia, gp), (Ib, gt)]))
+            AC(d["rk"], sl(B[6], 384, 512), AF.Relu, 0.5)
+            AC(w, d["rk"], AF.Exp, 30 * LN2, -3 * LN2)
+            MM(ACC(sl(B[5], 384, 512), [(ones, ge), (nones, gt)]))
+            AC(d["junk"], sl(B[5], 384, 512), AF.Identity, 0.0, 0.5, d["Hc"])
+        MM(ACC(sl(B[6], 384, 512), [(B4, gt)]))
+        AC(d["sg"], sl(B[6], 384, 512), AF.Sign, cb, -0.5)
+        l1, l2 = sl(d["L"], 0, 128), sl(d["L"], 128, 256)
+        MM(ACC(sl(B[7], 128, 256), [(SH, l1), (SH, l2), (EZ, gp), (EN, gt), (Ic, d["sg"])])
+           + ACC(sl(B[7], 256, 384), [(I, l1), (I, l2), (Id, d["sg"])]))
+        AC(d["L"], sl(B[7], 128, 384), AF.Relu, -4096.0)
+
+    for t in range(RO):
+        for h in (1, 0):
+            front(t, h)
+        for h in (1, 0):
+            probe(t, h)
+            back(t, h)
+        if t < RO - 1:
+            for h in (1, 0):
+                CP(("@", X, H[h]["ow"]), sl(zin, 128 * t + 64 * h, 128 * t + 64 * h + 64))
+            AC(par[0], H[0]["Hc"], AF.Identity, H[1]["Hc"])
+            AC(par[1], par[0], AF.Identity, -0.25, 0.5)
+            AC(par[2], par[1], AF.Identity, C1)
+            AC(par[3], par[2], AF.Identity, 2 * C1 + 2, -2.0)
+            AC(thr[t + 1], par[3], AF.Identity, par[0])
+    for h in (1, 0):
+        MM(ACC(sl(B[7], 256, 384), [(sl(H[h]["L"], 0, 128), I), (sl(H[h]["L"], 128, 256), I)]))
+        for c in range(4):
+            TS(sl(fo, 4 * h + c, 256, 8), sl(B[7], 256 + c, 384, 4), sl(KOf, c, c + 1), 2112.0 * h, AL.add, AL.add)
+    for q in range(8):
+        src = ("@", WM, sl(fo, 32 * q, 32 * q + 32))
+        dst = sl(ymb, 512 * q, 512 * q + 512)
+        if q % 2:
+            AC(dst, src, AF.Identity, 1.0, -1.0 / 4096)
+            DMA("s", ("ym", 512 * q - 512, 512 * q + 512, 1, 128), sl(ymb, 512 * q - 512, 512 * q + 512), 2.5)
+        else:
+            TS(dst, src, -1.0 / 4096, 1.0, AL.mult, AL.add)
+    for k in used:
+        SCRATCH["p" + k] = ("sbuf", [128, used[k]], DT[k])
+    return ops
+
+
+def meets(a, b):
+    if a[0] != b[0] or a[1] >= b[2] or b[1] >= a[2]:
+        return False
+    if a[3] > 1 and a[3] == b[3] and a[0] != "pu" and (a[1] - b[1]) % a[3]:
+        return False
+    return True
+
+
+def schedule(ops):
+    n = len(ops)
+    hist = {}
+    for i, o in enumerate(ops):
+        dep = set()
+        for r in o["r"]:
+            for (j, q, wr) in hist.get(r[0], []):
+                if wr and meets(q, r):
+                    dep.add(j)
+        for r in o["w"]:
+            lst = hist.get(r[0], [])
+            for (j, q, wr) in lst:
+                if meets(q, r):
+                    dep.add(j)
+            if o["e"] != "p":
+                hist[r[0]] = [x for x in lst if not (r[3] == 1 and r[4] >= x[1][4] and r[1] <= x[1][1] and x[1][2] <= r[2])]
+        for r in o["r"]:
+            hist.setdefault(r[0], []).append((i, r, False))
+        for r in o["w"]:
+            hist.setdefault(r[0], []).append((i, r, True))
+            if len(hist[r[0]]) > 400 and r[0][0] == "B":
+                hist[r[0]] = hist[r[0]][-300:]
+        dep.discard(i)
+        o["d"] = dep
+        o["b"] = sorted(set(r[0] for r in o["r"] + o["w"] if r[0][0] == "B"))
+    lat = 0.1
+    succ = [[] for k in range(n)]
+    for i, o in enumerate(ops):
+        for j in o["d"]:
+            succ[j].append(i)
+    pr = [0.0] * n
+    for i in range(n - 1, -1, -1):
+        pr[i] = ops[i]["c"] + max([pr[j] + lat for j in succ[i]] + [0.0])
+    left = [len(o["d"]) for o in ops]
+    ready = [i for i in range(n) if left[i] == 0]
+    free = {}
+    fin = [0.0] * n
+    bank = {}
+    order = []
+    while ready:
+        est = {}
+        for i in ready:
+            o = ops[i]
+            s = free.get(o["e"], 0.0)
+            for j in o["d"]:
+                s = max(s, fin[j] + (0.0 if o["e"] == "p" and ops[j]["e"] == "p" else lat))
+            for b in o["b"]:
+                for e, j in bank.get(b, {}).items():
+                    if e != o["e"]:
+                        s = max(s, fin[j] + lat)
+            est[i] = s
+        i0 = min(ready, key=lambda i: (est[i], -pr[i]))
+        c = [i for i in ready if ops[i]["e"] == ops[i0]["e"] and est[i] <= est[i0] + CFG["slack"]]
+        i = max(c, key=lambda k: pr[k] - 2 * (est[k] - est[i0]))
+        o = ops[i]
+        for b in o["b"]:
+            for e, j in bank.get(b, {}).items():
+                if e != o["e"]:
+                    o["d"].add(j)
+            bank.setdefault(b, {})[o["e"]] = i
+        o["s"] = est[i]
+        fin[i] = est[i] + o["c"]
+        free[o["e"]] = est[i] + (0.1 if o["k"] == "dma" else 0.4 if o["k"] == "send" else o["c"])
+        order.append(i)
+        ready.remove(i)
+        for j in succ[i]:
+            left[j] -= 1
+            if left[j] == 0:
+                ready.append(j)
+    pos = {}
+    for k, i in enumerate(order):
+        pos[i] = k
+    seen = {}
+    need = set()
+    for i in order:
+        o = ops[i]
+        best = {}
+        for j in o["d"]:
+            p = ops[j]
+            if p["k"] in ("dma", "send"):
+                best[("x", j)] = j
+            elif not (p["e"] == "p" and o["e"] == "p"):
+                if ("q", p["e"]) not in best or pos[j] > pos[best[("q", p["e"])]]:
+                    best[("q", p["e"])] = j
+        o["wt"] = []
+        for k, j in best.items():
+            if seen.get((o["e"], k), -1) < pos[j]:
+                seen[(o["e"], k)] = pos[j]
+                o["wt"].append(j)
+                need.add(j)
+    tot = {}
+    sems = ["loc"]
+    for i in order:
+        o = ops[i]
+        if o["k"] == "dma":
+            o["sem"] = ("d%d" % i, 16)
+        elif o["k"] == "send":
+            o["sem"] = (o["a"][2], CFG["eng"])
+        elif i in need:
+            tot["q" + o["e"]] = tot.get("q" + o["e"], 0) + 1
+            o["sem"] = ("q" + o["e"], tot["q" + o["e"]])
+        else:
+            o["sem"] = None
+        if o["sem"] and o["sem"][0] not in sems:
+            sems.append(o["sem"][0])
+    return order, sems, max(fin)
+
+
+OPS = build()
+ORDER, SEMAPHORES, SPAN = schedule(OPS)
+
+
+def rank_program(g, core, T, topo):
+    rank = T.rank_of(core)
+    if rank is None:
+        return
+    nxt = T.cores[(rank + 1) % len(T.cores)]
+    rid, pid = topo.addr(nxt)[0:2]
+    mask = 0
+    for e in topo.engines(core, nxt)[0:CFG["eng"]]:
+        mask |= 1 << e
+    Q = {"v": g.vector, "a": g.scalar, "p": g.tensor, "s": g.sync, "g": g}
+
+    def ap(r):
+        if not isinstance(r, tuple):
+            return r
+        if r[0] == "@":
+            return ap(r[1]).indirect(ap(r[2]))
+        if r[3] == 1:
+            return T[r[0]][0:r[4], r[1]:r[2]]
+        return T[r[0]][0:r[4], r[1]:r[2]:r[3]]
+
+    ends = {}
+    sent = 0
+    for i in ORDER:
+        o = OPS[i]
+        q = Q[o["e"]]
+        k = o["k"]
+        a = o["a"]
+        for j in o["wt"]:
+            q.wait_ge(T.sem[OPS[j]["sem"][0]], OPS[j]["sem"][1])
+        if k == "send":
+            g.remote_dma(ap(a[0]), ap(a[1]), T.sem[a[2]], T.sem["loc"], pid, rid, mask)
+            sent += CFG["eng"]
+            ends[a[2]] = CFG["eng"]
+            continue
+        if k == "ts":
+            if a[5] is None:
+                x = q.tensor_scalar(ap(a[0]), ap(a[1]), ap(a[2]), None, a[4])
+            else:
+                x = q.tensor_scalar(ap(a[0]), ap(a[1]), ap(a[2]), ap(a[3]), a[4], a[5])
+        elif k == "tt":
+            x = q.tensor_tensor(ap(a[0]), ap(a[1]), ap(a[2]), a[3])
+        elif k == "cp":
+            x = q.tensor_copy(ap(a[0]), ap(a[1]))
+        elif k == "sc":
+            x = q.tensor_tensor_scan(ap(a[0]), ap(a[1]), ap(a[2]), a[3], a[4], a[5])
+        elif k == "ms":
+            x = q.memset(ap(a[0]), a[1])
+        elif k == "ac":
+            if a[5]:
+                x = q.activation(ap(a[0]), ap(a[1]), a[2], bias=ap(a[3]), scale=ap(a[4]), accum_out=ap(a[5]))
+            else:
+                x = q.activation(ap(a[0]), ap(a[1]), a[2], bias=ap(a[3]), scale=ap(a[4]))
+        elif k == "mm":
+            for m in a:
+                x = q.matmul(ap(m[0]), ap(m[1]), ap(m[2]), m[3], m[4])
+        elif k == "tr":
+            x = q.transpose(ap(a[0]), ap(a[1]), ap(a[2]))
+        elif k == "io":
+            if a[0][0] == "pf":
+                x = g.iota(ap(a[0]), a[1], a[2], a[3], allow_small_or_imprecise_dtypes=True)
+            else:
+                x = g.iota(ap(a[0]), a[1], a[2], a[3])
+        else:
+            x = q.dma_start(ap(a[0]), ap(a[1]))
+        if o["sem"]:
+            x.then_inc(T.sem[o["sem"][0]], 16 if k == "dma" else 1)
+            ends[o["sem"][0]] = o["sem"][1]
+    g.wait_ge(T.sem["loc"], sent)
+    for s in ends:
+        g.wait_ge(T.sem[s], ends[s])

@@ -1,29 +1,43 @@
+from concourse.bass import DstId, RemoteDMATransfer
 from concourse.mybir import AluOpType as AL, ActivationFunctionType as AF
 
 RO = 6
-CFG = {"abs": (0, 0, 0, 0), "eng": 16, "slack": 0.0}
-DT = {"f": "float32", "i": "int32", "b": "bfloat16", "u": "uint16"}
+PARTS = ("front", "probe", "match", "mask", "rank", "write")
+CFG = {"abs": (), "vg": (), "vq": (), "au": (0, 1), "ve": (), "ap": (0, 1), "av": (), "ar": (0, 1), "t": "a", "ut": "a",
+       "md": 0, "eng": 16, "send": 2.0, "xl": 10.0, "lat": 0.1, "turns": 3, "slack": 0.0, "pen": 2.0,
+       "ahead": {p + "1": 3.0 for p in PARTS}, "pc": (512, 512, 512, 512)}
+DT = {"f": "float32", "i": "int32", "b": "bfloat16", "u": "uint16", "h": "float16"}
 SCRATCH = {}
 LN2 = 0.6931471805599453
-BIG = 262144.0
+CY = 0.85e-3
 C1 = 1.5 * 2.0 ** 23
 
 
 def build():
     ops = []
-    used = {"f": 0, "i": 0, "b": 0, "u": 0}
+    part = ["const"]
+    used = {"f": 0, "i": 0, "b": 0, "u": 0, "h": 0}
 
     def new(d, n):
         lo = used[d]
         used[d] = lo + (n + 15) // 16 * 16
-        return ("p" + d, lo, lo + n, 1, 128)
+        return ("p" + d, lo, lo + n, 1, 128, 0)
 
     def own(name, d, n, where="sbuf"):
         SCRATCH[name] = (where, [128, n], DT[d])
-        return (name, 0, n, 1, 128)
+        return (name, 0, n, 1, 128, 0)
 
-    def sl(r, a, b, st=1, pn=128):
-        return (r[0], r[1] + a, r[1] + b, st, pn)
+    def hbm(name, a, b):
+        return (name, a, b, 1, 128, 0)
+
+    def sl(r, a, b, st=1):
+        return (r[0], r[1] + a, r[1] + b, st, r[4], r[5])
+
+    def pt(r, p0, p1):
+        return r[:4] + (p1, p0)
+
+    def half(r, f):
+        return pt(r, 64 * f, 64 * f + 64)
 
     def cnt(r):
         if r[0] == "@":
@@ -31,7 +45,7 @@ def build():
         return len(range(r[1], r[2], r[3]))
 
     def two(r):
-        return r[0] in ("pb", "pu", "X", "WX", "WM", "zM", "NP", "zin", "yzb", "ymb")
+        return r[0] in ("pb", "ph", "pu", "m0s", "X0", "X1", "WS", "WX", "WM", "zM", "NP", "zin", "yzb", "ymb")
 
     def add(e, k, a, rd, wr, cost):
         R = []
@@ -48,18 +62,21 @@ def build():
                 R.append(r[2])
             else:
                 W.append(r)
-        ops.append({"e": e, "k": k, "a": a, "r": R, "w": W, "c": cost})
+        for r in R + W:
+            if r[0][0] == "B":
+                (W if e == "p" else R).append(("G" + r[0], 0, 1, 1, 128, 0))
+        ops.append({"e": e, "k": k, "a": a, "r": R, "w": W, "c": cost, "n": part[0]})
 
     def vc(out, ins, tt=False):
         n = cnt(out)
         if out[0] == "@":
-            return 0.05 + n * 3.8e-3
+            return 0.05 + n * 3.8 * CY
         if ins[0][0] == "@":
-            return 0.05 + n * 1.56e-3
+            return 0.05 + n * 1.56 * CY
         f = 0.5 if all(two(r) for r in ins + [out]) else 1.0
         if tt and all(r[0][0] != "B" for r in ins):
             f *= 2
-        return 0.04 + max(64, n * f) * 1e-3
+        return 0.05 + max(64, n * f) * CY
 
     def TS(out, in0, s1, s2, o0, o1=None):
         add("v", "ts", (out, in0, s1, s2, o0, o1), [in0, s1, s2], [out], vc(out, [in0]))
@@ -79,195 +96,248 @@ def build():
     def AC(out, a, fn, bias=0.0, scale=1.0, acc=None):
         n = cnt(out)
         add("a", "ac", (out, a, fn, bias, scale, acc), [a, bias, scale], [out] + ([acc] if acc else []),
-            0.07 + max(64, n * (1.56 if a[0] == "@" else 1.0)) * 1e-3)
+            0.065 + max(64, n * (1.56 if a[0] == "@" else 1.0)) * CY)
 
     def MM(lst):
         c = 0.03
         for o, l, r, s0, s1 in lst:
-            c += max(min(64, cnt(l)), cnt(r)) * (4 if l[0] == "pf" else 1) * 0.5e-3
+            c += max(min(64, cnt(l)), cnt(r)) * (4 if l[0] == "pf" else 1) * CY / 2
         add("p", "mm", lst, [x[1] for x in lst] + [x[2] for x in lst], [x[0] for x in lst], c)
 
     def ACC(out, pairs):
         n = len(pairs)
         return [(out, l, r, i == 0, i == n - 1) for i, (l, r) in enumerate(pairs)]
 
-    def TR(out, a, ident):
-        add("p", "tr", (out, a, ident), [a, ident], [out], 0.03 + 128 * 4 * 0.5e-3)
-
     def IO(out, pat, base, cm):
-        add("g", "io", (out, pat, base, cm), [], [out], 0.13 + cnt(out) * 2e-3)
+        add("g", "io", (out, pat, base, cm), [], [out], 0.13 + cnt(out) * 2 * CY)
 
     def DMA(q, out, a, cost):
         add(q, "dma", (out, a), [a], [out], cost)
 
-    X = own("X", "b", 8256)
+    X = [own("X%d" % h, "b", 8256) for h in range(2)]
+    WS = own("WS", "b", 4096)
     WX = own("WX", "b", 4224)
     WM = own("WM", "b", 4224)
-    zM = own("zM", "b", 4096)
+    zM = own("zM", "h", 4096)
     NP = own("NP", "b", 4096)
     zin = own("zin", "b", 768)
     yzb = own("yzb", "b", 768)
     ymb = own("ymb", "b", 4096)
     B = [own("B%d" % k, "f", 512, "psum") for k in range(8)]
-    m0s = own("m0s", "b", 32)
-    wts = own("wts", "b", 2)
+    m0s = own("m0s", "b", 64)
+    wts = own("wts", "b", 16)
 
-    DMA("s", sl(zin, 0, 128), ("z0", 0, 128, 1, 128), 2.0)
-    DMA("a", m0s, ("m0", 0, 32, 1, 128), 2.0)
-    DMA("a", wts, ("wt", 0, 2, 1, 128), 2.0)
-    DMA("s", sl(X, 0, 8192), ("xr", 0, 8192, 1, 128), 10.0)
+    for h in (1, 0):
+        for f in range(2):
+            DMA("a", half(sl(zin, 64 * h, 64 * h + 64), f), half(hbm("z0", 64 * f, 64 * f + 64), h), 2.0)
+            DMA("a", half(sl(m0s, 32 * h, 32 * h + 32), f), half(hbm("m0", 0, 32), h), 2.0)
+            DMA("a", half(sl(wts, 8 * h, 8 * h + 2), f), half(hbm("wt", 0, 2), h), 2.0)
+            DMA("s", half(sl(X[h], 0, 8192), f), half(hbm("xr", 0, 8192), h), CFG["xl"] * (2 - h))
 
     dif = new("i", 128); IO(dif, [[-1, 128]], 128, 1)
+    dif2 = new("i", 152); IO(dif2, [[-1, 152]], 24, 1)
     ip = new("i", 1); IO(ip, [[0, 1]], 0, 1)
     ip16 = new("i", 1); IO(ip16, [[0, 1]], 0, 16)
     ib = new("f", 128); IO(ib, [[16, 8], [0, 16]], 0, 0)
     im = new("i", 128); IO(im, [[1, 32], [0, 4]], 0, 0)
     k8 = new("f", 8); IO(k8, [[0, 2], [16, 4]], 0, 0)
     d5 = new("f", 5); IO(d5, [[-3, 5]], 0, 0)
-    i64 = new("f", 64); IO(i64, [[1, 64]], 0, 0)
     i16 = new("f", 64); IO(i16, [[0, 4], [1, 16]], 0, 0)
+    j65 = new("f", 260); IO(j65, [[-16, 4], [1, 65]], 0, 0)
+    n65 = new("f", 260); IO(n65, [[0, 4], [-1, 65]], -8192, 0)
     I = new("b", 128); TS(I, dif, 128.0, None, AL.is_equal)
-    If = new("f", 128); TS(If, dif, 128.0, None, AL.is_equal)
+    If32 = new("f", 128); TS(If32, dif, 128.0, 2.0 ** 19, AL.is_equal, AL.mult)
+    t0 = new("i", 128); TS(t0, dif, 63, None, AL.bitwise_and)
+    P2 = new("b", 128); TS(P2, t0, 0.0, None, AL.is_equal)
+    PH = [new("b", 128), new("b", 128)]; PF = [new("f", 128), new("f", 128)]
+    for f in range(2):
+        MS(half(PH[f], 1 - f), 0.0); CP(half(PH[f], f), half(P2, f))
+        AC(PF[f], PH[f], AF.Copy, 0.0, -16384.0)
     t1 = new("i", 1); pg = new("f", 1); TS(t1, ip, 112, None, AL.bitwise_and); CP(pg, t1)
     t2 = new("i", 1); pp = new("f", 1); TS(t2, ip, 15, None, AL.bitwise_and); CP(pp, t2)
     t3 = new("i", 1); s64 = new("f", 1); TS(t3, ip16, 1984, None, AL.bitwise_and); CP(s64, t3)
+    sc = new("f", 1); TS(sc, s64, 1.0 / 64, None, AL.mult)
     BD = new("b", 128); TS(BD, ib, pg, None, AL.is_equal)
     G8 = sl(BD, 0, 128, 16)
-    Wh = new("b", 16); Wr = [new("b", 128), new("b", 128)]
+    WhZ = [new("h", 16), new("h", 16)]; WhM = [new("b", 24), new("b", 24)]
+    Wr = [[new("b", 128), new("b", 128)], [new("b", 128), new("b", 128)]]
+    for h in (1, 0):
+        for e in range(2):
+            wc = sl(wts, 8 * h + e, 8 * h + e + 1)
+            TS(sl(WhZ[h], 8 * e, 8 * e + 8), G8, wc, -2.0 ** -12, AL.mult, AL.mult)
+            TS(sl(WhM[h], 8 * e, 8 * e + 8), G8, wc, -0.25, AL.mult, AL.mult)
+            TS(Wr[h][e], BD, wc, 32.0 - 64 * e, AL.mult, AL.mult)
+        CP(sl(WhM[h], 16, 24), G8)
+    OFF = new("b", 128)
     for e in range(2):
-        TS(sl(Wh, 8 * e, 8 * e + 8), G8, sl(wts, e, e + 1), None, AL.mult)
-        TS(Wr[e], BD, sl(wts, e, e + 1), None, AL.mult)
+        sg = 2.0 * e - 1.0
+        MS(pt(sl(OFF, 64 * e, 64 * e + 64), 0, 32), 64 * sg)
+        MS(pt(sl(OFF, 64 * e, 64 * e + 64), 32, 64), -sg / 64)
+    MS(pt(OFF, 64, 128), 0.0)
     om = new("u", 128); CP(om, im)
-    TS(sl(WM, 2112, 4160), ("@", m0s, om), -4096.0, 4096.0, AL.mult, AL.add)
-    AC(sl(WM, 0, 2048), ("@", m0s, om), AF.Identity, 4096.0, -4096.0)
-    MS(sl(WM, 2048, 2112), 4096.0); MS(sl(WM, 4160, 4224), 4096.0)
+    TS(sl(WM, 2112, 4160), ("@", sl(m0s, 32, 64), om), -1.0, None, AL.mult)
+    AC(sl(WM, 0, 2048), ("@", sl(m0s, 0, 32), om), AF.Copy, 0.0, -1.0)
+    MS(sl(WM, 2048, 2112), 0.0); MS(sl(WM, 4160, 4224), 0.0)
     t4 = new("i", 128); TS(t4, dif, 3, None, AL.bitwise_and)
     B4 = new("b", 128); TS(B4, t4, 0.0, None, AL.is_equal)
     SEL = sl(B4, 0, 4)
 
     def scaled(src, v):
-        o = new("b", 128)
+        o = new("b", cnt(src))
         AC(o, src, AF.Copy, 0.0, v)
         return o
-    I9 = scaled(I, 9.0); In9 = scaled(I, -9.0); Ig = scaled(I, -2.0 ** 18); Iw = scaled(I, 1.5 * 2.0 ** -63)
+    I9 = scaled(I, 9.0); Ig = scaled(I, -2.0 ** 18); Iw = scaled(I, 1.5 * 2.0 ** -63)
     I7 = scaled(I, -0.875); Ih = scaled(I, 0.5); Inh = scaled(I, -0.5); Iq = scaled(I, 0.25); B4q = scaled(B4, 0.25)
-    Ia = scaled(I, -32.5); Ib = scaled(I, 32.0); Ic = scaled(I, 4096.0); Id = scaled(I, -4096.0)
-    ones = new("b", 128); MS(ones, 1.0)
-    nones = new("b", 128); MS(nones, -1.0)
-    SH = new("b", 128); TS(SH, dif, 124.0, None, AL.is_equal)
+    Ia = scaled(I, -32.5); Ib = scaled(I, 32.0); In = scaled(I, -8192.0); Ine = scaled(I, -1.0); Im = scaled(I, -256.0)
+    I9h = new("h", 128); TS(I9h, I, 9.0, None, AL.mult)
+    ones = new("b", 192); MS(ones, 1.0)
+    o128 = sl(ones, 0, 128)
+    o32 = new("b", 128); MS(o32, 32.0)
+    oh = new("b", 40); MS(oh, -1.0 / 256)
+    halff = new("f", 128); MS(halff, 0.5)
     KOf = new("f", 8); TS(KOf, k8, pp, None, AL.add)
     KO = new("b", 8); CP(KO, KOf)
-    rad = new("f", 4); TS(rad, sl(KOf, 0, 4), 1.0 / 128, None, AL.mult)
-    negt = new("f", 4); TS(negt, sl(KOf, 0, 4), -1.0, -8192.0, AL.mult, AL.add)
-    ioK = new("f", 64); TS(ioK, i64, 1.0 / 64, None, AL.mult)
-    t6 = new("f", 64); TS(t6, i64, -1.0 / 128, 1.0 / 128, AL.mult, AL.add)
-    t7 = new("f", 64); TS(t7, i16, pp, BIG, AL.not_equal, AL.mult)
-    NM = new("f", 64); TT(NM, t6, t7, AL.add)
-    rs1 = new("f", 64); MS(rs1, 0.0); MS(sl(rs1, 0, 64, 16), BIG)
-    rs2 = new("f", 256); MS(rs2, 0.0); MS(sl(rs2, 0, 256, 64), BIG)
+    SEL3 = new("b", 12)
+    for e in range(3):
+        TS(sl(SEL3, 4 * e, 4 * e + 4), SEL, 2.0 ** (9 * e - 18), None, AL.mult)
+    c0 = new("f", 64); c1 = new("f", 64); ctl1 = new("f", 64); pq = new("f", 1)
+    TS(pq, pp, 1.0, None, AL.add)
+    TS(c0, i16, pp, None, AL.not_equal); TS(c1, i16, pq, 511.0, AL.is_equal, AL.mult); TT(ctl1, c0, c1, AL.add)
+    kn = new("f", 1); kr = new("f", 1); k0 = new("f", 1); k1 = new("f", 1); k2 = new("f", 1)
+    TS(k0, pp, 15.0, 511.0, AL.not_equal, AL.mult)
+    TS(kn, k0, -1.0, -1.0, AL.mult, AL.add)
+    kp = new("f", 1); TS(kp, k0, 1.0, None, AL.add)
+    TS(k1, pp, 15.0, 2.0 ** -29, AL.is_equal, AL.mult); TS(k2, pp, 15.0, 2.0 ** -38, AL.not_equal, AL.mult)
+    TT(kr, k1, k2, AL.add)
+    c2 = new("f", 260); ctl2 = new("f", 260)
+    TS(c2, j65, pp, 2.0 ** -14, AL.is_equal, AL.mult); TT(ctl2, c2, n65, AL.mult); MS(sl(ctl2, 0, 260, 65), 2.0 ** 40)
     Dm = new("f", 5); TS(Dm, d5, pp, None, AL.add)
-    e0 = new("f", 5); e1 = new("f", 5); e2 = new("f", 5); e3 = new("f", 5)
-    TS(e0, Dm, 0.0, 2.0 ** 18, AL.is_equal, AL.mult); TS(e1, Dm, 1.0, 512.0, AL.is_equal, AL.mult)
-    TS(e2, Dm, 2.0, None, AL.is_equal); TS(e3, Dm, 0.0, -2.0 ** 19, AL.is_lt, AL.mult)
+    ee = [new("f", 5) for e in range(3)]
+    for e in range(3):
+        TS(ee[e], Dm, float(e), -2.0 ** (18 - 9 * e), AL.is_equal, AL.mult)
+    e3 = new("f", 5); TS(e3, Dm, 0.0, 2.0 ** 19, AL.is_lt, AL.mult)
     f0 = new("f", 5); f1 = new("f", 5); tw = new("f", 5)
-    TT(f0, e0, e1, AL.add); TT(f1, e2, e3, AL.add); TT(tw, f0, f1, AL.add)
-    g0 = new("f", 5); g1 = new("f", 5); g2 = new("f", 5); rw = new("f", 5)
-    TS(g0, e0, 2.0 ** -36, None, AL.mult); TS(g1, e1, 2.0 ** -18, None, AL.mult)
-    TT(g2, g0, g1, AL.add); TT(rw, g2, e2, AL.add)
-    CN = new("b", 48); CM = new("b", 48); RT = new("f", 41)
-    TS(sl(CN, 0, 8), G8, -1.0, None, AL.mult)
+    TT(f0, ee[0], ee[1], AL.add); TT(f1, ee[2], e3, AL.add); TT(tw, f0, f1, AL.add)
+    CN = new("b", 40)
     for a in range(5):
-        TS(sl(CN, 8 * a + 8, 8 * a + 16), G8, sl(tw, a, a + 1), None, AL.mult)
-        AC(sl(RT, 8 * a, 8 * a + 8), G8, AF.Copy, 0.0, sl(rw, a, a + 1))
-    MS(sl(RT, 40, 41), -0.5)
-    TS(CM, CN, -1.0 / 4096, None, AL.mult)
-    REP = new("f", 128)
-    TR(sl(B[7], 128, 256, 1, 41), RT, If)
-    AC(sl(REP, 0, 128, 1, 41), sl(B[7], 128, 256, 1, 41), AF.Copy)
-    OG = new("b", 8); OP = new("b", 8); OT = new("b", 8); EZ = new("b", 128); EN = new("b", 128)
+        TS(sl(CN, 8 * a, 8 * a + 8), G8, sl(tw, a, a + 1), None, AL.mult)
+    REP = new("b", 384)
+    for e in range(3):
+        RT = new("b", 40)
+        for a in range(5):
+            AC(sl(RT, 8 * a, 8 * a + 8), G8, AF.Copy, 0.0, sl(ee[e], a, a + 1))
+        MM(ACC(pt(sl(B[7], 128 * e, 128 * e + 128), 0, 40), [(RT, I)]))
+        AC(pt(sl(REP, 128 * e, 128 * e + 128), 0, 40), pt(sl(B[7], 128 * e, 128 * e + 128), 0, 40), AF.Copy, 0.0,
+           -2.0 ** (9 * e - 10))
+    OG = new("b", 4); OP = new("b", 4); OT = new("b", 4); OU = new("b", 4); ON = new("b", 4)
     s6m = new("f", 1); TS(s6m, s64, -2048.0, None, AL.add)
-    TS(sl(OG, 0, 4), SEL, s6m, 0.5, AL.mult, AL.mult); MS(sl(OG, 4, 8), 0.0)
-    TS(sl(OP, 0, 4), SEL, 1024.0, None, AL.mult); TS(sl(OP, 4, 8), SEL, s64, 0.5, AL.mult, AL.mult)
-    TS(sl(OT, 0, 4), SEL, s64, -0.5, AL.mult, AL.mult); TS(sl(OT, 4, 8), SEL, s64, -0.5, AL.mult, AL.mult)
-    MS(sl(EZ, 4, 128), 0.0); MS(sl(EN, 4, 128), 0.0)
-    TS(sl(EZ, 0, 4), SEL, s64, 0.5, AL.mult, AL.mult); TS(sl(EN, 0, 4), SEL, s64, -0.5, AL.mult, AL.mult)
-    cb = new("f", 1); TS(cb, s64, -1.0 / 64, 15.5, AL.mult, AL.add)
+    TS(OG, SEL, s6m, 0.5, AL.mult, AL.mult); TS(OU, SEL, s6m, -0.5, AL.mult, AL.mult)
+    TS(OP, SEL, s64, 0.5, AL.mult, AL.mult); TS(OT, SEL, s64, -0.5, AL.mult, AL.mult)
+    MS(ON, 16.0)
+    PZ = new("b", 152); TS(PZ, dif2, 0.0, s64, AL.is_equal, AL.mult)
+    RK = new("b", 24)
+    for k in range(1, RO):
+        gk = new("f", 1)
+        TS(gk, s64, 64.0 * k, s64, AL.is_gt, AL.mult)
+        TS(sl(RK, 4 * k, 4 * k + 4), SEL, gk, None, AL.mult)
     thr = [new("f", 1) for t in range(RO)]
     MS(thr[0], 2.0)
     H = []
     for h in range(2):
         d = {}
-        for nm, dt_, n in (("w", "b", 128), ("L", "b", 256), ("rk", "b", 128), ("sig", "b", 384), ("x0", "b", 64), ("cm", "b", 128),
-                           ("hi", "i", 256), ("hj", "i", 256), ("h3", "i", 128),
-                           ("h4", "i", 128), ("h5", "i", 128), ("h6", "i", 128), ("h7", "i", 128), ("hf", "f", 128),
-                           ("off", "u", 128), ("r", "b", 128), ("mw", "b", 128), ("ge", "b", 128), ("gp", "b", 128),
-                           ("gt", "b", 128), ("D", "b", 64), ("e", "b", 64), ("ya", "f", 64), ("yb", "f", 64),
-                           ("Q", "b", 640), ("Rs", "f", 64), ("hh", "f", 64), ("nz", "b", 64), ("U", "b", 64),
-                           ("zU", "b", 64), ("ui", "i", 128), ("uj", "i", 128), ("u3", "i", 64), ("u4", "i", 64),
-                           ("u5", "i", 64), ("u6", "i", 64), ("u7", "i", 64), ("key", "f", 64), ("md", "f", 64),
-                           ("no", "f", 64), ("dd", "f", 256), ("mn", "f", 256), ("fa", "f", 4), ("fb", "f", 4),
-                           ("fc", "f", 4), ("ow", "u", 4), ("wt_", "f", 128), ("sg", "b", 128), ("cd", "b", 128),
-                           ("dl", "b", 128), ("junk", "b", 128), ("Hc", "f", 1), ("ab0", "b", 512), ("ab1", "b", 512)):
+        for nm, dt_, n in (("w", "b", 128), ("rk", "b", 128), ("sig", "b", 384), ("x0", "b", 64), ("zr", "h", 512),
+                           ("r", "i", 256), ("zw", "b", 128), ("cm", "b", 128), ("uv", "f", 256), ("x", "f", 128),
+                           ("fl", "f", 128), ("t", "f", 128),
+                           ("y", "f", 128), ("r2", "b", 128), ("off", "u", 128), ("mw", "b", 128), ("D", "b", 64),
+                           ("yb", "f", 64), ("Q", "b", 640), ("hh", "f", 192), ("nz", "b", 192), ("mj", "b", 64),
+                           ("U", "b", 64), ("zU", "b", 64), ("ur", "b", 128), ("uuv", "f", 128), ("ux", "f", 64),
+                           ("ufl", "f", 64), ("ut", "f", 64), ("uy", "f", 64), ("ur2", "f", 64), ("npl", "f", 64),
+                           ("no", "f", 64), ("dd", "f", 260), ("mn", "f", 260), ("ow", "u", 8), ("Hc", "f", 1),
+                           ("E", "b", 13 * 128), ("ab0", "b", 512), ("ab1", "b", 512)):
             d[nm] = new(dt_, n)
+        d["zl"] = [new("h", 512) for t in range(RO - 1)]
+        d["zs"] = [new("h", 64) for t in range(RO - 1)]
         d["o"] = [new("u", 8), new("u", 8)]
         H.append(d)
-        TS(d["rk"], ones, s64, 1.0 / 64, AL.mult, AL.mult)
+        TS(d["rk"], o128, sc, None, AL.mult)
         AC(d["w"], d["rk"], AF.Exp, 30 * LN2, -3 * LN2)
-        TS(sl(d["L"], 0, 128), ones, s64, None, AL.mult)
-        MS(sl(d["L"], 128, 256), 0.0)
         CP(d["o"][1], KOf)
-        MS(sl(d["Rs"], 0, 64, 1, 64), 1.0)
-    par = [new("f", 1) for k in range(5)]
+    par = new("f", 1)
     fo = new("u", 256)
-    npiece = [0]
 
-    def hashv(src, n, i0, i1, i3, i4, i5, i6, i7):
-        CP(i0, src)
-        TS(i1, i0, 4095, None, AL.bitwise_and)
-        TT(i3, sl(i1, 0, n), sl(i1, n, 2 * n), AL.mult)
-        TS(i5, sl(i1, 0, n), 37.0, None, AL.mult)
-        TS(i4, i3, 5, None, AL.arith_shift_right)
-        TT(i6, i4, i5, AL.add)
-        TS(i7, i6, 8191, None, AL.bitwise_and)
+    def hashf(n, sg, uv, x, fl, t, y, teng):
+        q = sg * sg
+        SC(x, sl(uv, 0, n), sl(uv, n, 2 * n), 0.0, AL.max, AL.mult)
+        if teng == "a":
+            AC(t, sl(uv, 0, n), AF.Identity, 259915760.0 * q, 1184.0 * sg)
+        else:
+            TS(t, sl(uv, 0, n), 1184.0 * sg, 259915760.0 * q, AL.mult, AL.add)
+        TS(fl, x, 8388591.5 * q, (2.0 ** 28 + 2.0 ** 23) * q, AL.add, AL.add)
+        SC(y, t, fl, 0.0, AL.max, AL.subtract)
 
     def front(t, h):
         d = H[h]
         z = sl(zin, 128 * t + 64 * h, 128 * t + 64 * h + 64)
-        MM([(sl(B[0], 64 * k, 64 * k + 64), I, z, True, True) for k in range(8)])
+        zr = d["zr"]
+        part[0] = "front%d" % h
+        if CFG["md"] and t:
+            zr = d["zl"][t - 1]
+            if CFG["md"] == 4:
+                CP(sl(zr, 256, 512), sl(zr, 0, 256))
+        else:
+            TS(sl(zr, 0, 64), z, -1024.0, None, AL.add)
+            TS(sl(zr, 64, 128), z, -1024.0, None, AL.add)
+            CP(sl(zr, 128, 256), sl(zr, 0, 128))
+            CP(sl(zr, 256, 512), sl(zr, 0, 256))
         for q in range(4):
-            TT(sl(zM, 2048 * h + 512 * q, 2048 * h + 512 * q + 512), sl(WM, 2112 * h + 512 * q, 2112 * h + 512 * q + 512),
-               B[0], AL.max)
-        MM([(sl(B[5], b, 256, 16), sl(zM, 2048 * h + b, 2048 * h + 2048, 16), Wh, True, True) for b in range(16)])
-        hashv(sl(B[5], 0, 256), 128, d["hi"], d["hj"], d["h3"], d["h4"], d["h5"], d["h6"], d["h7"])
-        CP(d["hf"], d["h7"])
-        TR(sl(B[5], 256, 384), d["hf"], If)
-        CP(d["off"], sl(B[5], 256, 384))
+            SC(sl(zM, 2048 * h + 512 * q, 2048 * h + 512 * q + 512), zr,
+               sl(WM, 2112 * h + 512 * q, 2112 * h + 512 * q + 512), 0.0, AL.min, AL.mult)
+        MM([(sl(B[0], b, 384, 16), sl(WM, 2112 * h + b, 2112 * h + 2048, 16), WhM[h], b == 0, False) for b in range(16)])
+        MM([(sl(B[0], b, 256, 16), sl(zM, 2048 * h + b, 2048 * h + 2048, 16), WhZ[h], False, b == 15) for b in range(16)])
+        TS(d["r"], sl(B[0], 0, 256), -0.5 + 2.0 ** -13, None, AL.add)
+        TT(sl(d["uv"], 0, 128), sl(B[0], 0, 128), sl(d["r"], 0, 128), AL.subtract)
+        TT(sl(d["uv"], 128, 256), sl(d["r"], 128, 256), sl(B[0], 128, 256), AL.subtract)
+        AC(d["cm"], sl(B[0], 256, 384), AF.Copy)
+        hashf(128, 2.0 ** -12, d["uv"], d["x"], d["fl"], d["t"], d["y"], CFG["t"])
+        if h in CFG["ar"]:
+            AC(d["r2"], d["y"], AF.Identity, 240.0, 64.0)
+        else:
+            TS(d["r2"], d["y"], 64.0, 240.0, AL.mult, AL.add)
+        MM([(sl(B[0], 384, 512), d["y"], If32, True, False)])
+        MM([(sl(B[0], 384, 512), d["r2"], In, False, True)])
+        TS(d["off"], sl(B[0], 384, 512), 240 * 8192 + 4095.5, None, AL.add)
 
     def probe(t, h):
         d = H[h]
         z = sl(zin, 128 * t + 64 * h, 128 * t + 64 * h + 64)
-        for x in range(2):
-            MM([(sl(B[3 + x], 64 + k, 384, 8), sl(WM, 2112 * h + 2 * k + x, 2112 * h + 2048, 16), sl(CM, 8, 48), k == 0, False)
-                for k in range(8)])
-        MM([(sl(B[5], 384 + b, 512, 16), sl(WM, 2112 * h + b, 2112 * h + 2048, 16), sl(CM, 0, 8), True, True) for b in range(16)])
-        AC(d["cm"], sl(B[5], 384, 512), AF.Copy)
-        for q in range(4):
-            xh = sl(WX, 2112 * h + 512 * q, 2112 * h + 512 * q + 512)
-            np_ = sl(NP, 2048 * h + 512 * q, 2048 * h + 512 * q + 512)
-            AC(xh, ("@", sl(X, 0, 8192), sl(d["off"], 32 * q, 32 * q + 32)), AF.Copy)
-            bk = B[1 + npiece[0] % 2]
-            npiece[0] += 1
-            MM(ACC(bk, [(I9, xh), (In9, sl(zM, 2048 * h + 512 * q, 2048 * h + 512 * q + 512))]))
-            if CFG["abs"][q]:
-                ab = d["ab%d" % (q // 2)]
-                AC(ab, bk, AF.Abs)
-                TS(np_, ab, 508.0, None, AL.is_gt)
+        a = 0
+        part[0] = "probe%d" % h
+        for q, n in enumerate(CFG["pc"]):
+            xh = sl(WX, 2112 * h + a, 2112 * h + a + n)
+            np_ = sl(NP, 2048 * h + a, 2048 * h + a + n)
+            src = ("@", sl(X[h], 0, 8192), sl(d["off"], a // 16, (a + n) // 16))
+            if (h, q) in CFG["vg"]:
+                CP(xh, src)
             else:
-                TS(np_, bk, 1.5 * 2.0 ** 33, 1.5 * 2.0 ** 33, AL.add, AL.not_equal)
+                AC(xh, src, AF.Copy)
+            bk = sl(B[1 + q % 2], 0, n)
+            MM([(bk, I9h, sl(zM, 2048 * h + a, 2048 * h + a + n), True, False)])
+            MM([(bk, I9, xh, False, True)])
+            if (h, q) in CFG["abs"]:
+                ab = sl(d["ab%d" % (q % 2)], 0, n)
+                AC(ab, bk, AF.Abs, -9216.0)
+                TS(np_, ab, 508.0, None, AL.is_lt)
+            else:
+                TS(np_, bk, 1.5 * 2.0 ** 33 - 9216, 1.5 * 2.0 ** 33, AL.add, AL.is_equal)
+            a += n
         AC(d["x0"], ("@", sl(WX, 2112 * h, 2112 * h + 2048), sl(d["o"][(t + 1) % 2], 4, 8)), AF.Copy)
-        MM(ACC(sl(B[5], 384, 448), [(Ih, z), (Inh, d["x0"]), (Iq, sl(ones, 0, 64))]))
-        AC(d["yb"], sl(B[5], 384, 448), AF.Identity, C1)
-        AC(sl(WX, 2112 * h + 2048, 2112 * h + 2112), d["yb"], AF.Identity, -C1)
+        av = sl(B[4 + 2 * h], 0, 64)
+        MM(ACC(av, [(Ih, z), (Iq, sl(ones, 0, 64)), (Inh, d["x0"])]))
+        if h in CFG["av"]:
+            AC(d["yb"], av, AF.Identity, C1)
+            AC(sl(WX, 2112 * h + 2048, 2112 * h + 2112), d["yb"], AF.Identity, -C1)
+        else:
+            TS(sl(WX, 2112 * h + 2048, 2112 * h + 2112), av, C1, -C1, AL.add, AL.add)
 
     def back(t, h):
         d = H[h]
@@ -275,63 +345,111 @@ def build():
         z = sl(zin, 128 * t + 64 * h, 128 * t + 64 * h + 64)
         gt, ge, gp = sl(d["sig"], 0, 128), sl(d["sig"], 128, 256), sl(d["sig"], 256, 384)
         w, o = d["w"], d["o"][t % 2]
-        MM([(sl(B[6], 0, 128), I, d["cm"], True, False)]
-           + [(sl(B[6], b, 128, 16), sl(NP, 2048 * h + b, 2048 * h + 2048, 16), sl(CN, 0, 8), False, b == 15) for b in range(16)])
-        AC(d["r"], sl(B[6], 0, 128), AF.Relu, thr[t])
+        F, S7 = [B[3 + 2 * h], B[4 + 2 * h]], B[7]
+        cn = sl(S7, 384, 512)
+        part[0] = "match%d" % h
         for x in range(2):
-            MM([(sl(B[3 + x], 64 + k, 384, 8), sl(NP, 2048 * h + 2 * k + x, 2048 * h + 2048, 16), sl(CN, 8, 48), False, False)
+            MM([(sl(F[x], 64 + k, 384, 8), sl(WM, 2112 * h + 2 * k + x, 2112 * h + 2048, 16), CN, k == 0, False)
                 for k in range(8)])
-        TT(d["mw"], d["r"], w, AL.mult)
-        MM(ACC(sl(B[6], 0, 128), [(I7, w), (B4q, d["mw"])]))
-        AC(gt, sl(B[6], 0, 128), AF.Sign)
-        MM(ACC(sl(B[6], 128, 256), [(I7, w), (B4, d["mw"])]) + ACC(sl(B[6], 256, 384), [(I7, w), (Iw, ones), (B4, d["mw"])]))
-        AC(sl(d["sig"], 128, 384), sl(B[6], 128, 384), AF.Sign)
-        MM(ACC(sl(B[7], 64, 72), [(I, KO), (gt, OT), (ge, OG), (gp, OP)]))
-        CP(o, sl(B[7], 64, 72))
+        MM([(cn, I, d["cm"], True, False)]
+           + [(sl(S7, 384 + b, 512, 16), sl(NP, 2048 * h + b, 2048 * h + 2048, 16), G8, False, b == 15) for b in range(16)])
+        AC(cn, cn, AF.Relu, thr[t])
+        for x in range(2):
+            MM([(sl(F[x], 64 + k, 384, 8), sl(NP, 2048 * h + 2 * k + x, 2048 * h + 2048, 16), CN, False, False)
+                for k in range(8)])
+        TT(d["mw"], cn, w, AL.mult)
+        MM(ACC(sl(S7, 0, 128), [(I7, w), (B4q, d["mw"])]) + ACC(sl(S7, 128, 256), [(I7, w), (B4, d["mw"])]))
+        AC(sl(d["sig"], 0, 256), sl(S7, 0, 256), AF.Sign, 0.0, 1.0, None if last else d["Hc"])
+        MM(ACC(sl(S7, 384, 388), [(I, sl(KO, 0, 4)), (o128, ON), (gt, OU), (ge, OG)])
+           + ACC(sl(S7, 256, 384), [(I7, w), (Iw, o128), (B4, d["mw"])]))
+        CP(sl(o, 0, 4), sl(S7, 384, 388))
+        AC(gp, sl(S7, 256, 384), AF.Sign)
         TT(d["D"], ("@", sl(WX, 2112 * h, 2112 * h + 2112), sl(o, 0, 4)), z, AL.subtract)
         nzr = sl(yzb, 128 * t + 64 * h, 128 * t + 64 * h + 64)
         AC(nzr, d["D"], AF.Abs)
         if not last:
-            add("g", "send", (sl(zin, 128 * t + 128 + 64 * h, 128 * t + 192 + 64 * h), nzr, "ar%d_%d" % (t, h)), [nzr],
-                [sl(zin, 128 * t + 128 + 64 * h, 128 * t + 192 + 64 * h)], 2.5)
-        if h == 0:
-            DMA("s", ("yz", 128 * t, 128 * t + 128, 1, 128), sl(yzb, 128 * t, 128 * t + 128), 2.0)
-        for x in range(2):
-            MM([(sl(B[3 + x], 64 * a + 64, 64 * a + 128), Ig, sl(gt, x, 128, 2), False, a == 4) for a in range(5)])
-            AC(sl(d["Q"], x, 640, 2), sl(B[3 + x], 64, 384), AF.Relu, -2.0 ** 18)
-        MM([(sl(B[7], b, 64, 16, 40), sl(d["Q"], b, 640, 16), SEL, True, True) for b in range(16)])
-        AC(sl(d["Rs"], 0, 64, 1, 40), sl(B[7], 0, 64, 1, 40), AF.Copy)
-        y = sl(B[7], 64, 128)
-        MM(ACC(y, [(sl(REP, 0, 128, 1, 41), sl(d["Rs"], 0, 64, 1, 41))]))
-        TS(d["hh"], y, 1.5 * 2.0 ** 32, -1.5 * 2.0 ** 32, AL.add, AL.add)
-        TT(d["nz"], y, d["hh"], AL.is_lt)
-        TT(d["U"], ("@", sl(WM, 2112 * h, 2112 * h + 2112), sl(o, 0, 4)), d["nz"], AL.mult)
-        CP(("@", sl(WM, 2112 * h, 2112 * h + 2048), sl(o, 4, 8)), d["U"])
+            zn = sl(zin, 128 * t + 128 + 64 * h, 128 * t + 192 + 64 * h)
+            to = [sl(d["zl"][t], 64 * k, 64 * k + 64) for k in range(CFG["md"])]
+            if to:
+                TS(d["zs"][t], nzr, -1024.0, None, AL.add)
+            add("g", "send", (zn, nzr, "ar%d_%d" % (t, h), d["zs"][t], to), [nzr] + ([d["zs"][t]] if to else []), [zn] + to,
+                CFG["send"] + 0.1 * CFG["md"])
+        for f in range(2):
+            DMA("s", half(hbm("yz", 128 * t + 64 * f, 128 * t + 64 * f + 64), h), half(nzr, f), 2.0)
+        part[0] = "mask%d" % h
         if not last:
-            TT(d["zU"], d["U"], z, AL.max)
-            MM(ACC(sl(B[7], 384, 448), [(Wr[0], d["zU"])]) + ACC(sl(B[7], 448, 512), [(Wr[1], d["zU"])]))
-            hashv(sl(B[7], 384, 512), 64, d["ui"], d["uj"], d["u3"], d["u4"], d["u5"], d["u6"], d["u7"])
-            TT(d["md"], NM, d["u7"], AL.subtract)
-            TT(d["key"], d["u7"], ioK, AL.add)
-            SC(d["no"], rs1, d["md"], 0.0, AL.add, AL.min)
-            for c in range(4):
-                AC(sl(d["dd"], 64 * c, 64 * c + 64), d["key"], AF.Abs, sl(d["no"], 16 * c + 15, 16 * c + 16))
-            SC(d["mn"], rs2, d["dd"], 0.0, AL.add, AL.min)
-            TT(d["fa"], sl(d["mn"], 63, 256, 64), rad, AL.is_lt)
-            TT(d["fb"], d["fa"], negt, AL.mult)
-            TT(d["fc"], d["fb"], sl(d["no"], 15, 64, 16), AL.min)
-            TS(d["ow"], d["fc"], -1.0, None, AL.mult)
-            MM(ACC(sl(B[6], 384, 512), [(I, d["rk"]), (Ia, gp), (Ib, gt)]))
-            AC(d["rk"], sl(B[6], 384, 512), AF.Relu, 0.5)
+            MM(ACC(sl(S7, 384, 388), [(I, sl(KO, 4, 8)), (gt, OT), (gp, OP)]))
+            CP(sl(o, 4, 8), sl(S7, 384, 388))
+        AC(d["mj"], ("@", sl(WM, 2112 * h, 2112 * h + 2112), sl(o, 0, 4)), AF.Copy)
+        for x in range(2):
+            MM([(sl(F[x], 64 * a + 64, 64 * a + 128), Ig, sl(gt, x, 128, 2), False, a == 4) for a in range(5)])
+            if (h, x) in CFG["vq"]:
+                TS(sl(d["Q"], x, 640, 2), sl(F[x], 64, 384), -2.0 ** 18, 0.0, AL.add, AL.max)
+            else:
+                AC(sl(d["Q"], x, 640, 2), sl(F[x], 64, 384), AF.Relu, -2.0 ** 18)
+        y = pt(sl(F[0], 0, 192), 0, 40)
+        MM([(y, oh, ones, True, False)])
+        MM([(pt(sl(F[0], b, 192, 16), 0, 40), sl(d["Q"], b, 640, 16), SEL3, False, b == 15) for b in range(16)])
+        hh, nz = pt(d["hh"], 0, 40), pt(d["nz"], 0, 40)
+        TS(hh, y, 1.5 * 2.0 ** 32, -1.5 * 2.0 ** 32, AL.add, AL.add)
+        TT(nz, y, hh, AL.is_ge)
+        Y = sl(F[1], 0, 64)
+        MM(ACC(Y, [(Im, d["mj"])] + [(pt(sl(REP, 128 * e, 128 * e + 128), 0, 40), pt(sl(d["nz"], 64 * e, 64 * e + 64), 0, 40))
+                                     for e in range(3)]))
+        if not last:
+            TT(d["zU"], Y, z, AL.min)
+        if h in CFG["au"]:
+            AC(d["U"], Y, AF.Sign, 0.0, -1.0)
+        else:
+            TS(d["U"], Y, -1.0, -1.0, AL.mult, AL.max)
+        if not last:
+            CP(("@", sl(WM, 2112 * h, 2112 * h + 2048), sl(o, 4, 8)), d["U"])
+        if t == RO - 2:
+            for f in range(2):
+                DMA("s", half(sl(WS, 2048 * f, 2048 * f + 2048), h), half(sl(WM, 2112 * h, 2112 * h + 2048), f), 3.0)
+        part[0] = "rank%d" % h
+        MM(ACC(sl(F[1], 384, 512), [(I, d["rk"]), (Ia, gp), (Ib, gt)]))
+        AC(d["rk"], sl(F[1], 384, 512), AF.Relu, 0.5)
+        if not last:
             AC(w, d["rk"], AF.Exp, 30 * LN2, -3 * LN2)
-            MM(ACC(sl(B[5], 384, 512), [(ones, ge), (nones, gt)]))
-            AC(d["junk"], sl(B[5], 384, 512), AF.Identity, 0.0, 0.5, d["Hc"])
-        MM(ACC(sl(B[6], 384, 512), [(B4, gt)]))
-        AC(d["sg"], sl(B[6], 384, 512), AF.Sign, cb, -0.5)
-        l1, l2 = sl(d["L"], 0, 128), sl(d["L"], 128, 256)
-        MM(ACC(sl(B[7], 128, 256), [(SH, l1), (SH, l2), (EZ, gp), (EN, gt), (Ic, d["sg"])])
-           + ACC(sl(B[7], 256, 384), [(I, l1), (I, l2), (Id, d["sg"])]))
-        AC(d["L"], sl(B[7], 128, 384), AF.Relu, -4096.0)
+            part[0] = "write%d" % h
+            MM([(sl(F[1], 128 + 64 * f, 192 + 64 * f), PH[f], z, True, True) for f in range(2)])
+            AC(d["zw"], sl(F[1], 128, 256), AF.Copy)
+            MM([(sl(F[0], 384, 512), o32, OFF, True, False)])
+            MM([(sl(F[0], 256 + 64 * k, 320 + 64 * k), Wr[h][k % 2], d["zU"], False, k == 3) for k in range(4)])
+            TS(d["ur"], sl(F[0], 384, 512), 1.5 * 2.0 ** 40, -1.5 * 2.0 ** 40, AL.add, AL.add)
+            TT(d["uuv"], sl(F[0], 256, 384), d["ur"], AL.subtract)
+            hashf(64, 32.0, d["uuv"], d["ux"], d["ufl"], d["ut"], d["uy"], CFG["ut"])
+            TS(d["ur2"], d["uy"], 1.5 * 2.0 ** 51, -(1.5 * 2.0 ** 51 + 2.0 ** 29), AL.add, AL.add)
+            TT(d["npl"], d["ur2"], d["uy"], AL.subtract)
+            SC(d["no"], ctl1, d["npl"], 0.0, AL.mult, AL.min)
+            for c in range(4):
+                if (h, c) in CFG["ve"]:
+                    TS(sl(d["dd"], 65 * c, 65 * c + 64), d["npl"], kp, sl(d["no"], 16 * c + 15, 16 * c + 16), AL.mult, AL.not_equal)
+                else:
+                    AC(sl(d["dd"], 65 * c, 65 * c + 64), d["npl"], AF.Abs, sl(d["no"], 16 * c + 15, 16 * c + 16), kn)
+            if h in CFG["ap"]:
+                AC(sl(d["dd"], 64, 260, 65), sl(d["no"], 15, 64, 16), AF.Identity, 12288.5 / 16384, kr)
+            else:
+                TS(sl(d["dd"], 64, 260, 65), sl(d["no"], 15, 64, 16), kr, 12288.5 / 16384, AL.mult, AL.add)
+            SC(d["mn"], ctl2, d["dd"], 0.0, AL.add, AL.min)
+            MM([(sl(F[0], 4 * f, 4 * f + 4), PF[f], sl(d["mn"], 64, 260, 65), True, True) for f in range(2)])
+            CP(d["ow"], sl(F[0], 0, 8))
+            for f in (1, 0):
+                CP(("@", X[h], sl(d["ow"], 4 * f, 4 * f + 4)), sl(d["zw"], 64 * f, 64 * f + 64))
+        else:
+            E = [sl(d["E"], 128 * k, 128 * k + 128) for k in range(13)]
+            for k in range(7):
+                TS(E[k], d["rk"], sc, float(k), AL.subtract, AL.is_equal)
+            for k in range(1, 6):
+                TS(E[7 + k], d["rk"], float(k), None, AL.is_equal)
+            for f in range(2):
+                L = half(sl(B[0], 128 * f, 128 * f + 128), h)
+                MM([(L, sl(E[k], 64 * f, 64 * f + 64), sl(PZ, 24 - 4 * k, 152 - 4 * k), k == 0, False) for k in range(7)]
+                   + [(sl(L, 4 * k, 4 * k + 4), sl(E[7 + k], 64 * f, 64 * f + 64), sl(RK, 4 * k, 4 * k + 4), False, k == 5)
+                      for k in range(1, 6)])
+            MM([(half(sl(B[0], 256 + 64 * f, 320 + 64 * f), h), sl(Ine, 64 * f, 64 * f + 64), d["U"], True, True)
+                for f in range(2)])
 
     for t in range(RO):
         for h in (1, 0):
@@ -340,32 +458,31 @@ def build():
             probe(t, h)
             back(t, h)
         if t < RO - 1:
-            for h in (1, 0):
-                CP(("@", X, H[h]["ow"]), sl(zin, 128 * t + 64 * h, 128 * t + 64 * h + 64))
-            AC(par[0], H[0]["Hc"], AF.Identity, H[1]["Hc"])
-            AC(par[1], par[0], AF.Identity, -0.25, 0.5)
-            AC(par[2], par[1], AF.Identity, C1)
-            AC(par[3], par[2], AF.Identity, 2 * C1 + 2, -2.0)
-            AC(thr[t + 1], par[3], AF.Identity, par[0])
-    for h in (1, 0):
-        MM(ACC(sl(B[7], 256, 384), [(sl(H[h]["L"], 0, 128), I), (sl(H[h]["L"], 128, 256), I)]))
+            tot = sl(B[7], 0, 1)
+            MM(ACC(tot, [(halff, H[1]["Hc"]), (halff, H[0]["Hc"])]))
+            TS(par, tot, 1.5 * 2.0 ** 24, -1.5 * 2.0 ** 24, AL.add, AL.add)
+            TS(thr[t + 1], par, tot, 2.0, AL.not_equal, AL.add)
+    part[0] = "end"
+    for f in range(2):
         for c in range(4):
-            TS(sl(fo, 4 * h + c, 256, 8), sl(B[7], 256 + c, 384, 4), sl(KOf, c, c + 1), 2112.0 * h, AL.add, AL.add)
+            TS(sl(fo, 4 * f + c, 256, 8), sl(B[0], 128 * f + c, 128 * f + 128, 4), sl(KOf, c, c + 1), 2048.0 * f, AL.add, AL.add)
+    AC(sl(ymb, 0, 128), sl(B[0], 256, 384), AF.Copy)
     for q in range(8):
-        src = ("@", WM, sl(fo, 32 * q, 32 * q + 32))
-        dst = sl(ymb, 512 * q, 512 * q + 512)
+        a = 128 if q == 0 else 512 * q
+        src = ("@", WS, sl(fo, a // 16, 32 * q + 32))
+        dst = sl(ymb, a, 512 * q + 512)
         if q % 2:
-            AC(dst, src, AF.Identity, 1.0, -1.0 / 4096)
-            DMA("s", ("ym", 512 * q - 512, 512 * q + 512, 1, 128), sl(ymb, 512 * q - 512, 512 * q + 512), 2.5)
+            AC(dst, src, AF.Copy, 0.0, -1.0)
+            DMA("s", hbm("ym", 512 * q - 512, 512 * q + 512), sl(ymb, 512 * q - 512, 512 * q + 512), 2.5)
         else:
-            TS(dst, src, -1.0 / 4096, 1.0, AL.mult, AL.add)
+            TS(dst, src, -1.0, None, AL.mult)
     for k in used:
         SCRATCH["p" + k] = ("sbuf", [128, used[k]], DT[k])
     return ops
 
 
 def meets(a, b):
-    if a[0] != b[0] or a[1] >= b[2] or b[1] >= a[2]:
+    if a[0] != b[0] or a[1] >= b[2] or b[1] >= a[2] or a[5] >= b[4] or b[5] >= a[4]:
         return False
     if a[3] > 1 and a[3] == b[3] and a[0] != "pu" and (a[1] - b[1]) % a[3]:
         return False
@@ -386,8 +503,9 @@ def schedule(ops):
             for (j, q, wr) in lst:
                 if meets(q, r):
                     dep.add(j)
-            if o["e"] != "p":
-                hist[r[0]] = [x for x in lst if not (r[3] == 1 and r[4] >= x[1][4] and r[1] <= x[1][1] and x[1][2] <= r[2])]
+            if o["e"] != "p" or r[0][0] == "G":
+                hist[r[0]] = [x for x in lst if not (r[3] == 1 and r[5] <= x[1][5] and r[4] >= x[1][4]
+                                                     and r[1] <= x[1][1] and x[1][2] <= r[2])]
         for r in o["r"]:
             hist.setdefault(r[0], []).append((i, r, False))
         for r in o["w"]:
@@ -397,50 +515,71 @@ def schedule(ops):
         dep.discard(i)
         o["d"] = dep
         o["b"] = sorted(set(r[0] for r in o["r"] + o["w"] if r[0][0] == "B"))
-    lat = 0.1
+    lat = CFG["lat"]
     succ = [[] for k in range(n)]
     for i, o in enumerate(ops):
         for j in o["d"]:
             succ[j].append(i)
+    busy = [0.1 if o["k"] == "dma" else 0.4 if o["k"] == "send" else o["c"] for o in ops]
     pr = [0.0] * n
     for i in range(n - 1, -1, -1):
         pr[i] = ops[i]["c"] + max([pr[j] + lat for j in succ[i]] + [0.0])
-    left = [len(o["d"]) for o in ops]
-    ready = [i for i in range(n) if left[i] == 0]
-    free = {}
-    fin = [0.0] * n
-    bank = {}
-    order = []
-    while ready:
-        est = {}
-        for i in ready:
+    key = [-pr[i] - CFG["ahead"].get(ops[i]["n"], 0.0) for i in range(n)]
+
+    def run(key, before, after):
+        left = [len(before[i]) for i in range(n)]
+        can = [0.0] * n
+        ready = [i for i in range(n) if left[i] == 0]
+        free = {}
+        held = {}
+        st = [0.0] * n
+        while ready:
+            est = {}
+            for i in ready:
+                o = ops[i]
+                s = max(can[i], free.get(o["e"], 0.0))
+                for b in o["b"]:
+                    for e, f in held.get(b, {}).items():
+                        if e != o["e"]:
+                            s = max(s, f + lat)
+                est[i] = s
+            i0 = min(ready, key=lambda i: (est[i], key[i]))
+            c = [i for i in ready if ops[i]["e"] == ops[i0]["e"] and est[i] <= est[i0] + CFG["slack"]]
+            i = min(c, key=lambda k: key[k] + CFG["pen"] * (est[k] - est[i0]))
             o = ops[i]
-            s = free.get(o["e"], 0.0)
-            for j in o["d"]:
-                s = max(s, fin[j] + (0.0 if o["e"] == "p" and ops[j]["e"] == "p" else lat))
+            st[i] = est[i]
             for b in o["b"]:
-                for e, j in bank.get(b, {}).items():
-                    if e != o["e"]:
-                        s = max(s, fin[j] + lat)
-            est[i] = s
-        i0 = min(ready, key=lambda i: (est[i], -pr[i]))
-        c = [i for i in ready if ops[i]["e"] == ops[i0]["e"] and est[i] <= est[i0] + CFG["slack"]]
-        i = max(c, key=lambda k: pr[k] - 2 * (est[k] - est[i0]))
+                held.setdefault(b, {})[o["e"]] = est[i] + o["c"]
+            free[o["e"]] = est[i] + busy[i]
+            ready.remove(i)
+            for j in after[i]:
+                can[j] = max(can[j], est[i] + o["c"] + (0.0 if o["e"] == "p" and ops[j]["e"] == "p" else lat))
+                left[j] -= 1
+                if left[j] == 0:
+                    ready.append(j)
+        return st
+
+    best = None
+    pre = [o["d"] for o in ops]
+    for turn in range(CFG["turns"]):
+        st = run(key, pre, succ)
+        end = max(st[i] + ops[i]["c"] for i in range(n))
+        if best is None or end < best[0]:
+            best = (end, st)
+        if turn + 1 < CFG["turns"]:
+            bw = run([-(st[i] + ops[i]["c"]) for i in range(n)], succ, pre)
+            key = [-(bw[i] + ops[i]["c"]) for i in range(n)]
+    span = best[0]
+    order = sorted(range(n), key=lambda i: (best[1][i], i))
+    bank = {}
+    for i in order:
         o = ops[i]
+        o["s"] = best[1][i]
         for b in o["b"]:
             for e, j in bank.get(b, {}).items():
                 if e != o["e"]:
                     o["d"].add(j)
             bank.setdefault(b, {})[o["e"]] = i
-        o["s"] = est[i]
-        fin[i] = est[i] + o["c"]
-        free[o["e"]] = est[i] + (0.1 if o["k"] == "dma" else 0.4 if o["k"] == "send" else o["c"])
-        order.append(i)
-        ready.remove(i)
-        for j in succ[i]:
-            left[j] -= 1
-            if left[j] == 0:
-                ready.append(j)
     pos = {}
     for k, i in enumerate(order):
         pos[i] = k
@@ -469,7 +608,7 @@ def schedule(ops):
         if o["k"] == "dma":
             o["sem"] = ("d%d" % i, 16)
         elif o["k"] == "send":
-            o["sem"] = (o["a"][2], CFG["eng"])
+            o["sem"] = (o["a"][2], 4 + 4 * CFG["md"] if CFG["md"] else CFG["eng"])
         elif i in need:
             tot["q" + o["e"]] = tot.get("q" + o["e"], 0) + 1
             o["sem"] = ("q" + o["e"], tot["q" + o["e"]])
@@ -477,7 +616,7 @@ def schedule(ops):
             o["sem"] = None
         if o["sem"] and o["sem"][0] not in sems:
             sems.append(o["sem"][0])
-    return order, sems, max(fin)
+    return order, sems, span
 
 
 OPS = build()
@@ -493,6 +632,7 @@ def rank_program(g, core, T, topo):
     mask = 0
     for e in topo.engines(core, nxt)[0:CFG["eng"]]:
         mask |= 1 << e
+    quad = [sum(1 << e for e in topo.engines(core, nxt)[k::4]) for k in range(4)]
     Q = {"v": g.vector, "a": g.scalar, "p": g.tensor, "s": g.sync, "g": g}
 
     def ap(r):
@@ -501,8 +641,8 @@ def rank_program(g, core, T, topo):
         if r[0] == "@":
             return ap(r[1]).indirect(ap(r[2]))
         if r[3] == 1:
-            return T[r[0]][0:r[4], r[1]:r[2]]
-        return T[r[0]][0:r[4], r[1]:r[2]:r[3]]
+            return T[r[0]][r[5]:r[4], r[1]:r[2]]
+        return T[r[0]][r[5]:r[4], r[1]:r[2]:r[3]]
 
     ends = {}
     sent = 0
@@ -514,9 +654,19 @@ def rank_program(g, core, T, topo):
         for j in o["wt"]:
             q.wait_ge(T.sem[OPS[j]["sem"][0]], OPS[j]["sem"][1])
         if k == "send":
-            g.remote_dma(ap(a[0]), ap(a[1]), T.sem[a[2]], T.sem["loc"], pid, rid, mask)
-            sent += CFG["eng"]
-            ends[a[2]] = CFG["eng"]
+            if a[4]:
+                to = DstId(rid=rid, pnc=pid)
+                tr = [RemoteDMATransfer(dst_ids=[to], dma_engine_mask=quad[0], remote_sem=T.sem[a[2]], src=ap(a[1]), dst=ap(a[0]))]
+                for e in range(3):
+                    ds = [ap(r) for r in a[4][e::3]]
+                    tr.append(RemoteDMATransfer(dst_ids=[to] * len(ds), dma_engine_mask=quad[e + 1], remote_sem=T.sem[a[2]],
+                                                src=ap(a[3]), dsts=ds))
+                g.remote_dma_fused(tr, local_sem=T.sem["loc"])
+                sent += 16
+            else:
+                g.remote_dma(ap(a[0]), ap(a[1]), T.sem[a[2]], T.sem["loc"], pid, rid, mask)
+                sent += CFG["eng"]
+            ends[a[2]] = o["sem"][1]
             continue
         if k == "ts":
             if a[5] is None:
@@ -539,8 +689,6 @@ def rank_program(g, core, T, topo):
         elif k == "mm":
             for m in a:
                 x = q.matmul(ap(m[0]), ap(m[1]), ap(m[2]), m[3], m[4])
-        elif k == "tr":
-            x = q.transpose(ap(a[0]), ap(a[1]), ap(a[2]))
         elif k == "io":
             if a[0][0] == "pf":
                 x = g.iota(ap(a[0]), a[1], a[2], a[3], allow_small_or_imprecise_dtypes=True)

@@ -3,9 +3,9 @@ from concourse.mybir import AluOpType as AL, ActivationFunctionType as AF
 
 RO = 6
 PARTS = ("front", "probe", "match", "mask", "rank", "write")
-CFG = {"abs": (), "vg": (), "vq": (), "au": (0, 1), "ve": (), "ap": (0, 1), "av": (), "ar": (0, 1), "t": "a", "ut": "a",
-       "md": 0, "eng": 16, "send": 2.0, "xl": 10.0, "lat": 0.1, "turns": 3, "slack": 0.0, "pen": 2.0,
-       "ahead": {p + "1": 3.0 for p in PARTS}, "pc": (512, 512, 512, 512)}
+CFG = {"abs": (), "vg": (), "vq": (), "au": (0, 1), "ve": (), "ap": (0, 1), "av": (0, 1), "ar": (0, 1), "t": "a", "ut": "a",
+       "raw": 0, "sx": 0, "sd": (), "d0": 0, "y7": 0, "md": 8, "eng": 16, "send": 2.0, "xl": 10.0, "lat": 0.1, "turns": 5, "more": 0, "step": 0.1, "slack": 0.0, "pen": 2.0,
+       "lead": (0, 1, 1.5, 2, 2.5, 3, 3.5, 4, 5), "vl": (1,), "pc": (512, 512, 512, 512)}
 DT = {"f": "float32", "i": "int32", "b": "bfloat16", "u": "uint16", "h": "float16"}
 SCRATCH = {}
 LN2 = 0.6931471805599453
@@ -15,7 +15,8 @@ C1 = 1.5 * 2.0 ** 23
 
 def build():
     ops = []
-    part = ["const"]
+    part = ["const", 0]
+    roles = set()
     used = {"f": 0, "i": 0, "b": 0, "u": 0, "h": 0}
 
     def new(d, n):
@@ -65,7 +66,11 @@ def build():
         for r in R + W:
             if r[0][0] == "B":
                 (W if e == "p" else R).append(("G" + r[0], 0, 1, 1, 128, 0))
-        ops.append({"e": e, "k": k, "a": a, "r": R, "w": W, "c": cost, "n": part[0]})
+        role = (part[1], part[0], e, k, W[0][0], W[0][1] % (128 if W[0][0] in ("zin", "yzb", "yz") else 1 << 20), 0)
+        while role in roles:
+            role = role[:6] + (role[6] + 1,)
+        roles.add(role)
+        ops.append({"e": e, "k": k, "a": a, "r": R, "w": W, "c": cost, "n": part[0], "role": role})
 
     def vc(out, ins, tt=False):
         n = cnt(out)
@@ -241,7 +246,8 @@ def build():
         TS(gk, s64, 64.0 * k, s64, AL.is_gt, AL.mult)
         TS(sl(RK, 4 * k, 4 * k + 4), SEL, gk, None, AL.mult)
     thr = [new("f", 1) for t in range(RO)]
-    MS(thr[0], 2.0)
+    MS(thr[0], -1.0 if CFG["sx"] else 2.0)
+    I40 = scaled(I, 40.0)
     H = []
     for h in range(2):
         d = {}
@@ -297,8 +303,9 @@ def build():
         TS(d["r"], sl(B[0], 0, 256), -0.5 + 2.0 ** -13, None, AL.add)
         TT(sl(d["uv"], 0, 128), sl(B[0], 0, 128), sl(d["r"], 0, 128), AL.subtract)
         TT(sl(d["uv"], 128, 256), sl(d["r"], 128, 256), sl(B[0], 128, 256), AL.subtract)
-        AC(d["cm"], sl(B[0], 256, 384), AF.Copy)
         hashf(128, 2.0 ** -12, d["uv"], d["x"], d["fl"], d["t"], d["y"], CFG["t"])
+        AC(d["cm"], sl(B[0], 256, 384), AF.Copy)
+        ops[-1]["r"].append(d["t"])
         if h in CFG["ar"]:
             AC(d["r2"], d["y"], AF.Identity, 240.0, 64.0)
         else:
@@ -316,7 +323,7 @@ def build():
             xh = sl(WX, 2112 * h + a, 2112 * h + a + n)
             np_ = sl(NP, 2048 * h + a, 2048 * h + a + n)
             src = ("@", sl(X[h], 0, 8192), sl(d["off"], a // 16, (a + n) // 16))
-            if (h, q) in CFG["vg"]:
+            if (h, q) in CFG["vg"] or (t == RO - 1 and h == 0 and q in CFG["vl"]):
                 CP(xh, src)
             else:
                 AC(xh, src, AF.Copy)
@@ -353,20 +360,30 @@ def build():
                 for k in range(8)])
         MM([(cn, I, d["cm"], True, False)]
            + [(sl(S7, 384 + b, 512, 16), sl(NP, 2048 * h + b, 2048 * h + 2048, 16), G8, False, b == 15) for b in range(16)])
-        AC(cn, cn, AF.Relu, thr[t])
+        if CFG["sx"]:
+            AC(d["cm"], cn, AF.Relu, thr[t], -1.0)
+            MM(ACC(cn, [(I, d["rk"]), (I40, d["cm"])]))
+            AC(d["mw"], cn, AF.Exp, 30 * LN2, -3 * LN2)
+        else:
+            AC(cn, cn, AF.Relu, thr[t])
+            TT(d["mw"], cn, w, AL.mult)
         for x in range(2):
             MM([(sl(F[x], 64 + k, 384, 8), sl(NP, 2048 * h + 2 * k + x, 2048 * h + 2048, 16), CN, False, False)
                 for k in range(8)])
-        TT(d["mw"], cn, w, AL.mult)
         MM(ACC(sl(S7, 0, 128), [(I7, w), (B4q, d["mw"])]) + ACC(sl(S7, 128, 256), [(I7, w), (B4, d["mw"])]))
         AC(sl(d["sig"], 0, 256), sl(S7, 0, 256), AF.Sign, 0.0, 1.0, None if last else d["Hc"])
-        MM(ACC(sl(S7, 384, 388), [(I, sl(KO, 0, 4)), (o128, ON), (gt, OU), (ge, OG)])
-           + ACC(sl(S7, 256, 384), [(I7, w), (Iw, o128), (B4, d["mw"])]))
+        MM(ACC(sl(S7, 384, 388), [(I, sl(KO, 0, 4)), (o128, ON), (gt, OU), (ge, OG)]))
         CP(sl(o, 0, 4), sl(S7, 384, 388))
+        MM(ACC(sl(S7, 256, 384), [(I7, w), (Iw, o128), (B4, d["mw"])]))
         AC(gp, sl(S7, 256, 384), AF.Sign)
-        TT(d["D"], ("@", sl(WX, 2112 * h, 2112 * h + 2112), sl(o, 0, 4)), z, AL.subtract)
         nzr = sl(yzb, 128 * t + 64 * h, 128 * t + 64 * h + 64)
-        AC(nzr, d["D"], AF.Abs)
+        if h in CFG["sd"]:
+            AC(d["D"], ("@", sl(WX, 2112 * h, 2112 * h + 2112), sl(o, 0, 4)), AF.Copy)
+            MM(ACC(sl(S7, 400, 464), [(Ine, z), (I, d["D"])]))
+            AC(nzr, sl(S7, 400, 464), AF.Abs)
+        else:
+            TT(d["D"], ("@", sl(WX, 2112 * h, 2112 * h + 2112), sl(o, 0, 4)), z, AL.subtract)
+            AC(nzr, d["D"], AF.Abs)
         if not last:
             zn = sl(zin, 128 * t + 128 + 64 * h, 128 * t + 192 + 64 * h)
             to = [sl(d["zl"][t], 64 * k, 64 * k + 64) for k in range(CFG["md"])]
@@ -387,10 +404,14 @@ def build():
                 TS(sl(d["Q"], x, 640, 2), sl(F[x], 64, 384), -2.0 ** 18, 0.0, AL.add, AL.max)
             else:
                 AC(sl(d["Q"], x, 640, 2), sl(F[x], 64, 384), AF.Relu, -2.0 ** 18)
-        y = pt(sl(F[0], 0, 192), 0, 40)
+        yb = S7 if CFG["y7"] and not last else F[0]
+        y = pt(sl(yb, 0, 192), 0, 40)
         MM([(y, oh, ones, True, False)])
-        MM([(pt(sl(F[0], b, 192, 16), 0, 40), sl(d["Q"], b, 640, 16), SEL3, False, b == 15) for b in range(16)])
-        hh, nz = pt(d["hh"], 0, 40), pt(d["nz"], 0, 40)
+        MM([(pt(sl(yb, b, 192, 16), 0, 40), sl(d["Q"], b, 640, 16), SEL3, False, b == 15) for b in range(16)])
+        a = 64 if CFG["d0"] else 0
+        if a:
+            AC(pt(sl(d["nz"], 0, 64), 0, 40), pt(sl(yb, 0, 64), 0, 40), AF.Relu, 0.0, 2.0)
+        hh, nz, y = pt(sl(d["hh"], a, 192), 0, 40), pt(sl(d["nz"], a, 192), 0, 40), sl(y, a, 192)
         TS(hh, y, 1.5 * 2.0 ** 32, -1.5 * 2.0 ** 32, AL.add, AL.add)
         TT(nz, y, hh, AL.is_ge)
         Y = sl(F[1], 0, 64)
@@ -408,8 +429,9 @@ def build():
             for f in range(2):
                 DMA("s", half(sl(WS, 2048 * f, 2048 * f + 2048), h), half(sl(WM, 2112 * h, 2112 * h + 2048), f), 3.0)
         part[0] = "rank%d" % h
-        MM(ACC(sl(F[1], 384, 512), [(I, d["rk"]), (Ia, gp), (Ib, gt)]))
-        AC(d["rk"], sl(F[1], 384, 512), AF.Relu, 0.5)
+        rb = sl(S7, 0, 128) if last else sl(F[1], 384, 512)
+        MM(ACC(rb, [(I, d["rk"]), (Ia, gp), (Ib, gt)]))
+        AC(d["rk"], rb, AF.Relu, 0.5)
         if not last:
             AC(w, d["rk"], AF.Exp, 30 * LN2, -3 * LN2)
             part[0] = "write%d" % h
@@ -421,7 +443,7 @@ def build():
             TT(d["uuv"], sl(F[0], 256, 384), d["ur"], AL.subtract)
             hashf(64, 32.0, d["uuv"], d["ux"], d["ufl"], d["ut"], d["uy"], CFG["ut"])
             TS(d["ur2"], d["uy"], 1.5 * 2.0 ** 51, -(1.5 * 2.0 ** 51 + 2.0 ** 29), AL.add, AL.add)
-            TT(d["npl"], d["ur2"], d["uy"], AL.subtract)
+            SC(d["npl"], d["ur2"], d["uy"], 0.0, AL.min, AL.subtract)
             SC(d["no"], ctl1, d["npl"], 0.0, AL.mult, AL.min)
             for c in range(4):
                 if (h, c) in CFG["ve"]:
@@ -443,15 +465,17 @@ def build():
                 TS(E[k], d["rk"], sc, float(k), AL.subtract, AL.is_equal)
             for k in range(1, 6):
                 TS(E[7 + k], d["rk"], float(k), None, AL.is_equal)
-            for f in range(2):
-                L = half(sl(B[0], 128 * f, 128 * f + 128), h)
-                MM([(L, sl(E[k], 64 * f, 64 * f + 64), sl(PZ, 24 - 4 * k, 152 - 4 * k), k == 0, False) for k in range(7)]
-                   + [(sl(L, 4 * k, 4 * k + 4), sl(E[7 + k], 64 * f, 64 * f + 64), sl(RK, 4 * k, 4 * k + 4), False, k == 5)
-                      for k in range(1, 6)])
-            MM([(half(sl(B[0], 256 + 64 * f, 320 + 64 * f), h), sl(Ine, 64 * f, 64 * f + 64), d["U"], True, True)
+            L = [half(sl(B[0], 128 * f, 128 * f + 128), h) for f in range(2)]
+            for k in range(7):
+                MM([(L[f], sl(E[k], 64 * f, 64 * f + 64), sl(PZ, 24 - 4 * k, 152 - 4 * k), k + f == 0, False) for f in range(2)])
+            for k in range(1, 6):
+                MM([(sl(L[f], 4 * k, 4 * k + 4), sl(E[7 + k], 64 * f, 64 * f + 64), sl(RK, 4 * k, 4 * k + 4), False, k + f == 6)
+                    for f in range(2)])
+            MM([(half(sl(B[5], 256 + 64 * f, 320 + 64 * f), h), sl(Ine, 64 * f, 64 * f + 64), d["U"], True, True)
                 for f in range(2)])
 
     for t in range(RO):
+        part[1] = t
         for h in (1, 0):
             front(t, h)
         for h in (1, 0):
@@ -461,12 +485,15 @@ def build():
             tot = sl(B[7], 0, 1)
             MM(ACC(tot, [(halff, H[1]["Hc"]), (halff, H[0]["Hc"])]))
             TS(par, tot, 1.5 * 2.0 ** 24, -1.5 * 2.0 ** 24, AL.add, AL.add)
-            TS(thr[t + 1], par, tot, 2.0, AL.not_equal, AL.add)
+            if CFG["sx"]:
+                TS(thr[t + 1], par, tot, -2.0, AL.is_equal, AL.add)
+            else:
+                TS(thr[t + 1], par, tot, 2.0, AL.not_equal, AL.add)
     part[0] = "end"
     for f in range(2):
         for c in range(4):
             TS(sl(fo, 4 * f + c, 256, 8), sl(B[0], 128 * f + c, 128 * f + 128, 4), sl(KOf, c, c + 1), 2048.0 * f, AL.add, AL.add)
-    AC(sl(ymb, 0, 128), sl(B[0], 256, 384), AF.Copy)
+    AC(sl(ymb, 0, 128), sl(B[5], 256, 384), AF.Copy)
     for q in range(8):
         a = 128 if q == 0 else 512 * q
         src = ("@", WS, sl(fo, a // 16, 32 * q + 32))
@@ -484,7 +511,7 @@ def build():
 def meets(a, b):
     if a[0] != b[0] or a[1] >= b[2] or b[1] >= a[2] or a[5] >= b[4] or b[5] >= a[4]:
         return False
-    if a[3] > 1 and a[3] == b[3] and a[0] != "pu" and (a[1] - b[1]) % a[3]:
+    if a[3] > 1 and a[3] == b[3] and (a[1] - b[1]) % a[3]:
         return False
     return True
 
@@ -498,6 +525,7 @@ def schedule(ops):
             for (j, q, wr) in hist.get(r[0], []):
                 if wr and meets(q, r):
                     dep.add(j)
+        o["raw"] = set(dep) if CFG["raw"] else None
         for r in o["w"]:
             lst = hist.get(r[0], [])
             for (j, q, wr) in lst:
@@ -524,7 +552,12 @@ def schedule(ops):
     pr = [0.0] * n
     for i in range(n - 1, -1, -1):
         pr[i] = ops[i]["c"] + max([pr[j] + lat for j in succ[i]] + [0.0])
-    key = [-pr[i] - CFG["ahead"].get(ops[i]["n"], 0.0) for i in range(n)]
+
+    def waits(i, j):
+        a, b = ops[min(i, j)], ops[max(i, j)]
+        if a["e"] != b["e"] or a["k"] in ("dma", "send") or b["k"] in ("dma", "send"):
+            return True
+        return a["e"] != "p" and (b["raw"] is None or min(i, j) in b["raw"])
 
     def run(key, before, after):
         left = [len(before[i]) for i in range(n)]
@@ -553,7 +586,7 @@ def schedule(ops):
             free[o["e"]] = est[i] + busy[i]
             ready.remove(i)
             for j in after[i]:
-                can[j] = max(can[j], est[i] + o["c"] + (0.0 if o["e"] == "p" and ops[j]["e"] == "p" else lat))
+                can[j] = max(can[j], est[i] + o["c"] + (lat if waits(i, j) else 0.0))
                 left[j] -= 1
                 if left[j] == 0:
                     ready.append(j)
@@ -561,14 +594,95 @@ def schedule(ops):
 
     best = None
     pre = [o["d"] for o in ops]
-    for turn in range(CFG["turns"]):
-        st = run(key, pre, succ)
-        end = max(st[i] + ops[i]["c"] for i in range(n))
-        if best is None or end < best[0]:
-            best = (end, st)
-        if turn + 1 < CFG["turns"]:
-            bw = run([-(st[i] + ops[i]["c"]) for i in range(n)], succ, pre)
-            key = [-(bw[i] + ops[i]["c"]) for i in range(n)]
+    for lead in CFG["lead"]:
+        key = [-pr[i] - (lead if ops[i]["n"][-1] == "1" else 0.0) for i in range(n)]
+        for turn in range(CFG["turns"]):
+            st = run(key, pre, succ)
+            end = max(st[i] + ops[i]["c"] for i in range(n))
+            if best is None or end < best[0]:
+                best = (end, st, key)
+            if turn + 1 < CFG["turns"]:
+                bw = run([-(st[i] + ops[i]["c"]) for i in range(n)], succ, pre)
+                key = [-(bw[i] + ops[i]["c"]) for i in range(n)]
+    seq = sorted(range(n), key=lambda i: (best[1][i], i))
+    eng = [o["e"] for o in ops]
+    cost = [o["c"] for o in ops]
+    bks = [o["b"] for o in ops]
+    prl = [[(j, cost[j] + (lat if waits(i, j) else 0.0)) for j in pre[i]] for i in range(n)]
+
+    def times(seq):
+        st = [0.0] * n
+        why = [-1] * n
+        free = {}
+        held = {}
+        for i in seq:
+            s, y = free.get(eng[i], (0.0, -1))
+            for j, c in prl[i]:
+                if st[j] + c > s:
+                    s, y = st[j] + c, -2 - j
+            for b in bks[i]:
+                hb = held.get(b)
+                if hb is None:
+                    held[b] = hb = {}
+                for e in hb:
+                    if e != eng[i] and hb[e][0] > s:
+                        s, y = hb[e]
+                hb[eng[i]] = None
+            st[i] = s
+            why[i] = y
+            free[eng[i]] = (s + busy[i], i)
+            for b in bks[i]:
+                held[b][eng[i]] = (s + cost[i] + lat, i)
+        last = max(range(n), key=lambda i: st[i] + cost[i])
+        return st[last] + cost[last], st, why, last
+
+    def move(seq, y, i, up):
+        a, b = seq.index(y), seq.index(i)
+        if a > b:
+            return seq
+        mid = seq[a:b + 1]
+        mv = {i if up else y}
+        for j in (mid[::-1] if up else mid):
+            if j in mv:
+                mv.update(pre[j] if up else succ[j])
+        if (y if up else i) in mv:
+            return seq
+        ins = [j for j in mid if j in mv]
+        out = [j for j in mid if j not in mv]
+        return seq[:a] + (ins + out if up else out + ins) + seq[b + 1:]
+
+    same = {}
+    for i, o in enumerate(ops):
+        same[o["role"]] = i
+    cur = times(seq)
+    top = (cur[0], cur[1])
+    rnd = 12345
+    for turn in range(CFG["more"]):
+        pairs = []
+        i = cur[3]
+        while i != -1:
+            y = cur[2][i]
+            if y >= 0 and y not in pre[i]:
+                pairs.append((y, i))
+            i = y if y >= -1 else -2 - y
+        if not pairs:
+            break
+        rnd = (rnd * 1103515245 + 12345) % 2147483648
+        y, i = pairs[(rnd >> 8) % len(pairs)]
+        s2 = seq
+        ry, ri = ops[y]["role"], ops[i]["role"]
+        for dt in (range(-RO, RO) if rnd >> 6 & 3 else [0]):
+            ky, ki = (ry[0] + dt,) + ry[1:], (ri[0] + dt,) + ri[1:]
+            if ky in same and ki in same:
+                s2 = move(s2, same[ky], same[ki], rnd >> 5 & 1)
+        if s2 is seq:
+            continue
+        nx = times(s2)
+        if nx[0] < cur[0] + CFG["step"] * (1 - turn / CFG["more"]) * (rnd % 32) / 32:
+            seq, cur = s2, nx
+            if cur[0] < top[0]:
+                top = (cur[0], cur[1])
+    best = top
     span = best[0]
     order = sorted(range(n), key=lambda i: (best[1][i], i))
     bank = {}
@@ -592,7 +706,7 @@ def schedule(ops):
             p = ops[j]
             if p["k"] in ("dma", "send"):
                 best[("x", j)] = j
-            elif not (p["e"] == "p" and o["e"] == "p"):
+            elif waits(i, j):
                 if ("q", p["e"]) not in best or pos[j] > pos[best[("q", p["e"])]]:
                     best[("q", p["e"])] = j
         o["wt"] = []

@@ -2,10 +2,10 @@ from concourse.bass import DstId, RemoteDMATransfer
 from concourse.mybir import AluOpType as AL, ActivationFunctionType as AF
 
 RO = 6
-PARTS = ("front", "probe", "match", "mask", "rank", "write")
-CFG = {"abs": (), "vg": (), "vq": (), "au": (0, 1), "ve": (), "ap": (0, 1), "av": (0, 1), "ar": (0, 1), "t": "a", "ut": "a",
-       "raw": 0, "sx": 0, "sd": (), "d0": 0, "y7": 0, "md": 8, "eng": 16, "send": 2.0, "xl": 10.0, "lat": 0.1, "turns": 5, "more": 0, "step": 0.1, "slack": 0.0, "pen": 2.0,
-       "lead": (0, 1, 1.5, 2, 2.5, 3, 3.5, 4, 5), "vl": (1,), "pc": (512, 512, 512, 512)}
+CFG = {"av": (0, 1), "au": (), "vl": (1,), "fin": (256, 384, 384), "send": 2.0, "xl": 7.5, "more": 5000, "give": 0.02,
+       "lat": 0.1, "turns": 5,
+       "slack": 0.1, "pen": 10.0, "lead": (0, 1, 1.5, 2, 2.5, 3, 3.5, 4, 5),
+       "wake": ((0.19, 0.0, 0.0), (0.17, 0.17, 0.0), (0.1, 0.1, 0.025)), "pc": (512, 512, 512, 512)}
 DT = {"f": "float32", "i": "int32", "b": "bfloat16", "u": "uint16", "h": "float16"}
 SCRATCH = {}
 LN2 = 0.6931471805599453
@@ -46,7 +46,7 @@ def build():
         return len(range(r[1], r[2], r[3]))
 
     def two(r):
-        return r[0] in ("pb", "ph", "pu", "m0s", "X0", "X1", "WS", "WX", "WM", "zM", "NP", "zin", "yzb", "ymb")
+        return r[0] in ("pb", "ph", "pu", "m0s", "X0", "X1", "WS0", "WS1", "Ub", "WX", "WM", "zM", "NP", "zin", "yzb", "ymb")
 
     def add(e, k, a, rd, wr, cost):
         R = []
@@ -103,6 +103,9 @@ def build():
         add("a", "ac", (out, a, fn, bias, scale, acc), [a, bias, scale], [out] + ([acc] if acc else []),
             0.065 + max(64, n * (1.56 if a[0] == "@" else 1.0)) * CY)
 
+    def AS(out, a, scale, bias=0.0):
+        AC(out, a, AF.Identity, bias, scale)
+
     def MM(lst):
         c = 0.03
         for o, l, r, s0, s1 in lst:
@@ -116,11 +119,18 @@ def build():
     def IO(out, pat, base, cm):
         add("g", "io", (out, pat, base, cm), [], [out], 0.13 + cnt(out) * 2 * CY)
 
+    def GS(out, v, diag=False):
+        if out[4] - out[5] < 128:
+            return MS(out, v)
+        zero = sl(Z[out[0]], 0, cnt(out))
+        add("g", "as", (out, zero, v, diag), [zero], [out], 0.17 + cnt(out) * 2 * CY)
+
     def DMA(q, out, a, cost):
         add(q, "dma", (out, a), [a], [out], cost)
 
     X = [own("X%d" % h, "b", 8256) for h in range(2)]
-    WS = own("WS", "b", 4096)
+    WS = [own("WS%d" % h, "b", 4096) for h in range(2)]
+    Ub = own("Ub", "b", 256)
     WX = own("WX", "b", 4224)
     WM = own("WM", "b", 4224)
     zM = own("zM", "h", 4096)
@@ -139,29 +149,36 @@ def build():
             DMA("a", half(sl(wts, 8 * h, 8 * h + 2), f), half(hbm("wt", 0, 2), h), 2.0)
             DMA("s", half(sl(X[h], 0, 8192), f), half(hbm("xr", 0, 8192), h), CFG["xl"] * (2 - h))
 
+    Z = {"pb": new("b", 192), "pf": new("f", 128)}
+    IO(Z["pb"], [[0, 192]], 0, 0); IO(Z["pf"], [[0, 128]], 0, 0)
+    Z["WM"] = Z["pb"]
     dif = new("i", 128); IO(dif, [[-1, 128]], 128, 1)
     dif2 = new("i", 152); IO(dif2, [[-1, 152]], 24, 1)
+    kt0 = new("f", 128); IO(kt0, [[-2, 16], [0, 8]], 30, 0)
     ip = new("i", 1); IO(ip, [[0, 1]], 0, 1)
     ip16 = new("i", 1); IO(ip16, [[0, 1]], 0, 16)
     ib = new("f", 128); IO(ib, [[16, 8], [0, 16]], 0, 0)
     im = new("i", 128); IO(im, [[1, 32], [0, 4]], 0, 0)
     k8 = new("f", 8); IO(k8, [[0, 2], [16, 4]], 0, 0)
+    k9 = new("f", 128); IO(k9, [[0, 32], [16, 4]], 0, 0)
+    KF = new("b", 128); IO(KF, [[0, 16], [16, 2], [0, 4]], 0, 0)
     d5 = new("f", 5); IO(d5, [[-3, 5]], 0, 0)
+    i8 = new("f", 128); IO(i8, [[0, 16], [1, 8]], 0, 0)
     i16 = new("f", 64); IO(i16, [[0, 4], [1, 16]], 0, 0)
     j65 = new("f", 260); IO(j65, [[-16, 4], [1, 65]], 0, 0)
     n65 = new("f", 260); IO(n65, [[0, 4], [-1, 65]], -8192, 0)
-    I = new("b", 128); TS(I, dif, 128.0, None, AL.is_equal)
-    If32 = new("f", 128); TS(If32, dif, 128.0, 2.0 ** 19, AL.is_equal, AL.mult)
+    IO(sl(j65, 48, 65), [[1, 17]], 0, 0); IO(sl(n65, 48, 65), [[-1, 17]], -8192, 0)
+    I = new("b", 128); GS(I, 1.0, True)
+    If32 = new("f", 128); GS(If32, 2.0 ** 19, True)
     t0 = new("i", 128); TS(t0, dif, 63, None, AL.bitwise_and)
     P2 = new("b", 128); TS(P2, t0, 0.0, None, AL.is_equal)
-    PH = [new("b", 128), new("b", 128)]; PF = [new("f", 128), new("f", 128)]
+    PF = [new("f", 128), new("f", 128)]
     for f in range(2):
-        MS(half(PH[f], 1 - f), 0.0); CP(half(PH[f], f), half(P2, f))
-        AC(PF[f], PH[f], AF.Copy, 0.0, -16384.0)
+        GS(half(PF[f], 1 - f), 0.0); AS(half(PF[f], f), half(P2, f), -16384.0)
     t1 = new("i", 1); pg = new("f", 1); TS(t1, ip, 112, None, AL.bitwise_and); CP(pg, t1)
     t2 = new("i", 1); pp = new("f", 1); TS(t2, ip, 15, None, AL.bitwise_and); CP(pp, t2)
     t3 = new("i", 1); s64 = new("f", 1); TS(t3, ip16, 1984, None, AL.bitwise_and); CP(s64, t3)
-    sc = new("f", 1); TS(sc, s64, 1.0 / 64, None, AL.mult)
+    sc = new("f", 1); AS(sc, s64, 1.0 / 64)
     BD = new("b", 128); TS(BD, ib, pg, None, AL.is_equal)
     G8 = sl(BD, 0, 128, 16)
     WhZ = [new("h", 16), new("h", 16)]; WhM = [new("b", 24), new("b", 24)]
@@ -171,52 +188,57 @@ def build():
             wc = sl(wts, 8 * h + e, 8 * h + e + 1)
             TS(sl(WhZ[h], 8 * e, 8 * e + 8), G8, wc, -2.0 ** -12, AL.mult, AL.mult)
             TS(sl(WhM[h], 8 * e, 8 * e + 8), G8, wc, -0.25, AL.mult, AL.mult)
-            TS(Wr[h][e], BD, wc, 32.0 - 64 * e, AL.mult, AL.mult)
-        CP(sl(WhM[h], 16, 24), G8)
+            wf = new("f", 1); AS(wf, wc, 32.0 - 64 * e); AS(Wr[h][e], BD, wf)
+        AS(sl(WhM[h], 16, 24), G8, 1.0)
     OFF = new("b", 128)
     for e in range(2):
         sg = 2.0 * e - 1.0
-        MS(pt(sl(OFF, 64 * e, 64 * e + 64), 0, 32), 64 * sg)
-        MS(pt(sl(OFF, 64 * e, 64 * e + 64), 32, 64), -sg / 64)
-    MS(pt(OFF, 64, 128), 0.0)
+        GS(pt(sl(OFF, 64 * e, 64 * e + 64), 0, 32), 64 * sg)
+        GS(pt(sl(OFF, 64 * e, 64 * e + 64), 32, 64), -sg / 64)
+    GS(pt(OFF, 64, 128), 0.0)
     om = new("u", 128); CP(om, im)
-    TS(sl(WM, 2112, 4160), ("@", sl(m0s, 32, 64), om), -1.0, None, AL.mult)
+    TS(sl(WM, 2112, 3136), ("@", sl(m0s, 32, 64), sl(om, 0, 64)), -1.0, None, AL.mult)
+    AC(sl(WM, 3136, 4160), ("@", sl(m0s, 32, 64), sl(om, 64, 128)), AF.Copy, 0.0, -1.0)
     AC(sl(WM, 0, 2048), ("@", sl(m0s, 0, 32), om), AF.Copy, 0.0, -1.0)
-    MS(sl(WM, 2048, 2112), 0.0); MS(sl(WM, 4160, 4224), 0.0)
+    GS(sl(WM, 2048, 2112), 0.0); GS(sl(WM, 4160, 4224), 0.0)
     t4 = new("i", 128); TS(t4, dif, 3, None, AL.bitwise_and)
     B4 = new("b", 128); TS(B4, t4, 0.0, None, AL.is_equal)
     SEL = sl(B4, 0, 4)
+    t5 = new("i", 1); t6 = new("f", 1); TS(t5, ip, 3, None, AL.bitwise_and); CP(t6, t5)
+    t7 = new("f", 128); TS(t7, i8, t6, None, AL.subtract)
 
-    def scaled(src, v):
-        o = new("b", cnt(src))
-        AC(o, src, AF.Copy, 0.0, v)
+    def diag(v):
+        o = new("b", 128)
+        GS(o, v, True)
         return o
-    I9 = scaled(I, 9.0); Ig = scaled(I, -2.0 ** 18); Iw = scaled(I, 1.5 * 2.0 ** -63)
-    I7 = scaled(I, -0.875); Ih = scaled(I, 0.5); Inh = scaled(I, -0.5); Iq = scaled(I, 0.25); B4q = scaled(B4, 0.25)
-    Ia = scaled(I, -32.5); Ib = scaled(I, 32.0); In = scaled(I, -8192.0); Ine = scaled(I, -1.0); Im = scaled(I, -256.0)
+    I9 = diag(9.0); Ig = diag(-2.0 ** 18); Iw = diag(1.5 * 2.0 ** -63); I7 = diag(-0.875); Ih = diag(0.5)
+    Inh = diag(-0.5); Iq = diag(0.25); Ia = diag(-32.5); Ib = diag(32.0); In = diag(-8192.0); Ine = diag(-1.0)
+    Im = diag(-256.0)
+    B4q = new("b", 128); AS(B4q, B4, 0.25)
     I9h = new("h", 128); TS(I9h, I, 9.0, None, AL.mult)
-    ones = new("b", 192); MS(ones, 1.0)
+    ones = new("b", 192); GS(ones, 1.0)
     o128 = sl(ones, 0, 128)
-    o32 = new("b", 128); MS(o32, 32.0)
-    oh = new("b", 40); MS(oh, -1.0 / 256)
-    halff = new("f", 128); MS(halff, 0.5)
-    KOf = new("f", 8); TS(KOf, k8, pp, None, AL.add)
-    KO = new("b", 8); CP(KO, KOf)
+    o32 = new("b", 128); GS(o32, 32.0)
+    oh = new("b", 40); GS(oh, -1.0 / 256)
+    halff = new("f", 128); GS(halff, 0.5)
+    KOf = new("f", 8); AS(KOf, k8, 1.0, pp)
+    KO = new("b", 8); AS(KO, k8, 1.0, pp)
+    KC = new("b", 128); AS(KC, k9, 1.0, pp)
     SEL3 = new("b", 12)
     for e in range(3):
-        TS(sl(SEL3, 4 * e, 4 * e + 4), SEL, 2.0 ** (9 * e - 18), None, AL.mult)
+        AS(sl(SEL3, 4 * e, 4 * e + 4), SEL, 2.0 ** (9 * e - 18))
     c0 = new("f", 64); c1 = new("f", 64); ctl1 = new("f", 64); pq = new("f", 1)
-    TS(pq, pp, 1.0, None, AL.add)
+    AS(pq, pp, 1.0, 1.0)
     TS(c0, i16, pp, None, AL.not_equal); TS(c1, i16, pq, 511.0, AL.is_equal, AL.mult); TT(ctl1, c0, c1, AL.add)
     kn = new("f", 1); kr = new("f", 1); k0 = new("f", 1); k1 = new("f", 1); k2 = new("f", 1)
     TS(k0, pp, 15.0, 511.0, AL.not_equal, AL.mult)
-    TS(kn, k0, -1.0, -1.0, AL.mult, AL.add)
-    kp = new("f", 1); TS(kp, k0, 1.0, None, AL.add)
+    AS(kn, k0, -1.0, -1.0)
     TS(k1, pp, 15.0, 2.0 ** -29, AL.is_equal, AL.mult); TS(k2, pp, 15.0, 2.0 ** -38, AL.not_equal, AL.mult)
     TT(kr, k1, k2, AL.add)
     c2 = new("f", 260); ctl2 = new("f", 260)
     TS(c2, j65, pp, 2.0 ** -14, AL.is_equal, AL.mult); TT(ctl2, c2, n65, AL.mult); MS(sl(ctl2, 0, 260, 65), 2.0 ** 40)
-    Dm = new("f", 5); TS(Dm, d5, pp, None, AL.add)
+    MS(sl(ctl2, 48, 49), 2.0 ** 40)
+    Dm = new("f", 5); AS(Dm, d5, 1.0, pp)
     ee = [new("f", 5) for e in range(3)]
     for e in range(3):
         TS(ee[e], Dm, float(e), -2.0 ** (18 - 9 * e), AL.is_equal, AL.mult)
@@ -225,29 +247,32 @@ def build():
     TT(f0, ee[0], ee[1], AL.add); TT(f1, ee[2], e3, AL.add); TT(tw, f0, f1, AL.add)
     CN = new("b", 40)
     for a in range(5):
-        TS(sl(CN, 8 * a, 8 * a + 8), G8, sl(tw, a, a + 1), None, AL.mult)
+        AS(sl(CN, 8 * a, 8 * a + 8), G8, sl(tw, a, a + 1))
     REP = new("b", 384)
     for e in range(3):
         RT = new("b", 40)
         for a in range(5):
-            AC(sl(RT, 8 * a, 8 * a + 8), G8, AF.Copy, 0.0, sl(ee[e], a, a + 1))
+            AS(sl(RT, 8 * a, 8 * a + 8), G8, sl(ee[e], a, a + 1))
         MM(ACC(pt(sl(B[7], 128 * e, 128 * e + 128), 0, 40), [(RT, I)]))
-        AC(pt(sl(REP, 128 * e, 128 * e + 128), 0, 40), pt(sl(B[7], 128 * e, 128 * e + 128), 0, 40), AF.Copy, 0.0,
-           -2.0 ** (9 * e - 10))
+        AS(pt(sl(REP, 128 * e, 128 * e + 128), 0, 40), pt(sl(B[7], 128 * e, 128 * e + 128), 0, 40), -2.0 ** (9 * e - 10))
     OG = new("b", 4); OP = new("b", 4); OT = new("b", 4); OU = new("b", 4); ON = new("b", 4)
-    s6m = new("f", 1); TS(s6m, s64, -2048.0, None, AL.add)
-    TS(OG, SEL, s6m, 0.5, AL.mult, AL.mult); TS(OU, SEL, s6m, -0.5, AL.mult, AL.mult)
-    TS(OP, SEL, s64, 0.5, AL.mult, AL.mult); TS(OT, SEL, s64, -0.5, AL.mult, AL.mult)
-    MS(ON, 16.0)
+    s6m = new("f", 1); s32 = new("f", 1); AS(s6m, s64, 0.5, -1024.0); AS(s32, s64, 0.5)
+    AS(OG, SEL, s6m); AS(OU, OG, -1.0); AS(OP, SEL, s32); AS(OT, OP, -1.0)
+    GS(ON, 16.0)
     PZ = new("b", 152); TS(PZ, dif2, 0.0, s64, AL.is_equal, AL.mult)
     RK = new("b", 24)
-    for k in range(1, RO):
+    for k in range(RO - 1):
         gk = new("f", 1)
         TS(gk, s64, 64.0 * k, s64, AL.is_gt, AL.mult)
-        TS(sl(RK, 4 * k, 4 * k + 4), SEL, gk, None, AL.mult)
+        AS(sl(RK, 4 * k, 4 * k + 4), SEL, gk)
+    BF = [new("b", 128), new("b", 128)]
+    for f in range(2):
+        TS(BF[f], t7, 4.0 * f, None, AL.is_equal)
+    t8 = new("i", 1); TS(t8, ip, 64, None, AL.bitwise_and)
+    k64 = new("f", 1); TS(k64, t8, -0.5, 0.5, AL.mult, AL.add)
+    KT = new("f", 128); AS(KT, kt0, 1.0, k64)
     thr = [new("f", 1) for t in range(RO)]
-    MS(thr[0], -1.0 if CFG["sx"] else 2.0)
-    I40 = scaled(I, 40.0)
+    GS(thr[0], 2.0)
     H = []
     for h in range(2):
         d = {}
@@ -259,38 +284,33 @@ def build():
                            ("U", "b", 64), ("zU", "b", 64), ("ur", "b", 128), ("uuv", "f", 128), ("ux", "f", 64),
                            ("ufl", "f", 64), ("ut", "f", 64), ("uy", "f", 64), ("ur2", "f", 64), ("npl", "f", 64),
                            ("no", "f", 64), ("dd", "f", 260), ("mn", "f", 260), ("ow", "u", 8), ("Hc", "f", 1),
-                           ("E", "b", 13 * 128), ("ab0", "b", 512), ("ab1", "b", 512)):
+                           ("E", "b", 11 * 128), ("LB", "b", 136), ("dl", "b", 128), ("sh", "b", 128), ("md", "b", 128),
+                           ("fo", "u", 128)):
             d[nm] = new(dt_, n)
         d["zl"] = [new("h", 512) for t in range(RO - 1)]
         d["zs"] = [new("h", 64) for t in range(RO - 1)]
         d["o"] = [new("u", 8), new("u", 8)]
         H.append(d)
-        TS(d["rk"], o128, sc, None, AL.mult)
+        AS(d["rk"], o128, sc)
         AC(d["w"], d["rk"], AF.Exp, 30 * LN2, -3 * LN2)
         CP(d["o"][1], KOf)
     par = new("f", 1)
-    fo = new("u", 256)
 
-    def hashf(n, sg, uv, x, fl, t, y, teng):
+    def hashf(n, sg, uv, x, fl, t, y):
         q = sg * sg
         SC(x, sl(uv, 0, n), sl(uv, n, 2 * n), 0.0, AL.max, AL.mult)
-        if teng == "a":
-            AC(t, sl(uv, 0, n), AF.Identity, 259915760.0 * q, 1184.0 * sg)
-        else:
-            TS(t, sl(uv, 0, n), 1184.0 * sg, 259915760.0 * q, AL.mult, AL.add)
+        AS(t, sl(uv, 0, n), 1184.0 * sg, 259915760.0 * q)
         TS(fl, x, 8388591.5 * q, (2.0 ** 28 + 2.0 ** 23) * q, AL.add, AL.add)
         SC(y, t, fl, 0.0, AL.max, AL.subtract)
 
     def front(t, h):
         d = H[h]
         z = sl(zin, 128 * t + 64 * h, 128 * t + 64 * h + 64)
-        zr = d["zr"]
         part[0] = "front%d" % h
-        if CFG["md"] and t:
+        if t:
             zr = d["zl"][t - 1]
-            if CFG["md"] == 4:
-                CP(sl(zr, 256, 512), sl(zr, 0, 256))
         else:
+            zr = d["zr"]
             TS(sl(zr, 0, 64), z, -1024.0, None, AL.add)
             TS(sl(zr, 64, 128), z, -1024.0, None, AL.add)
             CP(sl(zr, 128, 256), sl(zr, 0, 128))
@@ -303,13 +323,10 @@ def build():
         TS(d["r"], sl(B[0], 0, 256), -0.5 + 2.0 ** -13, None, AL.add)
         TT(sl(d["uv"], 0, 128), sl(B[0], 0, 128), sl(d["r"], 0, 128), AL.subtract)
         TT(sl(d["uv"], 128, 256), sl(d["r"], 128, 256), sl(B[0], 128, 256), AL.subtract)
-        hashf(128, 2.0 ** -12, d["uv"], d["x"], d["fl"], d["t"], d["y"], CFG["t"])
+        hashf(128, 2.0 ** -12, d["uv"], d["x"], d["fl"], d["t"], d["y"])
         AC(d["cm"], sl(B[0], 256, 384), AF.Copy)
         ops[-1]["r"].append(d["t"])
-        if h in CFG["ar"]:
-            AC(d["r2"], d["y"], AF.Identity, 240.0, 64.0)
-        else:
-            TS(d["r2"], d["y"], 64.0, 240.0, AL.mult, AL.add)
+        AS(d["r2"], d["y"], 64.0, 240.0)
         MM([(sl(B[0], 384, 512), d["y"], If32, True, False)])
         MM([(sl(B[0], 384, 512), d["r2"], In, False, True)])
         TS(d["off"], sl(B[0], 384, 512), 240 * 8192 + 4095.5, None, AL.add)
@@ -321,21 +338,15 @@ def build():
         part[0] = "probe%d" % h
         for q, n in enumerate(CFG["pc"]):
             xh = sl(WX, 2112 * h + a, 2112 * h + a + n)
-            np_ = sl(NP, 2048 * h + a, 2048 * h + a + n)
             src = ("@", sl(X[h], 0, 8192), sl(d["off"], a // 16, (a + n) // 16))
-            if (h, q) in CFG["vg"] or (t == RO - 1 and h == 0 and q in CFG["vl"]):
+            if t == RO - 1 and h == 0 and q in CFG["vl"]:
                 CP(xh, src)
             else:
                 AC(xh, src, AF.Copy)
             bk = sl(B[1 + q % 2], 0, n)
             MM([(bk, I9h, sl(zM, 2048 * h + a, 2048 * h + a + n), True, False)])
             MM([(bk, I9, xh, False, True)])
-            if (h, q) in CFG["abs"]:
-                ab = sl(d["ab%d" % (q % 2)], 0, n)
-                AC(ab, bk, AF.Abs, -9216.0)
-                TS(np_, ab, 508.0, None, AL.is_lt)
-            else:
-                TS(np_, bk, 1.5 * 2.0 ** 33 - 9216, 1.5 * 2.0 ** 33, AL.add, AL.is_equal)
+            TS(sl(NP, 2048 * h + a, 2048 * h + a + n), bk, 1.5 * 2.0 ** 33 - 9216, 1.5 * 2.0 ** 33, AL.add, AL.is_equal)
             a += n
         AC(d["x0"], ("@", sl(WX, 2112 * h, 2112 * h + 2048), sl(d["o"][(t + 1) % 2], 4, 8)), AF.Copy)
         av = sl(B[4 + 2 * h], 0, 64)
@@ -360,13 +371,8 @@ def build():
                 for k in range(8)])
         MM([(cn, I, d["cm"], True, False)]
            + [(sl(S7, 384 + b, 512, 16), sl(NP, 2048 * h + b, 2048 * h + 2048, 16), G8, False, b == 15) for b in range(16)])
-        if CFG["sx"]:
-            AC(d["cm"], cn, AF.Relu, thr[t], -1.0)
-            MM(ACC(cn, [(I, d["rk"]), (I40, d["cm"])]))
-            AC(d["mw"], cn, AF.Exp, 30 * LN2, -3 * LN2)
-        else:
-            AC(cn, cn, AF.Relu, thr[t])
-            TT(d["mw"], cn, w, AL.mult)
+        AC(cn, cn, AF.Relu, thr[t])
+        TT(d["mw"], cn, w, AL.mult)
         for x in range(2):
             MM([(sl(F[x], 64 + k, 384, 8), sl(NP, 2048 * h + 2 * k + x, 2048 * h + 2048, 16), CN, False, False)
                 for k in range(8)])
@@ -374,23 +380,38 @@ def build():
         AC(sl(d["sig"], 0, 256), sl(S7, 0, 256), AF.Sign, 0.0, 1.0, None if last else d["Hc"])
         MM(ACC(sl(S7, 384, 388), [(I, sl(KO, 0, 4)), (o128, ON), (gt, OU), (ge, OG)]))
         CP(sl(o, 0, 4), sl(S7, 384, 388))
-        MM(ACC(sl(S7, 256, 384), [(I7, w), (Iw, o128), (B4, d["mw"])]))
-        AC(gp, sl(S7, 256, 384), AF.Sign)
-        nzr = sl(yzb, 128 * t + 64 * h, 128 * t + 64 * h + 64)
-        if h in CFG["sd"]:
-            AC(d["D"], ("@", sl(WX, 2112 * h, 2112 * h + 2112), sl(o, 0, 4)), AF.Copy)
-            MM(ACC(sl(S7, 400, 464), [(Ine, z), (I, d["D"])]))
-            AC(nzr, sl(S7, 400, 464), AF.Abs)
+        if last:
+            sg = sl(S7, 0, 128)
+            MM([(half(sg, k), sl(gt, 64 * f, 64 * f + 64), BF[f], f == 0, f == 1) for k in range(2) for f in range(2)])
+            TT(d["sh"], sg, KT, AL.is_lt)
+            TT(d["md"], d["sh"], d["dl"], AL.mult)
+            MM(ACC(sl(S7, 128, 256), [(I, sl(d["LB"], 8, 136)), (I, KC), (o128, KF), (I, d["md"])]))
+            CP(d["fo"], sl(S7, 128, 256))
+            a = 0
+            for n in CFG["fin"]:
+                for q in range(2):
+                    src = ("@", WS[h], sl(d["fo"], (a + n * q) // 16, (a + n * q + n) // 16))
+                    dst = sl(ymb, 2048 * h + a + n * q, 2048 * h + a + n * q + n)
+                    if q:
+                        AC(dst, src, AF.Copy, 0.0, -1.0)
+                    else:
+                        TS(dst, src, -1.0, None, AL.mult)
+                for k in range(2):
+                    b = max(a, 128 - 128 * k)
+                    DMA("s", half(hbm("ym", 2048 * k + b, 2048 * k + a + 2 * n), h),
+                        half(sl(ymb, 2048 * h + b, 2048 * h + a + 2 * n), k), 1.7 + n / 640)
+                a += 2 * n
         else:
-            TT(d["D"], ("@", sl(WX, 2112 * h, 2112 * h + 2112), sl(o, 0, 4)), z, AL.subtract)
-            AC(nzr, d["D"], AF.Abs)
+            MM(ACC(sl(S7, 256, 384), [(I7, w), (Iw, o128), (B4, d["mw"])]))
+            AC(gp, sl(S7, 256, 384), AF.Sign)
+        nzr = sl(yzb, 128 * t + 64 * h, 128 * t + 64 * h + 64)
+        TT(d["D"], ("@", sl(WX, 2112 * h, 2112 * h + 2112), sl(o, 0, 4)), z, AL.subtract)
+        AC(nzr, d["D"], AF.Abs)
         if not last:
             zn = sl(zin, 128 * t + 128 + 64 * h, 128 * t + 192 + 64 * h)
-            to = [sl(d["zl"][t], 64 * k, 64 * k + 64) for k in range(CFG["md"])]
-            if to:
-                TS(d["zs"][t], nzr, -1024.0, None, AL.add)
-            add("g", "send", (zn, nzr, "ar%d_%d" % (t, h), d["zs"][t], to), [nzr] + ([d["zs"][t]] if to else []), [zn] + to,
-                CFG["send"] + 0.1 * CFG["md"])
+            to = [sl(d["zl"][t], 64 * k, 64 * k + 64) for k in range(8)]
+            TS(d["zs"][t], nzr, -1024.0, None, AL.add)
+            add("g", "send", (zn, nzr, "ar%d_%d" % (t, h), d["zs"][t], to), [nzr, d["zs"][t]], [zn] + to, CFG["send"] + 0.8)
         for f in range(2):
             DMA("s", half(hbm("yz", 128 * t + 64 * f, 128 * t + 64 * f + 64), h), half(nzr, f), 2.0)
         part[0] = "mask%d" % h
@@ -400,18 +421,11 @@ def build():
         AC(d["mj"], ("@", sl(WM, 2112 * h, 2112 * h + 2112), sl(o, 0, 4)), AF.Copy)
         for x in range(2):
             MM([(sl(F[x], 64 * a + 64, 64 * a + 128), Ig, sl(gt, x, 128, 2), False, a == 4) for a in range(5)])
-            if (h, x) in CFG["vq"]:
-                TS(sl(d["Q"], x, 640, 2), sl(F[x], 64, 384), -2.0 ** 18, 0.0, AL.add, AL.max)
-            else:
-                AC(sl(d["Q"], x, 640, 2), sl(F[x], 64, 384), AF.Relu, -2.0 ** 18)
-        yb = S7 if CFG["y7"] and not last else F[0]
-        y = pt(sl(yb, 0, 192), 0, 40)
+            AC(sl(d["Q"], x, 640, 2), sl(F[x], 64, 384), AF.Relu, -2.0 ** 18)
+        y = pt(sl(F[0], 0, 192), 0, 40)
         MM([(y, oh, ones, True, False)])
-        MM([(pt(sl(yb, b, 192, 16), 0, 40), sl(d["Q"], b, 640, 16), SEL3, False, b == 15) for b in range(16)])
-        a = 64 if CFG["d0"] else 0
-        if a:
-            AC(pt(sl(d["nz"], 0, 64), 0, 40), pt(sl(yb, 0, 64), 0, 40), AF.Relu, 0.0, 2.0)
-        hh, nz, y = pt(sl(d["hh"], a, 192), 0, 40), pt(sl(d["nz"], a, 192), 0, 40), sl(y, a, 192)
+        MM([(pt(sl(F[0], b, 192, 16), 0, 40), sl(d["Q"], b, 640, 16), SEL3, False, b == 15) for b in range(16)])
+        hh, nz = pt(d["hh"], 0, 40), pt(d["nz"], 0, 40)
         TS(hh, y, 1.5 * 2.0 ** 32, -1.5 * 2.0 ** 32, AL.add, AL.add)
         TT(nz, y, hh, AL.is_ge)
         Y = sl(F[1], 0, 64)
@@ -423,56 +437,64 @@ def build():
             AC(d["U"], Y, AF.Sign, 0.0, -1.0)
         else:
             TS(d["U"], Y, -1.0, -1.0, AL.mult, AL.max)
-        if not last:
-            CP(("@", sl(WM, 2112 * h, 2112 * h + 2048), sl(o, 4, 8)), d["U"])
+        if last:
+            part[0] = "rank%d" % h
+            MM([(half(sl(F[0], 256 + 64 * f, 320 + 64 * f), 0), sl(Ine, 64 * f, 64 * f + 64), d["U"], True, True)
+                for f in range(2)])
+            AC(half(sl(Ub, 128 * h, 128 * h + 128), 0), half(sl(F[0], 256, 384), 0), AF.Copy)
+            DMA("s", half(hbm("ym", 0, 128), h), half(sl(Ub, 128 * h, 128 * h + 128), 0), 2.0)
+            return
+        CP(("@", sl(WM, 2112 * h, 2112 * h + 2048), sl(o, 4, 8)), d["U"])
         if t == RO - 2:
             for f in range(2):
-                DMA("s", half(sl(WS, 2048 * f, 2048 * f + 2048), h), half(sl(WM, 2112 * h, 2112 * h + 2048), f), 3.0)
+                for k in range(2):
+                    DMA("s", half(sl(WS[h], 2048 * f, 2048 * f + 2048), k), half(sl(WM, 2112 * h, 2112 * h + 2048), f), 3.0)
         part[0] = "rank%d" % h
-        rb = sl(S7, 0, 128) if last else sl(F[1], 384, 512)
-        MM(ACC(rb, [(I, d["rk"]), (Ia, gp), (Ib, gt)]))
-        AC(d["rk"], rb, AF.Relu, 0.5)
-        if not last:
-            AC(w, d["rk"], AF.Exp, 30 * LN2, -3 * LN2)
-            part[0] = "write%d" % h
-            MM([(sl(F[1], 128 + 64 * f, 192 + 64 * f), PH[f], z, True, True) for f in range(2)])
-            AC(d["zw"], sl(F[1], 128, 256), AF.Copy)
-            MM([(sl(F[0], 384, 512), o32, OFF, True, False)])
-            MM([(sl(F[0], 256 + 64 * k, 320 + 64 * k), Wr[h][k % 2], d["zU"], False, k == 3) for k in range(4)])
-            TS(d["ur"], sl(F[0], 384, 512), 1.5 * 2.0 ** 40, -1.5 * 2.0 ** 40, AL.add, AL.add)
-            TT(d["uuv"], sl(F[0], 256, 384), d["ur"], AL.subtract)
-            hashf(64, 32.0, d["uuv"], d["ux"], d["ufl"], d["ut"], d["uy"], CFG["ut"])
-            TS(d["ur2"], d["uy"], 1.5 * 2.0 ** 51, -(1.5 * 2.0 ** 51 + 2.0 ** 29), AL.add, AL.add)
-            SC(d["npl"], d["ur2"], d["uy"], 0.0, AL.min, AL.subtract)
-            SC(d["no"], ctl1, d["npl"], 0.0, AL.mult, AL.min)
+        MM(ACC(sl(F[1], 384, 512), [(I, d["rk"]), (Ia, gp), (Ib, gt)]))
+        AC(d["rk"], sl(F[1], 384, 512), AF.Relu, 0.5)
+        AC(w, d["rk"], AF.Exp, 30 * LN2, -3 * LN2)
+        part[0] = "write%d" % h
+        for f in range(2):
+            for k in range(2):
+                DMA("s", half(sl(d["zw"], 64 * f, 64 * f + 64), k), half(z, f), 2.0)
+        MM([(sl(F[0], 384, 512), o32, OFF, True, False)])
+        MM([(sl(F[0], 256 + 64 * k, 320 + 64 * k), Wr[h][k % 2], d["zU"], False, k == 3) for k in range(4)])
+        TS(d["ur"], sl(F[0], 384, 512), 1.5 * 2.0 ** 40, -1.5 * 2.0 ** 40, AL.add, AL.add)
+        TT(d["uuv"], sl(F[0], 256, 384), d["ur"], AL.subtract)
+        hashf(64, 32.0, d["uuv"], d["ux"], d["ufl"], d["ut"], d["uy"])
+        TS(d["ur2"], d["uy"], 1.5 * 2.0 ** 51, -(1.5 * 2.0 ** 51 + 2.0 ** 29), AL.add, AL.add)
+        SC(d["npl"], d["ur2"], d["uy"], 0.0, AL.min, AL.subtract)
+        SC(d["no"], ctl1, d["npl"], 0.0, AL.mult, AL.min)
+        for c in range(4):
+            a = 0 if c else 48
+            AC(sl(d["dd"], 65 * c + a, 65 * c + 64), sl(d["npl"], 0, 64 - a), AF.Abs, sl(d["no"], 16 * c + 15, 16 * c + 16), kn)
+        TS(sl(d["dd"], 64, 260, 65), sl(d["no"], 15, 64, 16), kr, 12288.5 / 16384, AL.mult, AL.add)
+        SC(sl(d["mn"], 48, 260), sl(ctl2, 48, 260), sl(d["dd"], 48, 260), 0.0, AL.add, AL.min)
+        MM([(sl(F[0], 4 * f, 4 * f + 4), PF[f], sl(d["mn"], 64, 260, 65), True, True) for f in range(2)])
+        CP(d["ow"], sl(F[0], 0, 8))
+        for f in (1, 0):
+            CP(("@", X[h], sl(d["ow"], 4 * f, 4 * f + 4)), sl(d["zw"], 64 * f, 64 * f + 64))
+
+    def lists(h):
+        d = H[h]
+        part[0] = "list%d" % h
+        E = [sl(d["E"], 128 * k, 128 * k + 128) for k in range(11)]
+        for k in range(6):
+            TS(E[k], d["rk"], sc, float(k), AL.subtract, AL.is_equal)
+        for k in range(5):
+            TS(E[6 + k], d["rk"], float(k), None, AL.is_equal)
+        L = [sl(B[4 + 2 * h], 128 + 80 * f, 196 + 80 * f) for f in range(2)]
+        for u in (1, 0):
+            for k in range(6):
+                MM([(half(L[f], u), sl(E[k], 64 * f, 64 * f + 64), sl(PZ, 20 - 4 * k + 64 * u, 88 - 4 * k + 64 * u),
+                     k + f == 0, k + f + u == 7) for f in range(2)])
+        for k in range(5):
+            MM([(half(sl(L[f], 4 * k + 4, 4 * k + 8), 0), sl(E[6 + k], 64 * f, 64 * f + 64), sl(RK, 4 * k, 4 * k + 4),
+                 False, k + f == 5) for f in range(2)])
+        for f in range(2):
             for c in range(4):
-                if (h, c) in CFG["ve"]:
-                    TS(sl(d["dd"], 65 * c, 65 * c + 64), d["npl"], kp, sl(d["no"], 16 * c + 15, 16 * c + 16), AL.mult, AL.not_equal)
-                else:
-                    AC(sl(d["dd"], 65 * c, 65 * c + 64), d["npl"], AF.Abs, sl(d["no"], 16 * c + 15, 16 * c + 16), kn)
-            if h in CFG["ap"]:
-                AC(sl(d["dd"], 64, 260, 65), sl(d["no"], 15, 64, 16), AF.Identity, 12288.5 / 16384, kr)
-            else:
-                TS(sl(d["dd"], 64, 260, 65), sl(d["no"], 15, 64, 16), kr, 12288.5 / 16384, AL.mult, AL.add)
-            SC(d["mn"], ctl2, d["dd"], 0.0, AL.add, AL.min)
-            MM([(sl(F[0], 4 * f, 4 * f + 4), PF[f], sl(d["mn"], 64, 260, 65), True, True) for f in range(2)])
-            CP(d["ow"], sl(F[0], 0, 8))
-            for f in (1, 0):
-                CP(("@", X[h], sl(d["ow"], 4 * f, 4 * f + 4)), sl(d["zw"], 64 * f, 64 * f + 64))
-        else:
-            E = [sl(d["E"], 128 * k, 128 * k + 128) for k in range(13)]
-            for k in range(7):
-                TS(E[k], d["rk"], sc, float(k), AL.subtract, AL.is_equal)
-            for k in range(1, 6):
-                TS(E[7 + k], d["rk"], float(k), None, AL.is_equal)
-            L = [half(sl(B[0], 128 * f, 128 * f + 128), h) for f in range(2)]
-            for k in range(7):
-                MM([(L[f], sl(E[k], 64 * f, 64 * f + 64), sl(PZ, 24 - 4 * k, 152 - 4 * k), k + f == 0, False) for f in range(2)])
-            for k in range(1, 6):
-                MM([(sl(L[f], 4 * k, 4 * k + 4), sl(E[7 + k], 64 * f, 64 * f + 64), sl(RK, 4 * k, 4 * k + 4), False, k + f == 6)
-                    for f in range(2)])
-            MM([(half(sl(B[5], 256 + 64 * f, 320 + 64 * f), h), sl(Ine, 64 * f, 64 * f + 64), d["U"], True, True)
-                for f in range(2)])
+                AS(sl(d["LB"], 4 * f + c, 136, 8), sl(L[f], c, 68, 4), 1.0)
+        TT(d["dl"], sl(d["LB"], 0, 128), sl(d["LB"], 8, 136), AL.subtract)
 
     for t in range(RO):
         part[1] = t
@@ -481,28 +503,13 @@ def build():
         for h in (1, 0):
             probe(t, h)
             back(t, h)
+            if t == RO - 2:
+                lists(h)
         if t < RO - 1:
             tot = sl(B[7], 0, 1)
             MM(ACC(tot, [(halff, H[1]["Hc"]), (halff, H[0]["Hc"])]))
             TS(par, tot, 1.5 * 2.0 ** 24, -1.5 * 2.0 ** 24, AL.add, AL.add)
-            if CFG["sx"]:
-                TS(thr[t + 1], par, tot, -2.0, AL.is_equal, AL.add)
-            else:
-                TS(thr[t + 1], par, tot, 2.0, AL.not_equal, AL.add)
-    part[0] = "end"
-    for f in range(2):
-        for c in range(4):
-            TS(sl(fo, 4 * f + c, 256, 8), sl(B[0], 128 * f + c, 128 * f + 128, 4), sl(KOf, c, c + 1), 2048.0 * f, AL.add, AL.add)
-    AC(sl(ymb, 0, 128), sl(B[5], 256, 384), AF.Copy)
-    for q in range(8):
-        a = 128 if q == 0 else 512 * q
-        src = ("@", WS, sl(fo, a // 16, 32 * q + 32))
-        dst = sl(ymb, a, 512 * q + 512)
-        if q % 2:
-            AC(dst, src, AF.Copy, 0.0, -1.0)
-            DMA("s", hbm("ym", 512 * q - 512, 512 * q + 512), sl(ymb, 512 * q - 512, 512 * q + 512), 2.5)
-        else:
-            TS(dst, src, -1.0, None, AL.mult)
+            TS(thr[t + 1], par, tot, 2.0, AL.not_equal, AL.add)
     for k in used:
         SCRATCH["p" + k] = ("sbuf", [128, used[k]], DT[k])
     return ops
@@ -525,7 +532,6 @@ def schedule(ops):
             for (j, q, wr) in hist.get(r[0], []):
                 if wr and meets(q, r):
                     dep.add(j)
-        o["raw"] = set(dep) if CFG["raw"] else None
         for r in o["w"]:
             lst = hist.get(r[0], [])
             for (j, q, wr) in lst:
@@ -543,23 +549,29 @@ def schedule(ops):
         dep.discard(i)
         o["d"] = dep
         o["b"] = sorted(set(r[0] for r in o["r"] + o["w"] if r[0][0] == "B"))
-    lat = CFG["lat"]
     succ = [[] for k in range(n)]
     for i, o in enumerate(ops):
         for j in o["d"]:
             succ[j].append(i)
-    busy = [0.1 if o["k"] == "dma" else 0.4 if o["k"] == "send" else o["c"] for o in ops]
-    pr = [0.0] * n
-    for i in range(n - 1, -1, -1):
-        pr[i] = ops[i]["c"] + max([pr[j] + lat for j in succ[i]] + [0.0])
+    pre = [o["d"] for o in ops]
+    eng = [o["e"] for o in ops]
+    bks = [o["b"] for o in ops]
 
     def waits(i, j):
-        a, b = ops[min(i, j)], ops[max(i, j)]
-        if a["e"] != b["e"] or a["k"] in ("dma", "send") or b["k"] in ("dma", "send"):
-            return True
-        return a["e"] != "p" and (b["raw"] is None or min(i, j) in b["raw"])
+        return ops[i]["e"] != "p" or ops[j]["e"] != "p"
 
-    def run(key, before, after):
+    def case(lat, own, call):
+        cost = [o["c"] + (call if o["e"] == "v" else 0.0) for o in ops]
+        busy = [0.1 if o["k"] == "dma" else 0.4 if o["k"] == "send" else cost[i] for i, o in enumerate(ops)]
+        gap = {}
+        for i in range(n):
+            for j in pre[i]:
+                far = eng[i] != eng[j] or ops[i]["k"] == "dma" or ops[j]["k"] == "dma"
+                gap[(i, j)] = gap[(j, i)] = lat if far else own if waits(i, j) else 0.0
+        return lat, cost, busy, gap, [[(j, cost[j] + gap[(i, j)]) for j in pre[i]] for i in range(n)]
+
+    def run(key, before, after, slack, m):
+        lat, cost, busy, gap = m[0:4]
         left = [len(before[i]) for i in range(n)]
         can = [0.0] * n
         ready = [i for i in range(n) if left[i] == 0]
@@ -577,40 +589,23 @@ def schedule(ops):
                             s = max(s, f + lat)
                 est[i] = s
             i0 = min(ready, key=lambda i: (est[i], key[i]))
-            c = [i for i in ready if ops[i]["e"] == ops[i0]["e"] and est[i] <= est[i0] + CFG["slack"]]
+            c = [i for i in ready if ops[i]["e"] == ops[i0]["e"] and est[i] <= est[i0] + slack]
             i = min(c, key=lambda k: key[k] + CFG["pen"] * (est[k] - est[i0]))
             o = ops[i]
             st[i] = est[i]
             for b in o["b"]:
-                held.setdefault(b, {})[o["e"]] = est[i] + o["c"]
+                held.setdefault(b, {})[o["e"]] = est[i] + cost[i]
             free[o["e"]] = est[i] + busy[i]
             ready.remove(i)
             for j in after[i]:
-                can[j] = max(can[j], est[i] + o["c"] + (lat if waits(i, j) else 0.0))
+                can[j] = max(can[j], est[i] + cost[i] + gap[(i, j)])
                 left[j] -= 1
                 if left[j] == 0:
                     ready.append(j)
         return st
 
-    best = None
-    pre = [o["d"] for o in ops]
-    for lead in CFG["lead"]:
-        key = [-pr[i] - (lead if ops[i]["n"][-1] == "1" else 0.0) for i in range(n)]
-        for turn in range(CFG["turns"]):
-            st = run(key, pre, succ)
-            end = max(st[i] + ops[i]["c"] for i in range(n))
-            if best is None or end < best[0]:
-                best = (end, st, key)
-            if turn + 1 < CFG["turns"]:
-                bw = run([-(st[i] + ops[i]["c"]) for i in range(n)], succ, pre)
-                key = [-(bw[i] + ops[i]["c"]) for i in range(n)]
-    seq = sorted(range(n), key=lambda i: (best[1][i], i))
-    eng = [o["e"] for o in ops]
-    cost = [o["c"] for o in ops]
-    bks = [o["b"] for o in ops]
-    prl = [[(j, cost[j] + (lat if waits(i, j) else 0.0)) for j in pre[i]] for i in range(n)]
-
-    def times(seq):
+    def times(seq, m):
+        lat, cost, busy, gap, prl = m
         st = [0.0] * n
         why = [-1] * n
         free = {}
@@ -621,13 +616,10 @@ def schedule(ops):
                 if st[j] + c > s:
                     s, y = st[j] + c, -2 - j
             for b in bks[i]:
-                hb = held.get(b)
-                if hb is None:
-                    held[b] = hb = {}
+                hb = held.setdefault(b, {})
                 for e in hb:
                     if e != eng[i] and hb[e][0] > s:
                         s, y = hb[e]
-                hb[eng[i]] = None
             st[i] = s
             why[i] = y
             free[eng[i]] = (s + busy[i], i)
@@ -636,54 +628,61 @@ def schedule(ops):
         last = max(range(n), key=lambda i: st[i] + cost[i])
         return st[last] + cost[last], st, why, last
 
-    def move(seq, y, i, up):
-        a, b = seq.index(y), seq.index(i)
-        if a > b:
-            return seq
-        mid = seq[a:b + 1]
-        mv = {i if up else y}
-        for j in (mid[::-1] if up else mid):
-            if j in mv:
-                mv.update(pre[j] if up else succ[j])
-        if (y if up else i) in mv:
-            return seq
-        ins = [j for j in mid if j in mv]
-        out = [j for j in mid if j not in mv]
-        return seq[:a] + (ins + out if up else out + ins) + seq[b + 1:]
+    def judge(key):
+        seq = sorted(range(n), key=lambda k: (key[k], k))
+        ts = [times(seq, m) for m in cases]
+        return sum(t[0] for t in ts) / len(ts), ts
 
-    same = {}
+    cases = [case(*c) for c in CFG["wake"]]
+    best = None
+    for m in cases:
+        pr = [0.0] * n
+        for i in range(n - 1, -1, -1):
+            pr[i] = m[1][i] + max([pr[j] + m[3][(i, j)] for j in succ[i]] + [0.0])
+        for lead in CFG["lead"]:
+            key = [-pr[i] - (lead if ops[i]["n"][-1] == "1" else 0.0) for i in range(n)]
+            for turn in range(CFG["turns"]):
+                st = run(key, pre, succ, CFG["slack"], m)
+                nx = judge(st)
+                if best is None or nx[0] < best[0]:
+                    best = nx
+                bw = run([-(st[i] + m[1][i]) for i in range(n)], succ, pre, CFG["slack"], m)
+                key = [-(bw[i] + m[1][i]) for i in range(n)]
+    mates = {}
     for i, o in enumerate(ops):
-        same[o["role"]] = i
-    cur = times(seq)
-    top = (cur[0], cur[1])
-    rnd = 12345
+        mates.setdefault(o["role"][1:], []).append(i)
+    cur = best
+    rnd = 2
     for turn in range(CFG["more"]):
         pairs = []
-        i = cur[3]
+        now = cur[1][turn % len(cases)]
+        i = now[3]
         while i != -1:
-            y = cur[2][i]
+            y = now[2][i]
             if y >= 0 and y not in pre[i]:
                 pairs.append((y, i))
             i = y if y >= -1 else -2 - y
-        if not pairs:
-            break
         rnd = (rnd * 1103515245 + 12345) % 2147483648
-        y, i = pairs[(rnd >> 8) % len(pairs)]
-        s2 = seq
-        ry, ri = ops[y]["role"], ops[i]["role"]
-        for dt in (range(-RO, RO) if rnd >> 6 & 3 else [0]):
-            ky, ki = (ry[0] + dt,) + ry[1:], (ri[0] + dt,) + ri[1:]
-            if ky in same and ki in same:
-                s2 = move(s2, same[ky], same[ki], rnd >> 5 & 1)
-        if s2 is seq:
-            continue
-        nx = times(s2)
-        if nx[0] < cur[0] + CFG["step"] * (1 - turn / CFG["more"]) * (rnd % 32) / 32:
-            seq, cur = s2, nx
-            if cur[0] < top[0]:
-                top = (cur[0], cur[1])
-    best = top
+        y, i = pairs[(rnd >> 12) % len(pairs)]
+        key = list(now[1])
+        far = 0.001 + (rnd >> 4 & 31) / 100
+        who, by = (i, key[y] - key[i] - far) if rnd >> 11 & 1 else (y, key[i] - key[y] + far)
+        todo = [who] if rnd >> 9 & 3 else list(mates[ops[who]["role"][1:]])
+        for j in todo:
+            key[j] += by
+        while todo:
+            j = todo.pop()
+            for k in (succ[j] if by > 0 else pre[j]):
+                if (key[j] >= key[k]) if by > 0 else (key[k] >= key[j]):
+                    key[k] = key[j] + (1e-4 if by > 0 else -1e-4)
+                    todo.append(k)
+        nx = judge(key)
+        if nx[0] < cur[0] + CFG["give"] * (1 - turn / CFG["more"]) * (rnd & 15) / 8:
+            cur = nx
+            if cur[0] < best[0]:
+                best = cur
     span = best[0]
+    best = best[1][0]
     order = sorted(range(n), key=lambda i: (best[1][i], i))
     bank = {}
     for i in order:
@@ -722,7 +721,7 @@ def schedule(ops):
         if o["k"] == "dma":
             o["sem"] = ("d%d" % i, 16)
         elif o["k"] == "send":
-            o["sem"] = (o["a"][2], 4 + 4 * CFG["md"] if CFG["md"] else CFG["eng"])
+            o["sem"] = (o["a"][2], 36)
         elif i in need:
             tot["q" + o["e"]] = tot.get("q" + o["e"], 0) + 1
             o["sem"] = ("q" + o["e"], tot["q" + o["e"]])
@@ -743,9 +742,6 @@ def rank_program(g, core, T, topo):
         return
     nxt = T.cores[(rank + 1) % len(T.cores)]
     rid, pid = topo.addr(nxt)[0:2]
-    mask = 0
-    for e in topo.engines(core, nxt)[0:CFG["eng"]]:
-        mask |= 1 << e
     quad = [sum(1 << e for e in topo.engines(core, nxt)[k::4]) for k in range(4)]
     Q = {"v": g.vector, "a": g.scalar, "p": g.tensor, "s": g.sync, "g": g}
 
@@ -768,18 +764,14 @@ def rank_program(g, core, T, topo):
         for j in o["wt"]:
             q.wait_ge(T.sem[OPS[j]["sem"][0]], OPS[j]["sem"][1])
         if k == "send":
-            if a[4]:
-                to = DstId(rid=rid, pnc=pid)
-                tr = [RemoteDMATransfer(dst_ids=[to], dma_engine_mask=quad[0], remote_sem=T.sem[a[2]], src=ap(a[1]), dst=ap(a[0]))]
-                for e in range(3):
-                    ds = [ap(r) for r in a[4][e::3]]
-                    tr.append(RemoteDMATransfer(dst_ids=[to] * len(ds), dma_engine_mask=quad[e + 1], remote_sem=T.sem[a[2]],
-                                                src=ap(a[3]), dsts=ds))
-                g.remote_dma_fused(tr, local_sem=T.sem["loc"])
-                sent += 16
-            else:
-                g.remote_dma(ap(a[0]), ap(a[1]), T.sem[a[2]], T.sem["loc"], pid, rid, mask)
-                sent += CFG["eng"]
+            to = DstId(rid=rid, pnc=pid)
+            tr = [RemoteDMATransfer(dst_ids=[to], dma_engine_mask=quad[0], remote_sem=T.sem[a[2]], src=ap(a[1]), dst=ap(a[0]))]
+            for e in range(3):
+                ds = [ap(r) for r in a[4][e::3]]
+                tr.append(RemoteDMATransfer(dst_ids=[to] * len(ds), dma_engine_mask=quad[e + 1], remote_sem=T.sem[a[2]],
+                                            src=ap(a[3]), dsts=ds))
+            g.remote_dma_fused(tr, local_sem=T.sem["loc"])
+            sent += 16
             ends[a[2]] = o["sem"][1]
             continue
         if k == "ts":
@@ -803,8 +795,11 @@ def rank_program(g, core, T, topo):
         elif k == "mm":
             for m in a:
                 x = q.matmul(ap(m[0]), ap(m[1]), ap(m[2]), m[3], m[4])
+        elif k == "as":
+            w = a[1][2] - a[1][1]
+            x = g.affine_select(ap(a[0]), ap(a[1]), [[-1 if a[3] else 0, w]], AL.not_equal, a[2], 0, 1 if a[3] else 0)
         elif k == "io":
-            if a[0][0] == "pf":
+            if a[0][0] != "pi":
                 x = g.iota(ap(a[0]), a[1], a[2], a[3], allow_small_or_imprecise_dtypes=True)
             else:
                 x = g.iota(ap(a[0]), a[1], a[2], a[3])

from concourse.bass import DstId, RemoteDMATransfer
from concourse.mybir import AluOpType as AL, ActivationFunctionType as AF

RO = 6
CFG = {"av": (0, 1), "au": (), "vl": (1,), "fin": (256, 384, 384), "send": 2.0, "xl": 7.5, "more": 5000, "give": 0.02,
       "lat": 0.1, "turns": 5,
       "slack": 0.1, "pen": 10.0, "lead": (0, 1, 1.5, 2, 2.5, 3, 3.5, 4, 5),
       "wake": ((0.19, 0.0, 0.0), (0.17, 0.17, 0.0), (0.1, 0.1, 0.025)), "pc": (512, 512, 512, 512)}
DT = {"f": "float32", "i": "int32", "b": "bfloat16", "u": "uint16", "h": "float16"}
SCRATCH = {}
LN2 = 0.6931471805599453
CY = 0.85e-3
C1 = 1.5 * 2.0 ** 23


def build():
    ops = []
    part = ["const", 0]
    roles = set()
    used = {"f": 0, "i": 0, "b": 0, "u": 0, "h": 0}

    def new(d, n):
        lo = used[d]
        used[d] = lo + (n + 15) // 16 * 16
        return ("p" + d, lo, lo + n, 1, 128, 0)

    def own(name, d, n, where="sbuf"):
        SCRATCH[name] = (where, [128, n], DT[d])
        return (name, 0, n, 1, 128, 0)

    def hbm(name, a, b):
        return (name, a, b, 1, 128, 0)

    def sl(r, a, b, st=1):
        return (r[0], r[1] + a, r[1] + b, st, r[4], r[5])

    def pt(r, p0, p1):
        return r[:4] + (p1, p0)

    def half(r, f):
        return pt(r, 64 * f, 64 * f + 64)

    def cnt(r):
        if r[0] == "@":
            return 16 * cnt(r[2])
        return len(range(r[1], r[2], r[3]))

    def two(r):
        return r[0] in ("pb", "ph", "pu", "m0s", "X0", "X1", "WS0", "WS1", "Ub", "WX", "WM", "zM", "NP", "zin", "yzb", "ymb")

    def add(e, k, a, rd, wr, cost):
        R = []
        W = []
        for r in rd:
            if isinstance(r, tuple):
                if r[0] == "@":
                    R.extend([r[1], r[2]])
                else:
                    R.append(r)
        for r in wr:
            if r[0] == "@":
                W.append(r[1])
                R.append(r[2])
            else:
                W.append(r)
        for r in R + W:
            if r[0][0] == "B":
                (W if e == "p" else R).append(("G" + r[0], 0, 1, 1, 128, 0))
        role = (part[1], part[0], e, k, W[0][0], W[0][1] % (128 if W[0][0] in ("zin", "yzb", "yz") else 1 << 20), 0)
        while role in roles:
            role = role[:6] + (role[6] + 1,)
        roles.add(role)
        ops.append({"e": e, "k": k, "a": a, "r": R, "w": W, "c": cost, "n": part[0], "role": role})

    def vc(out, ins, tt=False):
        n = cnt(out)
        if out[0] == "@":
            return 0.05 + n * 3.8 * CY
        if ins[0][0] == "@":
            return 0.05 + n * 1.56 * CY
        f = 0.5 if all(two(r) for r in ins + [out]) else 1.0
        if tt and all(r[0][0] != "B" for r in ins):
            f *= 2
        return 0.05 + max(64, n * f) * CY

    def TS(out, in0, s1, s2, o0, o1=None):
        add("v", "ts", (out, in0, s1, s2, o0, o1), [in0, s1, s2], [out], vc(out, [in0]))

    def TT(out, a, b, o):
        add("v", "tt", (out, a, b, o), [a, b], [out], vc(out, [a, b], True))

    def CP(out, a):
        add("v", "cp", (out, a), [a], [out], vc(out, [a]))

    def SC(out, a, b, ini, o0, o1):
        add("v", "sc", (out, a, b, ini, o0, o1), [a, b], [out], vc(out, [a, b]))

    def MS(out, v):
        add("v", "ms", (out, v), [], [out], vc(out, [out]))

    def AC(out, a, fn, bias=0.0, scale=1.0, acc=None):
        n = cnt(out)
        add("a", "ac", (out, a, fn, bias, scale, acc), [a, bias, scale], [out] + ([acc] if acc else []),
            0.065 + max(64, n * (1.56 if a[0] == "@" else 1.0)) * CY)

    def AS(out, a, scale, bias=0.0):
        AC(out, a, AF.Identity, bias, scale)

    def MM(lst):
        c = 0.03
        for o, l, r, s0, s1 in lst:
            c += max(min(64, cnt(l)), cnt(r)) * (4 if l[0] == "pf" else 1) * CY / 2
        add("p", "mm", lst, [x[1] for x in lst] + [x[2] for x in lst], [x[0] for x in lst], c)

    def ACC(out, pairs):
        n = len(pairs)
        return [(out, l, r, i == 0, i == n - 1) for i, (l, r) in enumerate(pairs)]

    def IO(out, pat, base, cm):
        add("g", "io", (out, pat, base, cm), [], [out], 0.13 + cnt(out) * 2 * CY)

    def GS(out, v, diag=False):
        if out[4] - out[5] < 128:
            return MS(out, v)
        zero = sl(Z[out[0]], 0, cnt(out))
        add("g", "as", (out, zero, v, diag), [zero], [out], 0.17 + cnt(out) * 2 * CY)

    def DMA(q, out, a, cost):
        add(q, "dma", (out, a), [a], [out], cost)

    X = [own("X%d" % h, "b", 8256) for h in range(2)]
    WS = [own("WS%d" % h, "b", 4096) for h in range(2)]
    Ub = own("Ub", "b", 256)
    WX = own("WX", "b", 4224)
    WM = own("WM", "b", 4224)
    zM = own("zM", "h", 4096)
    NP = own("NP", "b", 4096)
    zin = own("zin", "b", 768)
    yzb = own("yzb", "b", 768)
    ymb = own("ymb", "b", 4096)
    B = [own("B%d" % k, "f", 512, "psum") for k in range(8)]
    m0s = own("m0s", "b", 64)
    wts = own("wts", "b", 16)

    for h in (1, 0):
        for f in range(2):
            DMA("a", half(sl(zin, 64 * h, 64 * h + 64), f), half(hbm("z0", 64 * f, 64 * f + 64), h), 2.0)
            DMA("a", half(sl(m0s, 32 * h, 32 * h + 32), f), half(hbm("m0", 0, 32), h), 2.0)
            DMA("a", half(sl(wts, 8 * h, 8 * h + 2), f), half(hbm("wt", 0, 2), h), 2.0)
            DMA("s", half(sl(X[h], 0, 8192), f), half(hbm("xr", 0, 8192), h), CFG["xl"] * (2 - h))

    Z = {"pb": new("b", 192), "pf": new("f", 128)}
    IO(Z["pb"], [[0, 192]], 0, 0); IO(Z["pf"], [[0, 128]], 0, 0)
    Z["WM"] = Z["pb"]
    dif = new("i", 128); IO(dif, [[-1, 128]], 128, 1)
    dif2 = new("i", 152); IO(dif2, [[-1, 152]], 24, 1)
    kt0 = new("f", 128); IO(kt0, [[-2, 16], [0, 8]], 30, 0)
    ip = new("i", 1); IO(ip, [[0, 1]], 0, 1)
    ip16 = new("i", 1); IO(ip16, [[0, 1]], 0, 16)
    ib = new("f", 128); IO(ib, [[16, 8], [0, 16]], 0, 0)
    im = new("i", 128); IO(im, [[1, 32], [0, 4]], 0, 0)
    k8 = new("f", 8); IO(k8, [[0, 2], [16, 4]], 0, 0)
    k9 = new("f", 128); IO(k9, [[0, 32], [16, 4]], 0, 0)
    KF = new("b", 128); IO(KF, [[0, 16], [16, 2], [0, 4]], 0, 0)
    d5 = new("f", 5); IO(d5, [[-3, 5]], 0, 0)
    i8 = new("f", 128); IO(i8, [[0, 16], [1, 8]], 0, 0)
    i16 = new("f", 64); IO(i16, [[0, 4], [1, 16]], 0, 0)
    j65 = new("f", 260); IO(j65, [[-16, 4], [1, 65]], 0, 0)
    n65 = new("f", 260); IO(n65, [[0, 4], [-1, 65]], -8192, 0)
    IO(sl(j65, 48, 65), [[1, 17]], 0, 0); IO(sl(n65, 48, 65), [[-1, 17]], -8192, 0)
    I = new("b", 128); GS(I, 1.0, True)
    If32 = new("f", 128); GS(If32, 2.0 ** 19, True)
    t0 = new("i", 128); TS(t0, dif, 63, None, AL.bitwise_and)
    P2 = new("b", 128); TS(P2, t0, 0.0, None, AL.is_equal)
    PF = [new("f", 128), new("f", 128)]
    for f in range(2):
        GS(half(PF[f], 1 - f), 0.0); AS(half(PF[f], f), half(P2, f), -16384.0)
    t1 = new("i", 1); pg = new("f", 1); TS(t1, ip, 112, None, AL.bitwise_and); CP(pg, t1)
    t2 = new("i", 1); pp = new("f", 1); TS(t2, ip, 15, None, AL.bitwise_and); CP(pp, t2)
    t3 = new("i", 1); s64 = new("f", 1); TS(t3, ip16, 1984, None, AL.bitwise_and); CP(s64, t3)
    sc = new("f", 1); AS(sc, s64, 1.0 / 64)
    BD = new("b", 128); TS(BD, ib, pg, None, AL.is_equal)
    G8 = sl(BD, 0, 128, 16)
    WhZ = [new("h", 16), new("h", 16)]; WhM = [new("b", 24), new("b", 24)]
    Wr = [[new("b", 128), new("b", 128)], [new("b", 128), new("b", 128)]]
    for h in (1, 0):
        for e in range(2):
            wc = sl(wts, 8 * h + e, 8 * h + e + 1)
            TS(sl(WhZ[h], 8 * e, 8 * e + 8), G8, wc, -2.0 ** -12, AL.mult, AL.mult)
            TS(sl(WhM[h], 8 * e, 8 * e + 8), G8, wc, -0.25, AL.mult, AL.mult)
            wf = new("f", 1); AS(wf, wc, 32.0 - 64 * e); AS(Wr[h][e], BD, wf)
        AS(sl(WhM[h], 16, 24), G8, 1.0)
    OFF = new("b", 128)
    for e in range(2):
        sg = 2.0 * e - 1.0
        GS(pt(sl(OFF, 64 * e, 64 * e + 64), 0, 32), 64 * sg)
        GS(pt(sl(OFF, 64 * e, 64 * e + 64), 32, 64), -sg / 64)
    GS(pt(OFF, 64, 128), 0.0)
    om = new("u", 128); CP(om, im)
    TS(sl(WM, 2112, 3136), ("@", sl(m0s, 32, 64), sl(om, 0, 64)), -1.0, None, AL.mult)
    AC(sl(WM, 3136, 4160), ("@", sl(m0s, 32, 64), sl(om, 64, 128)), AF.Copy, 0.0, -1.0)
    AC(sl(WM, 0, 2048), ("@", sl(m0s, 0, 32), om), AF.Copy, 0.0, -1.0)
    GS(sl(WM, 2048, 2112), 0.0); GS(sl(WM, 4160, 4224), 0.0)
    t4 = new("i", 128); TS(t4, dif, 3, None, AL.bitwise_and)
    B4 = new("b", 128); TS(B4, t4, 0.0, None, AL.is_equal)
    SEL = sl(B4, 0, 4)
    t5 = new("i", 1); t6 = new("f", 1); TS(t5, ip, 3, None, AL.bitwise_and); CP(t6, t5)
    t7 = new("f", 128); TS(t7, i8, t6, None, AL.subtract)

    def diag(v):
        o = new("b", 128)
        GS(o, v, True)
        return o
    I9 = diag(9.0); Ig = diag(-2.0 ** 18); Iw = diag(1.5 * 2.0 ** -63); I7 = diag(-0.875); Ih = diag(0.5)
    Inh = diag(-0.5); Iq = diag(0.25); Ia = diag(-32.5); Ib = diag(32.0); In = diag(-8192.0); Ine = diag(-1.0)
    Im = diag(-256.0)
    B4q = new("b", 128); AS(B4q, B4, 0.25)
    I9h = new("h", 128); TS(I9h, I, 9.0, None, AL.mult)
    ones = new("b", 192); GS(ones, 1.0)
    o128 = sl(ones, 0, 128)
    o32 = new("b", 128); GS(o32, 32.0)
    oh = new("b", 40); GS(oh, -1.0 / 256)
    halff = new("f", 128); GS(halff, 0.5)
    KOf = new("f", 8); AS(KOf, k8, 1.0, pp)
    KO = new("b", 8); AS(KO, k8, 1.0, pp)
    KC = new("b", 128); AS(KC, k9, 1.0, pp)
    SEL3 = new("b", 12)
    for e in range(3):
        AS(sl(SEL3, 4 * e, 4 * e + 4), SEL, 2.0 ** (9 * e - 18))
    c0 = new("f", 64); c1 = new("f", 64); ctl1 = new("f", 64); pq = new("f", 1)
    AS(pq, pp, 1.0, 1.0)
    TS(c0, i16, pp, None, AL.not_equal); TS(c1, i16, pq, 511.0, AL.is_equal, AL.mult); TT(ctl1, c0, c1, AL.add)
    kn = new("f", 1); kr = new("f", 1); k0 = new("f", 1); k1 = new("f", 1); k2 = new("f", 1)
    TS(k0, pp, 15.0, 511.0, AL.not_equal, AL.mult)
    AS(kn, k0, -1.0, -1.0)
    TS(k1, pp, 15.0, 2.0 ** -29, AL.is_equal, AL.mult); TS(k2, pp, 15.0, 2.0 ** -38, AL.not_equal, AL.mult)
    TT(kr, k1, k2, AL.add)
    c2 = new("f", 260); ctl2 = new("f", 260)
    TS(c2, j65, pp, 2.0 ** -14, AL.is_equal, AL.mult); TT(ctl2, c2, n65, AL.mult); MS(sl(ctl2, 0, 260, 65), 2.0 ** 40)
    MS(sl(ctl2, 48, 49), 2.0 ** 40)
    Dm = new("f", 5); AS(Dm, d5, 1.0, pp)
    ee = [new("f", 5) for e in range(3)]
    for e in range(3):
        TS(ee[e], Dm, float(e), -2.0 ** (18 - 9 * e), AL.is_equal, AL.mult)
    e3 = new("f", 5); TS(e3, Dm, 0.0, 2.0 ** 19, AL.is_lt, AL.mult)
    f0 = new("f", 5); f1 = new("f", 5); tw = new("f", 5)
    TT(f0, ee[0], ee[1], AL.add); TT(f1, ee[2], e3, AL.add); TT(tw, f0, f1, AL.add)
    CN = new("b", 40)
    for a in range(5):
        AS(sl(CN, 8 * a, 8 * a + 8), G8, sl(tw, a, a + 1))
    REP = new("b", 384)
    for e in range(3):
        RT = new("b", 40)
        for a in range(5):
            AS(sl(RT, 8 * a, 8 * a + 8), G8, sl(ee[e], a, a + 1))
        MM(ACC(pt(sl(B[7], 128 * e, 128 * e + 128), 0, 40), [(RT, I)]))
        AS(pt(sl(REP, 128 * e, 128 * e + 128), 0, 40), pt(sl(B[7], 128 * e, 128 * e + 128), 0, 40), -2.0 ** (9 * e - 10))
    OG = new("b", 4); OP = new("b", 4); OT = new("b", 4); OU = new("b", 4); ON = new("b", 4)
    s6m = new("f", 1); s32 = new("f", 1); AS(s6m, s64, 0.5, -1024.0); AS(s32, s64, 0.5)
    AS(OG, SEL, s6m); AS(OU, OG, -1.0); AS(OP, SEL, s32); AS(OT, OP, -1.0)
    GS(ON, 16.0)
    PZ = new("b", 152); TS(PZ, dif2, 0.0, s64, AL.is_equal, AL.mult)
    RK = new("b", 24)
    for k in range(RO - 1):
        gk = new("f", 1)
        TS(gk, s64, 64.0 * k, s64, AL.is_gt, AL.mult)
        AS(sl(RK, 4 * k, 4 * k + 4), SEL, gk)
    BF = [new("b", 128), new("b", 128)]
    for f in range(2):
        TS(BF[f], t7, 4.0 * f, None, AL.is_equal)
    t8 = new("i", 1); TS(t8, ip, 64, None, AL.bitwise_and)
    k64 = new("f", 1); TS(k64, t8, -0.5, 0.5, AL.mult, AL.add)
    KT = new("f", 128); AS(KT, kt0, 1.0, k64)
    thr = [new("f", 1) for t in range(RO)]
    GS(thr[0], 2.0)
    H = []
    for h in range(2):
        d = {}
        for nm, dt_, n in (("w", "b", 128), ("rk", "b", 128), ("sig", "b", 384), ("x0", "b", 64), ("zr", "h", 512),
                           ("r", "i", 256), ("zw", "b", 128), ("cm", "b", 128), ("uv", "f", 256), ("x", "f", 128),
                           ("fl", "f", 128), ("t", "f", 128),
                           ("y", "f", 128), ("r2", "b", 128), ("off", "u", 128), ("mw", "b", 128), ("D", "b", 64),
                           ("yb", "f", 64), ("Q", "b", 640), ("hh", "f", 192), ("nz", "b", 192), ("mj", "b", 64),
                           ("U", "b", 64), ("zU", "b", 64), ("ur", "b", 128), ("uuv", "f", 128), ("ux", "f", 64),
                           ("ufl", "f", 64), ("ut", "f", 64), ("uy", "f", 64), ("ur2", "f", 64), ("npl", "f", 64),
                           ("no", "f", 64), ("dd", "f", 260), ("mn", "f", 260), ("ow", "u", 8), ("Hc", "f", 1),
                           ("E", "b", 11 * 128), ("LB", "b", 136), ("dl", "b", 128), ("sh", "b", 128), ("md", "b", 128),
                           ("fo", "u", 128)):
            d[nm] = new(dt_, n)
        d["zl"] = [new("h", 512) for t in range(RO - 1)]
        d["zs"] = [new("h", 64) for t in range(RO - 1)]
        d["o"] = [new("u", 8), new("u", 8)]
        H.append(d)
        AS(d["rk"], o128, sc)
        AC(d["w"], d["rk"], AF.Exp, 30 * LN2, -3 * LN2)
        CP(d["o"][1], KOf)
    par = new("f", 1)

    def hashf(n, sg, uv, x, fl, t, y):
        q = sg * sg
        SC(x, sl(uv, 0, n), sl(uv, n, 2 * n), 0.0, AL.max, AL.mult)
        AS(t, sl(uv, 0, n), 1184.0 * sg, 259915760.0 * q)
        TS(fl, x, 8388591.5 * q, (2.0 ** 28 + 2.0 ** 23) * q, AL.add, AL.add)
        SC(y, t, fl, 0.0, AL.max, AL.subtract)

    def front(t, h):
        d = H[h]
        z = sl(zin, 128 * t + 64 * h, 128 * t + 64 * h + 64)
        part[0] = "front%d" % h
        if t:
            zr = d["zl"][t - 1]
        else:
            zr = d["zr"]
            TS(sl(zr, 0, 64), z, -1024.0, None, AL.add)
            TS(sl(zr, 64, 128), z, -1024.0, None, AL.add)
            CP(sl(zr, 128, 256), sl(zr, 0, 128))
            CP(sl(zr, 256, 512), sl(zr, 0, 256))
        for q in range(4):
            SC(sl(zM, 2048 * h + 512 * q, 2048 * h + 512 * q + 512), zr,
               sl(WM, 2112 * h + 512 * q, 2112 * h + 512 * q + 512), 0.0, AL.min, AL.mult)
        MM([(sl(B[0], b, 384, 16), sl(WM, 2112 * h + b, 2112 * h + 2048, 16), WhM[h], b == 0, False) for b in range(16)])
        MM([(sl(B[0], b, 256, 16), sl(zM, 2048 * h + b, 2048 * h + 2048, 16), WhZ[h], False, b == 15) for b in range(16)])
        TS(d["r"], sl(B[0], 0, 256), -0.5 + 2.0 ** -13, None, AL.add)
        TT(sl(d["uv"], 0, 128), sl(B[0], 0, 128), sl(d["r"], 0, 128), AL.subtract)
        TT(sl(d["uv"], 128, 256), sl(d["r"], 128, 256), sl(B[0], 128, 256), AL.subtract)
        hashf(128, 2.0 ** -12, d["uv"], d["x"], d["fl"], d["t"], d["y"])
        AC(d["cm"], sl(B[0], 256, 384), AF.Copy)
        ops[-1]["r"].append(d["t"])
        AS(d["r2"], d["y"], 64.0, 240.0)
        MM([(sl(B[0], 384, 512), d["y"], If32, True, False)])
        MM([(sl(B[0], 384, 512), d["r2"], In, False, True)])
        TS(d["off"], sl(B[0], 384, 512), 240 * 8192 + 4095.5, None, AL.add)

    def probe(t, h):
        d = H[h]
        z = sl(zin, 128 * t + 64 * h, 128 * t + 64 * h + 64)
        a = 0
        part[0] = "probe%d" % h
        for q, n in enumerate(CFG["pc"]):
            xh = sl(WX, 2112 * h + a, 2112 * h + a + n)
            src = ("@", sl(X[h], 0, 8192), sl(d["off"], a // 16, (a + n) // 16))
            if t == RO - 1 and h == 0 and q in CFG["vl"]:
                CP(xh, src)
            else:
                AC(xh, src, AF.Copy)
            bk = sl(B[1 + q % 2], 0, n)
            MM([(bk, I9h, sl(zM, 2048 * h + a, 2048 * h + a + n), True, False)])
            MM([(bk, I9, xh, False, True)])
            TS(sl(NP, 2048 * h + a, 2048 * h + a + n), bk, 1.5 * 2.0 ** 33 - 9216, 1.5 * 2.0 ** 33, AL.add, AL.is_equal)
            a += n
        AC(d["x0"], ("@", sl(WX, 2112 * h, 2112 * h + 2048), sl(d["o"][(t + 1) % 2], 4, 8)), AF.Copy)
        av = sl(B[4 + 2 * h], 0, 64)
        MM(ACC(av, [(Ih, z), (Iq, sl(ones, 0, 64)), (Inh, d["x0"])]))
        if h in CFG["av"]:
            AC(d["yb"], av, AF.Identity, C1)
            AC(sl(WX, 2112 * h + 2048, 2112 * h + 2112), d["yb"], AF.Identity, -C1)
        else:
            TS(sl(WX, 2112 * h + 2048, 2112 * h + 2112), av, C1, -C1, AL.add, AL.add)

    def back(t, h):
        d = H[h]
        last = t == RO - 1
        z = sl(zin, 128 * t + 64 * h, 128 * t + 64 * h + 64)
        gt, ge, gp = sl(d["sig"], 0, 128), sl(d["sig"], 128, 256), sl(d["sig"], 256, 384)
        w, o = d["w"], d["o"][t % 2]
        F, S7 = [B[3 + 2 * h], B[4 + 2 * h]], B[7]
        cn = sl(S7, 384, 512)
        part[0] = "match%d" % h
        for x in range(2):
            MM([(sl(F[x], 64 + k, 384, 8), sl(WM, 2112 * h + 2 * k + x, 2112 * h + 2048, 16), CN, k == 0, False)
                for k in range(8)])
        MM([(cn, I, d["cm"], True, False)]
           + [(sl(S7, 384 + b, 512, 16), sl(NP, 2048 * h + b, 2048 * h + 2048, 16), G8, False, b == 15) for b in range(16)])
        AC(cn, cn, AF.Relu, thr[t])
        TT(d["mw"], cn, w, AL.mult)
        for x in range(2):
            MM([(sl(F[x], 64 + k, 384, 8), sl(NP, 2048 * h + 2 * k + x, 2048 * h + 2048, 16), CN, False, False)
                for k in range(8)])
        MM(ACC(sl(S7, 0, 128), [(I7, w), (B4q, d["mw"])]) + ACC(sl(S7, 128, 256), [(I7, w), (B4, d["mw"])]))
        AC(sl(d["sig"], 0, 256), sl(S7, 0, 256), AF.Sign, 0.0, 1.0, None if last else d["Hc"])
        MM(ACC(sl(S7, 384, 388), [(I, sl(KO, 0, 4)), (o128, ON), (gt, OU), (ge, OG)]))
        CP(sl(o, 0, 4), sl(S7, 384, 388))
        if last:
            sg = sl(S7, 0, 128)
            MM([(half(sg, k), sl(gt, 64 * f, 64 * f + 64), BF[f], f == 0, f == 1) for k in range(2) for f in range(2)])
            TT(d["sh"], sg, KT, AL.is_lt)
            TT(d["md"], d["sh"], d["dl"], AL.mult)
            MM(ACC(sl(S7, 128, 256), [(I, sl(d["LB"], 8, 136)), (I, KC), (o128, KF), (I, d["md"])]))
            CP(d["fo"], sl(S7, 128, 256))
            a = 0
            for n in CFG["fin"]:
                for q in range(2):
                    src = ("@", WS[h], sl(d["fo"], (a + n * q) // 16, (a + n * q + n) // 16))
                    dst = sl(ymb, 2048 * h + a + n * q, 2048 * h + a + n * q + n)
                    if q:
                        AC(dst, src, AF.Copy, 0.0, -1.0)
                    else:
                        TS(dst, src, -1.0, None, AL.mult)
                for k in range(2):
                    b = max(a, 128 - 128 * k)
                    DMA("s", half(hbm("ym", 2048 * k + b, 2048 * k + a + 2 * n), h),
                        half(sl(ymb, 2048 * h + b, 2048 * h + a + 2 * n), k), 1.7 + n / 640)
                a += 2 * n
        else:
            MM(ACC(sl(S7, 256, 384), [(I7, w), (Iw, o128), (B4, d["mw"])]))
            AC(gp, sl(S7, 256, 384), AF.Sign)
        nzr = sl(yzb, 128 * t + 64 * h, 128 * t + 64 * h + 64)
        TT(d["D"], ("@", sl(WX, 2112 * h, 2112 * h + 2112), sl(o, 0, 4)), z, AL.subtract)
        AC(nzr, d["D"], AF.Abs)
        if not last:
            zn = sl(zin, 128 * t + 128 + 64 * h, 128 * t + 192 + 64 * h)
            to = [sl(d["zl"][t], 64 * k, 64 * k + 64) for k in range(8)]
            TS(d["zs"][t], nzr, -1024.0, None, AL.add)
            add("g", "send", (zn, nzr, "ar%d_%d" % (t, h), d["zs"][t], to), [nzr, d["zs"][t]], [zn] + to, CFG["send"] + 0.8)
        for f in range(2):
            DMA("s", half(hbm("yz", 128 * t + 64 * f, 128 * t + 64 * f + 64), h), half(nzr, f), 2.0)
        part[0] = "mask%d" % h
        if not last:
            MM(ACC(sl(S7, 384, 388), [(I, sl(KO, 4, 8)), (gt, OT), (gp, OP)]))
            CP(sl(o, 4, 8), sl(S7, 384, 388))
        AC(d["mj"], ("@", sl(WM, 2112 * h, 2112 * h + 2112), sl(o, 0, 4)), AF.Copy)
        for x in range(2):
            MM([(sl(F[x], 64 * a + 64, 64 * a + 128), Ig, sl(gt, x, 128, 2), False, a == 4) for a in range(5)])
            AC(sl(d["Q"], x, 640, 2), sl(F[x], 64, 384), AF.Relu, -2.0 ** 18)
        y = pt(sl(F[0], 0, 192), 0, 40)
        MM([(y, oh, ones, True, False)])
        MM([(pt(sl(F[0], b, 192, 16), 0, 40), sl(d["Q"], b, 640, 16), SEL3, False, b == 15) for b in range(16)])
        hh, nz = pt(d["hh"], 0, 40), pt(d["nz"], 0, 40)
        TS(hh, y, 1.5 * 2.0 ** 32, -1.5 * 2.0 ** 32, AL.add, AL.add)
        TT(nz, y, hh, AL.is_ge)
        Y = sl(F[1], 0, 64)
        MM(ACC(Y, [(Im, d["mj"])] + [(pt(sl(REP, 128 * e, 128 * e + 128), 0, 40), pt(sl(d["nz"], 64 * e, 64 * e + 64), 0, 40))
                                     for e in range(3)]))
        if not last:
            TT(d["zU"], Y, z, AL.min)
        if h in CFG["au"]:
            AC(d["U"], Y, AF.Sign, 0.0, -1.0)
        else:
            TS(d["U"], Y, -1.0, -1.0, AL.mult, AL.max)
        if last:
            part[0] = "rank%d" % h
            MM([(half(sl(F[0], 256 + 64 * f, 320 + 64 * f), 0), sl(Ine, 64 * f, 64 * f + 64), d["U"], True, True)
                for f in range(2)])
            AC(half(sl(Ub, 128 * h, 128 * h + 128), 0), half(sl(F[0], 256, 384), 0), AF.Copy)
            DMA("s", half(hbm("ym", 0, 128), h), half(sl(Ub, 128 * h, 128 * h + 128), 0), 2.0)
            return
        CP(("@", sl(WM, 2112 * h, 2112 * h + 2048), sl(o, 4, 8)), d["U"])
        if t == RO - 2:
            for f in range(2):
                for k in range(2):
                    DMA("s", half(sl(WS[h], 2048 * f, 2048 * f + 2048), k), half(sl(WM, 2112 * h, 2112 * h + 2048), f), 3.0)
        part[0] = "rank%d" % h
        MM(ACC(sl(F[1], 384, 512), [(I, d["rk"]), (Ia, gp), (Ib, gt)]))
        AC(d["rk"], sl(F[1], 384, 512), AF.Relu, 0.5)
        AC(w, d["rk"], AF.Exp, 30 * LN2, -3 * LN2)
        part[0] = "write%d" % h
        for f in range(2):
            for k in range(2):
                DMA("s", half(sl(d["zw"], 64 * f, 64 * f + 64), k), half(z, f), 2.0)
        MM([(sl(F[0], 384, 512), o32, OFF, True, False)])
        MM([(sl(F[0], 256 + 64 * k, 320 + 64 * k), Wr[h][k % 2], d["zU"], False, k == 3) for k in range(4)])
        TS(d["ur"], sl(F[0], 384, 512), 1.5 * 2.0 ** 40, -1.5 * 2.0 ** 40, AL.add, AL.add)
        TT(d["uuv"], sl(F[0], 256, 384), d["ur"], AL.subtract)
        hashf(64, 32.0, d["uuv"], d["ux"], d["ufl"], d["ut"], d["uy"])
        TS(d["ur2"], d["uy"], 1.5 * 2.0 ** 51, -(1.5 * 2.0 ** 51 + 2.0 ** 29), AL.add, AL.add)
        SC(d["npl"], d["ur2"], d["uy"], 0.0, AL.min, AL.subtract)
        SC(d["no"], ctl1, d["npl"], 0.0, AL.mult, AL.min)
        for c in range(4):
            a = 0 if c else 48
            AC(sl(d["dd"], 65 * c + a, 65 * c + 64), sl(d["npl"], 0, 64 - a), AF.Abs, sl(d["no"], 16 * c + 15, 16 * c + 16), kn)
        TS(sl(d["dd"], 64, 260, 65), sl(d["no"], 15, 64, 16), kr, 12288.5 / 16384, AL.mult, AL.add)
        SC(sl(d["mn"], 48, 260), sl(ctl2, 48, 260), sl(d["dd"], 48, 260), 0.0, AL.add, AL.min)
        MM([(sl(F[0], 4 * f, 4 * f + 4), PF[f], sl(d["mn"], 64, 260, 65), True, True) for f in range(2)])
        CP(d["ow"], sl(F[0], 0, 8))
        for f in (1, 0):
            CP(("@", X[h], sl(d["ow"], 4 * f, 4 * f + 4)), sl(d["zw"], 64 * f, 64 * f + 64))

    def lists(h):
        d = H[h]
        part[0] = "list%d" % h
        E = [sl(d["E"], 128 * k, 128 * k + 128) for k in range(11)]
        for k in range(6):
            TS(E[k], d["rk"], sc, float(k), AL.subtract, AL.is_equal)
        for k in range(5):
            TS(E[6 + k], d["rk"], float(k), None, AL.is_equal)
        L = [sl(B[4 + 2 * h], 128 + 80 * f, 196 + 80 * f) for f in range(2)]
        for u in (1, 0):
            for k in range(6):
                MM([(half(L[f], u), sl(E[k], 64 * f, 64 * f + 64), sl(PZ, 20 - 4 * k + 64 * u, 88 - 4 * k + 64 * u),
                     k + f == 0, k + f + u == 7) for f in range(2)])
        for k in range(5):
            MM([(half(sl(L[f], 4 * k + 4, 4 * k + 8), 0), sl(E[6 + k], 64 * f, 64 * f + 64), sl(RK, 4 * k, 4 * k + 4),
                 False, k + f == 5) for f in range(2)])
        for f in range(2):
            for c in range(4):
                AS(sl(d["LB"], 4 * f + c, 136, 8), sl(L[f], c, 68, 4), 1.0)
        TT(d["dl"], sl(d["LB"], 0, 128), sl(d["LB"], 8, 136), AL.subtract)

    for t in range(RO):
        part[1] = t
        for h in (1, 0):
            front(t, h)
        for h in (1, 0):
            probe(t, h)
            back(t, h)
            if t == RO - 2:
                lists(h)
        if t < RO - 1:
            tot = sl(B[7], 0, 1)
            MM(ACC(tot, [(halff, H[1]["Hc"]), (halff, H[0]["Hc"])]))
            TS(par, tot, 1.5 * 2.0 ** 24, -1.5 * 2.0 ** 24, AL.add, AL.add)
            TS(thr[t + 1], par, tot, 2.0, AL.not_equal, AL.add)
    for k in used:
        SCRATCH["p" + k] = ("sbuf", [128, used[k]], DT[k])
    return ops


def meets(a, b):
    if a[0] != b[0] or a[1] >= b[2] or b[1] >= a[2] or a[5] >= b[4] or b[5] >= a[4]:
        return False
    if a[3] > 1 and a[3] == b[3] and (a[1] - b[1]) % a[3]:
        return False
    return True


def schedule(ops):
    n = len(ops)
    hist = {}
    for i, o in enumerate(ops):
        dep = set()
        for r in o["r"]:
            for (j, q, wr) in hist.get(r[0], []):
                if wr and meets(q, r):
                    dep.add(j)
        for r in o["w"]:
            lst = hist.get(r[0], [])
            for (j, q, wr) in lst:
                if meets(q, r):
                    dep.add(j)
            if o["e"] != "p" or r[0][0] == "G":
                hist[r[0]] = [x for x in lst if not (r[3] == 1 and r[5] <= x[1][5] and r[4] >= x[1][4]
                                                     and r[1] <= x[1][1] and x[1][2] <= r[2])]
        for r in o["r"]:
            hist.setdefault(r[0], []).append((i, r, False))
        for r in o["w"]:
            hist.setdefault(r[0], []).append((i, r, True))
            if len(hist[r[0]]) > 400 and r[0][0] == "B":
                hist[r[0]] = hist[r[0]][-300:]
        dep.discard(i)
        o["d"] = dep
        o["b"] = sorted(set(r[0] for r in o["r"] + o["w"] if r[0][0] == "B"))
    succ = [[] for k in range(n)]
    for i, o in enumerate(ops):
        for j in o["d"]:
            succ[j].append(i)
    pre = [o["d"] for o in ops]
    eng = [o["e"] for o in ops]
    bks = [o["b"] for o in ops]

    def waits(i, j):
        return ops[i]["e"] != "p" or ops[j]["e"] != "p"

    def case(lat, own, call):
        cost = [o["c"] + (call if o["e"] == "v" else 0.0) for o in ops]
        busy = [0.1 if o["k"] == "dma" else 0.4 if o["k"] == "send" else cost[i] for i, o in enumerate(ops)]
        gap = {}
        for i in range(n):
            for j in pre[i]:
                far = eng[i] != eng[j] or ops[i]["k"] == "dma" or ops[j]["k"] == "dma"
                gap[(i, j)] = gap[(j, i)] = lat if far else own if waits(i, j) else 0.0
        return lat, cost, busy, gap, [[(j, cost[j] + gap[(i, j)]) for j in pre[i]] for i in range(n)]

    def run(key, before, after, slack, m):
        lat, cost, busy, gap = m[0:4]
        left = [len(before[i]) for i in range(n)]
        can = [0.0] * n
        ready = [i for i in range(n) if left[i] == 0]
        free = {}
        held = {}
        st = [0.0] * n
        while ready:
            est = {}
            for i in ready:
                o = ops[i]
                s = max(can[i], free.get(o["e"], 0.0))
                for b in o["b"]:
                    for e, f in held.get(b, {}).items():
                        if e != o["e"]:
                            s = max(s, f + lat)
                est[i] = s
            i0 = min(ready, key=lambda i: (est[i], key[i]))
            c = [i for i in ready if ops[i]["e"] == ops[i0]["e"] and est[i] <= est[i0] + slack]
            i = min(c, key=lambda k: key[k] + CFG["pen"] * (est[k] - est[i0]))
            o = ops[i]
            st[i] = est[i]
            for b in o["b"]:
                held.setdefault(b, {})[o["e"]] = est[i] + cost[i]
            free[o["e"]] = est[i] + busy[i]
            ready.remove(i)
            for j in after[i]:
                can[j] = max(can[j], est[i] + cost[i] + gap[(i, j)])
                left[j] -= 1
                if left[j] == 0:
                    ready.append(j)
        return st

    def times(seq, m):
        lat, cost, busy, gap, prl = m
        st = [0.0] * n
        why = [-1] * n
        free = {}
        held = {}
        for i in seq:
            s, y = free.get(eng[i], (0.0, -1))
            for j, c in prl[i]:
                if st[j] + c > s:
                    s, y = st[j] + c, -2 - j
            for b in bks[i]:
                hb = held.setdefault(b, {})
                for e in hb:
                    if e != eng[i] and hb[e][0] > s:
                        s, y = hb[e]
            st[i] = s
            why[i] = y
            free[eng[i]] = (s + busy[i], i)
            for b in bks[i]:
                held[b][eng[i]] = (s + cost[i] + lat, i)
        last = max(range(n), key=lambda i: st[i] + cost[i])
        return st[last] + cost[last], st, why, last

    def judge(key):
        seq = sorted(range(n), key=lambda k: (key[k], k))
        ts = [times(seq, m) for m in cases]
        return sum(t[0] for t in ts) / len(ts), ts

    cases = [case(*c) for c in CFG["wake"]]
    best = None
    for m in cases:
        pr = [0.0] * n
        for i in range(n - 1, -1, -1):
            pr[i] = m[1][i] + max([pr[j] + m[3][(i, j)] for j in succ[i]] + [0.0])
        for lead in CFG["lead"]:
            key = [-pr[i] - (lead if ops[i]["n"][-1] == "1" else 0.0) for i in range(n)]
            for turn in range(CFG["turns"]):
                st = run(key, pre, succ, CFG["slack"], m)
                nx = judge(st)
                if best is None or nx[0] < best[0]:
                    best = nx
                bw = run([-(st[i] + m[1][i]) for i in range(n)], succ, pre, CFG["slack"], m)
                key = [-(bw[i] + m[1][i]) for i in range(n)]
    mates = {}
    for i, o in enumerate(ops):
        mates.setdefault(o["role"][1:], []).append(i)
    cur = best
    rnd = 2
    for turn in range(CFG["more"]):
        pairs = []
        now = cur[1][turn % len(cases)]
        i = now[3]
        while i != -1:
            y = now[2][i]
            if y >= 0 and y not in pre[i]:
                pairs.append((y, i))
            i = y if y >= -1 else -2 - y
        rnd = (rnd * 1103515245 + 12345) % 2147483648
        y, i = pairs[(rnd >> 12) % len(pairs)]
        key = list(now[1])
        far = 0.001 + (rnd >> 4 & 31) / 100
        who, by = (i, key[y] - key[i] - far) if rnd >> 11 & 1 else (y, key[i] - key[y] + far)
        todo = [who] if rnd >> 9 & 3 else list(mates[ops[who]["role"][1:]])
        for j in todo:
            key[j] += by
        while todo:
            j = todo.pop()
            for k in (succ[j] if by > 0 else pre[j]):
                if (key[j] >= key[k]) if by > 0 else (key[k] >= key[j]):
                    key[k] = key[j] + (1e-4 if by > 0 else -1e-4)
                    todo.append(k)
        nx = judge(key)
        if nx[0] < cur[0] + CFG["give"] * (1 - turn / CFG["more"]) * (rnd & 15) / 8:
            cur = nx
            if cur[0] < best[0]:
                best = cur
    span = best[0]
    best = best[1][0]
    order = sorted(range(n), key=lambda i: (best[1][i], i))
    bank = {}
    for i in order:
        o = ops[i]
        o["s"] = best[1][i]
        for b in o["b"]:
            for e, j in bank.get(b, {}).items():
                if e != o["e"]:
                    o["d"].add(j)
            bank.setdefault(b, {})[o["e"]] = i
    pos = {}
    for k, i in enumerate(order):
        pos[i] = k
    seen = {}
    need = set()
    for i in order:
        o = ops[i]
        best = {}
        for j in o["d"]:
            p = ops[j]
            if p["k"] in ("dma", "send"):
                best[("x", j)] = j
            elif waits(i, j):
                if ("q", p["e"]) not in best or pos[j] > pos[best[("q", p["e"])]]:
                    best[("q", p["e"])] = j
        o["wt"] = []
        for k, j in best.items():
            if seen.get((o["e"], k), -1) < pos[j]:
                seen[(o["e"], k)] = pos[j]
                o["wt"].append(j)
                need.add(j)
    tot = {}
    sems = ["loc"]
    for i in order:
        o = ops[i]
        if o["k"] == "dma":
            o["sem"] = ("d%d" % i, 16)
        elif o["k"] == "send":
            o["sem"] = (o["a"][2], 36)
        elif i in need:
            tot["q" + o["e"]] = tot.get("q" + o["e"], 0) + 1
            o["sem"] = ("q" + o["e"], tot["q" + o["e"]])
        else:
            o["sem"] = None
        if o["sem"] and o["sem"][0] not in sems:
            sems.append(o["sem"][0])
    return order, sems, span


OPS = build()
ORDER, SEMAPHORES, SPAN = schedule(OPS)


def rank_program(g, core, T, topo):
    rank = T.rank_of(core)
    if rank is None:
        return
    nxt = T.cores[(rank + 1) % len(T.cores)]
    rid, pid = topo.addr(nxt)[0:2]
    quad = [sum(1 << e for e in topo.engines(core, nxt)[k::4]) for k in range(4)]
    Q = {"v": g.vector, "a": g.scalar, "p": g.tensor, "s": g.sync, "g": g}

    def ap(r):
        if not isinstance(r, tuple):
            return r
        if r[0] == "@":
            return ap(r[1]).indirect(ap(r[2]))
        if r[3] == 1:
            return T[r[0]][r[5]:r[4], r[1]:r[2]]
        return T[r[0]][r[5]:r[4], r[1]:r[2]:r[3]]

    ends = {}
    sent = 0
    for i in ORDER:
        o = OPS[i]
        q = Q[o["e"]]
        k = o["k"]
        a = o["a"]
        for j in o["wt"]:
            q.wait_ge(T.sem[OPS[j]["sem"][0]], OPS[j]["sem"][1])
        if k == "send":
            to = DstId(rid=rid, pnc=pid)
            tr = [RemoteDMATransfer(dst_ids=[to], dma_engine_mask=quad[0], remote_sem=T.sem[a[2]], src=ap(a[1]), dst=ap(a[0]))]
            for e in range(3):
                ds = [ap(r) for r in a[4][e::3]]
                tr.append(RemoteDMATransfer(dst_ids=[to] * len(ds), dma_engine_mask=quad[e + 1], remote_sem=T.sem[a[2]],
                                            src=ap(a[3]), dsts=ds))
            g.remote_dma_fused(tr, local_sem=T.sem["loc"])
            sent += 16
            ends[a[2]] = o["sem"][1]
            continue
        if k == "ts":
            if a[5] is None:
                x = q.tensor_scalar(ap(a[0]), ap(a[1]), ap(a[2]), None, a[4])
            else:
                x = q.tensor_scalar(ap(a[0]), ap(a[1]), ap(a[2]), ap(a[3]), a[4], a[5])
        elif k == "tt":
            x = q.tensor_tensor(ap(a[0]), ap(a[1]), ap(a[2]), a[3])
        elif k == "cp":
            x = q.tensor_copy(ap(a[0]), ap(a[1]))
        elif k == "sc":
            x = q.tensor_tensor_scan(ap(a[0]), ap(a[1]), ap(a[2]), a[3], a[4], a[5])
        elif k == "ms":
            x = q.memset(ap(a[0]), a[1])
        elif k == "ac":
            if a[5]:
                x = q.activation(ap(a[0]), ap(a[1]), a[2], bias=ap(a[3]), scale=ap(a[4]), accum_out=ap(a[5]))
            else:
                x = q.activation(ap(a[0]), ap(a[1]), a[2], bias=ap(a[3]), scale=ap(a[4]))
        elif k == "mm":
            for m in a:
                x = q.matmul(ap(m[0]), ap(m[1]), ap(m[2]), m[3], m[4])
        elif k == "as":
            w = a[1][2] - a[1][1]
            x = g.affine_select(ap(a[0]), ap(a[1]), [[-1 if a[3] else 0, w]], AL.not_equal, a[2], 0, 1 if a[3] else 0)
        elif k == "io":
            if a[0][0] != "pi":
                x = g.iota(ap(a[0]), a[1], a[2], a[3], allow_small_or_imprecise_dtypes=True)
            else:
                x = g.iota(ap(a[0]), a[1], a[2], a[3])
        else:
            x = q.dma_start(ap(a[0]), ap(a[1]))
        if o["sem"]:
            x.then_inc(T.sem[o["sem"][0]], 16 if k == "dma" else 1)
            ends[o["sem"][0]] = o["sem"][1]
    g.wait_ge(T.sem["loc"], sent)
    for s in ends:
        g.wait_ge(T.sem[s], ends[s])
